import numpy as np
import ml_dtypes


def mxq(x, axis, fmt="e4m3"):
    dtype, down = {"e4m3": (ml_dtypes.float8_e4m3fn, 7), "e5m2": (ml_dtypes.float8_e5m2, 14)}[fmt]
    v = np.moveaxis(np.asarray(x, np.float32).astype(ml_dtypes.bfloat16).astype(np.float64), axis, -1)
    blocks = v.reshape(v.shape[:-1] + (-1, 32))
    amax = np.abs(blocks).max(-1, keepdims=True)
    byte = np.maximum(np.where(amax > 0, np.frexp(amax)[1] - 1 + 127, 0) - down, 1)
    scale = np.exp2(byte - 127.0)
    codes = (blocks / scale).astype(np.float32).astype(dtype).astype(np.float64)
    return np.moveaxis((codes * scale).reshape(v.shape), -1, axis)


WIDE = False


def mx_kscale(k):
    if not WIDE:
        return np.ones(k)
    levels = np.array([10, -10, 5, -5, 0])
    if k % 512:
        return np.exp2(np.random.permutation(np.resize(levels, k // 32))).repeat(32)
    a = np.empty((k // 512, 16))
    for p in range(k // 512):
        a[p, :8] = np.random.permutation(np.resize(levels, 8))
        for g in range(8):
            far = levels[np.abs(levels - a[p, g]) >= 10]
            a[p, g + 8] = far[np.random.randint(len(far))]
    return np.exp2(a.ravel()).repeat(32)


def f64(x):
    return np.asarray(x).astype(np.float64)


def striped(idx):
    return np.tile(idx.reshape(-1, 16).T, (8, 1)).astype(np.uint16)


def unstriped(offs):
    return offs[:16].T.reshape(-1).astype(np.int64)


E2M1 = np.array([0.0, 0.5, 1.0, 1.5, 2.0, 3.0, 4.0, 6.0, -0.0, -0.5, -1.0, -1.5, -2.0, -3.0, -4.0, -6.0])


def pack_weight(w, fmt):
    k, n = w.shape
    w = f64(np.asarray(w, np.float32).astype(ml_dtypes.bfloat16)).reshape(k // 32, 32, n)
    amax = np.abs(w).max(1)
    if fmt == "e4m3":
        byte = np.frexp(amax)[1] - 1 + 127 - 7
    else:
        mant, ex = np.frexp(amax / 6.0)
        byte = np.where(mant > 0.5, ex, ex - 1) + 127
    byte = np.clip(np.where(amax > 0, byte, 1), 1, 254)
    scaled = (w * np.exp2(127.0 - byte)[:, None, :]).reshape(k, n).astype(np.float32)
    by_word = np.ascontiguousarray(scaled.reshape(k // 512, 128, 4, n).transpose(0, 1, 3, 2))
    if fmt == "e4m3":
        words = by_word.astype(ml_dtypes.float8_e4m3fn).view(np.uint8)
    else:
        c = by_word.astype(ml_dtypes.float4_e2m1fn).view(np.uint8) & 0xF
        words = (c[..., 0::2] | (c[..., 1::2] << 4)).reshape(k // 512, 128, 2 * n)
    return np.ascontiguousarray(words), np.ascontiguousarray(byte.astype(np.uint8).reshape(k // 512, 16, n))


def unpack_weight(words, scales, fmt):
    g, _, n = scales.shape
    words = np.ascontiguousarray(words).reshape(g, 128, n, -1)
    if fmt == "e4m3":
        vals = words.view(ml_dtypes.float8_e4m3fn).astype(np.float64)
    else:
        nib = np.empty((g, 128, n, 4), np.uint8)
        nib[..., 0::2] = words & 0xF
        nib[..., 1::2] = words >> 4
        vals = E2M1[nib]
    vals = vals * np.repeat(np.exp2(scales.astype(np.float64) - 127.0), 8, axis=1)[..., None]
    return vals.transpose(0, 1, 3, 2).reshape(g * 512, n)


def gelu(v):
    return 0.5 * v * (1.0 + np.tanh(np.sqrt(2.0 / np.pi) * (v + 0.044715 * v**3)))


K, T, E, C, H, N = 512, 1280, 10, 128, 512, 256


def by_expert(wq, xq):
    return np.concatenate([wq[e].T @ xq[:, e * C:(e + 1) * C] for e in range(E)], axis=1)


def setup_inputs():
    n = np.random.standard_normal
    s = mx_kscale(K)
    u = mx_kscale(H)
    slot_token = np.random.permutation(T)[:E * C]
    x = pack_weight(n((K, T)) * s[:, None], "e4m3")
    w = pack_weight(n((K, N)) / np.sqrt(K) / s[:, None], "e2m1")
    wa = [pack_weight(m, "e2m1") for m in n((E, K, H)) / np.sqrt(K) / s[None, :, None] * u]
    wb = [pack_weight(m, "e2m1") for m in n((E, H, N)) / np.sqrt(H) / u[None, :, None]]
    return {
        "x_words": x[0],
        "x_scales": x[1],
        "w_words": w[0],
        "w_scales": w[1],
        "wa_words": np.stack([m[0] for m in wa]),
        "wa_scales": np.stack([m[1] for m in wa]),
        "wb_words": np.stack([m[0] for m in wb]),
        "wb_scales": np.stack([m[1] for m in wb]),
        "gate": np.tile(np.random.uniform(0.2, 1.0, E * C), (128, 1)).astype(np.float32),
        "offs": striped(slot_token),
    }


def reference(x_words, x_scales, w_words, w_scales, wa_words, wa_scales, wb_words, wb_scales, gate, offs):
    w = unpack_weight(w_words, w_scales, "e2m1")
    wa = np.stack([unpack_weight(wa_words[e], wa_scales[e], "e2m1") for e in range(E)])
    wb = np.stack([unpack_weight(wb_words[e], wb_scales[e], "e2m1") for e in range(E)])
    idx = unstriped(offs)
    x = unpack_weight(x_words, x_scales, "e4m3")
    base = w.T @ x
    h = gelu(by_expert(wa, x[:, idx]))
    y = by_expert(wb, mxq(h, 0, "e4m3"))
    c = np.zeros((N, T))
    c[:, idx] = f64(gate[:1]) * y
    return base + c

@@ -1,0 +1,219 @@
+from contextlib import ExitStack
+
+import concourse.mybir as mybir
+from concourse.masks import make_identity
+
+K, T, E, C, H, N = 512, 1280, 10, 128, 512, 256
+FLOPS = 2 * K * N * T + 2 * K * H * E * C + 2 * H * N * E * C
+
+F32 = mybir.dt.float32
+BF16 = mybir.dt.bfloat16
+I32 = mybir.dt.int32
+U32 = mybir.dt.uint32
+U16 = mybir.dt.uint16
+U8 = mybir.dt.uint8
+FP8X4 = mybir.dt.float8_e4m3fn_x4
+FP4X4 = mybir.dt.float4_e2m1fn_x4
+ACT = mybir.ActivationFunctionType
+ADD = mybir.AluOpType.add
+
+P = 128
+PAIR = 2
+G = E // PAIR
+GS = PAIR * C
+TOKEN_CHUNKS = [(0, 512), (512, 1024), (1024, 1280)]
+
+
+def tile_moe_adp_gelu_kernel(
+    tc, x_words, x_scales, w_words, w_scales, wa_words, wa_scales, wb_words, wb_scales, gate, offs, out
+):
+    nc = tc.nc
+    with ExitStack() as ctx:
+        keep = ctx.enter_context(tc.tile_pool(name="keep", bufs=1))
+        ring = ctx.enter_context(tc.tile_pool(name="ring", bufs=3))
+        psum = ctx.enter_context(tc.psum_pool(name="psum", bufs=1))
+
+        offsets = keep.tile([P, T // 16], U16, name="offsets")
+        xw = keep.tile([P, T], I32, name="xw", align_bytes=64)
+        xs = keep.tile([P, T], U8, name="xs", align_bytes=64)
+        xwg = keep.tile([P, T], U32, name="xwg", align_bytes=64)
+        xsg = keep.tile([P, T], U8, name="xsg", align_bytes=64)
+        ww = keep.tile([P, 2 * N], U8, name="ww", align_bytes=64)
+        ws = keep.tile([P, N], U8, name="ws", align_bytes=64)
+        wa = keep.tile([P, E, 2 * H], U8, name="wa", align_bytes=64)
+        was = keep.tile([P, E, H], U8, name="was", align_bytes=64)
+        wb = keep.tile([P, E, 2 * N], U8, name="wb", align_bytes=64)
+        wbs = keep.tile([P, E, N], U8, name="wbs", align_bytes=64)
+        grow = keep.tile([P, P], F32, name="grow")
+        gcol = keep.tile([P, E], F32, name="gcol")
+        ident = keep.tile([P, P], F32, name="ident")
+        warm = keep.tile([P, 8], F32, name="warm")
+        warm_out = keep.tile([P, 8], F32, name="warm_out")
+        win = [keep.tile([P, T], F32, name="win%d" % t) for t in range(2)]
+        res = [keep.tile([P, T], F32, name="res%d" % t) for t in range(2)]
+        ys = [keep.tile([P, 2, GS], F32, name="ys%d" % g) for g in range(G)]
+
+        nc.vector.memset(xs[:].bitcast(I32), 0)
+        nc.vector.memset(was[:].bitcast(I32), 0)
+        nc.vector.memset(wbs[:].bitcast(I32), 0)
+        nc.vector.memset(ws[:].bitcast(I32), 0)
+        nc.gpsimd.memset(warm[:], 0.0)
+        nc.scalar.activation(out=warm_out[:], in_=warm[:], func=ACT.Gelu_apprx_tanh)
+        make_identity(nc, ident[:])
+
+        def load_plane(plane, rows):
+            src = rows.bitcast(I32).rearrange("(q r) n -> r q n", r=4)
+            for r in range(4):
+                nc.sync.dma_start(out=plane[r:P:32, :].bitcast(I32), in_=src[r])
+
+        def load_planes(planes, rows, e0, e1):
+            src = rows.bitcast(I32)[e0:e1, 0].rearrange("e (q r) n -> r q e n", r=4)
+            for r in range(4):
+                nc.sync.dma_start(out=planes[r:P:32, e0:e1, :].bitcast(I32), in_=src[r])
+
+        def load_words(words, src, e0, e1):
+            nc.sync.dma_start(
+                out=words[:, e0:e1, :].bitcast(I32), in_=src.bitcast(I32)[e0:e1, 0].rearrange("e p n -> p e n")
+            )
+
+        nc.sync.dma_start(offsets[:], offs)
+        load_plane(xs, x_scales[0])
+        nc.sync.dma_start(out=xw[:], in_=x_words[0].rearrange("p t d -> p (t d)").bitcast(I32))
+        load_planes(was, wa_scales, 0, 2)
+        load_words(wa, wa_words, 0, 2)
+        nc.sync.dma_start(out=grow[:], in_=gate.rearrange("r (e j) -> (r e) j", j=C)[0:P, :])
+        load_planes(wbs, wb_scales, 0, E)
+        load_words(wb, wb_words, 0, 2)
+        load_planes(was, wa_scales, 2, E)
+        load_words(wa, wa_words, 2, 4)
+        load_words(wb, wb_words, 2, 4)
+        load_words(wa, wa_words, 4, 6)
+        load_words(wb, wb_words, 4, E)
+        load_words(wa, wa_words, 6, E)
+        load_plane(ws, w_scales[0])
+        nc.sync.dma_start(out=ww[:].bitcast(I32), in_=w_words[0].bitcast(I32))
+
+        def gather_bytes(a, b):
+            nc.vector.tensor_copy(out=xsg[:, a:b], in_=xs[:].indirect(offsets[:, a // 16 : b // 16]))
+
+        def gather_words(a, b):
+            nc.vector.tensor_copy(out=xwg[:, a:b], in_=xw[:].bitcast(U32).indirect(offsets[:, a // 16 : b // 16]))
+
+        gather_bytes(0, 512)
+        gather_words(0, 256)
+        gather_words(256, 512)
+        gather_bytes(512, 1280)
+        gather_words(512, 768)
+        gather_words(768, 1280)
+
+        hb = {}
+        hin = {}
+        hq = {}
+        yt = {}
+
+        def first_layer(g):
+            hb[g] = ring.tile([P, PAIR, H], BF16, name="hb", align_bytes=64)
+            for x in range(PAIR):
+                e = PAIR * g + x
+                slots = slice(e * C, (e + 1) * C)
+                acc = psum.tile([P, H], F32, name="l1", bufs=2)
+                nc.tensor.matmul_mx(
+                    out=acc[:],
+                    lhsT=xwg[:, slots].bitcast(FP8X4),
+                    lhsT_scale=xsg[:, slots],
+                    rhs=wa[:, e, :].bitcast(FP4X4),
+                    rhs_scale=was[:, e, :],
+                    start=True,
+                    stop=True,
+                )
+                nc.scalar.activation(
+                    out=hb[g][:, x, :].rearrange("j (u p d) -> j u p d", u=2, d=2),
+                    in_=acc[:].rearrange("j (p u d) -> j u p d", u=2, d=2),
+                    func=ACT.Gelu_apprx_tanh,
+                )
+
+        def turn_h(g):
+            turned = psum.tile([P, PAIR, 2, C], F32, name="t1")
+            for x in range(PAIR):
+                words = hb[g][:, x, :].bitcast(F32)
+                for u in range(2):
+                    nc.tensor.transpose(turned[:, x, u, :], words[:, u * P : (u + 1) * P], ident[:])
+            hin[g] = ring.tile([P, GS * 4], BF16, name="hin", align_bytes=64)
+            nc.scalar.copy(
+                out=hin[g][:].bitcast(F32).rearrange("p (x j u) -> p x j u", x=PAIR, u=2),
+                in_=turned[:].rearrange("p x u j -> p x j u"),
+            )
+
+        def quantise(g):
+            codes = ring.tile([P, GS], U32, name="hcodes", align_bytes=64)
+            scales = ring.tile([P, GS], U8, name="hscales", align_bytes=64)
+            nc.vector.quantize_mx(out=codes[:].bitcast(FP8X4), scales=scales[:], in_=hin[g][:])
+            hq[g] = (codes, scales)
+
+        def second_layer(g):
+            codes, scales = hq[g]
+            acc = psum.tile([P, PAIR, N], F32, name="l2")
+            yt[g] = ring.tile([P, PAIR, N], F32, name="yt")
+            for x in range(PAIR):
+                e = PAIR * g + x
+                nc.tensor.matmul_mx(
+                    out=acc[:, x, :],
+                    lhsT=codes[:, x * C : (x + 1) * C].bitcast(FP8X4),
+                    lhsT_scale=scales[:, x * C : (x + 1) * C],
+                    rhs=wb[:, e, :].bitcast(FP4X4),
+                    rhs_scale=wbs[:, e, :],
+                    start=True,
+                    stop=True,
+                )
+            for x in range(PAIR):
+                e = PAIR * g + x
+                nc.scalar.activation(out=yt[g][:, x, :], in_=acc[:, x, :], func=ACT.Copy, scale=gcol[:, e : e + 1])
+
+        def turn_y(g):
+            turned = psum.tile([P, 2, PAIR, C], F32, name="t2")
+            for t in range(2):
+                for x in range(PAIR):
+                    nc.tensor.transpose(turned[:, t, x, :], yt[g][:, x, t * P : (t + 1) * P], ident[:])
+            nc.scalar.copy(out=ys[g][:], in_=turned[:].rearrange("p t x j -> p t (x j)"))
+
+        def scatter(t, g):
+            nc.vector.tensor_copy(
+                out=win[t][:].indirect(offsets[:, g * GS // 16 : (g + 1) * GS // 16]), in_=ys[g][:, t, :]
+            )
+
+        def gate_columns():
+            turned = psum.tile([P, 2, PAIR, C], F32, name="t2")
+            nc.tensor.transpose(turned[:, 0, 0, :], grow[:], ident[:])
+            nc.scalar.copy(out=gcol[:], in_=turned[:, 0, 0, 0:E])
+
+        def finish(t):
+            for a, b in TOKEN_CHUNKS:
+                acc = psum.tile([P, 512], F32, name="base", bufs=3)
+                nc.tensor.matmul_mx(
+                    out=acc[:, 0 : b - a],
+                    lhsT=ww[:, t * 2 * P : (t + 1) * 2 * P].bitcast(FP4X4),
+                    lhsT_scale=ws[:, t * P : (t + 1) * P],
+                    rhs=xw[:, a:b].bitcast(FP8X4),
+                    rhs_scale=xs[:, a:b],
+                    start=True,
+                    stop=True,
+                )
+                nc.vector.tensor_tensor(out=res[t][:, a:b], in0=acc[:, 0 : b - a], in1=win[t][:, a:b], op=ADD)
+                nc.sync.dma_start(out=out[t * P : (t + 1) * P, a:b], in_=res[t][:, a:b])
+
+        first_layer(0)
+        gate_columns()
+        turn_h(0)
+        for g in range(G):
+            quantise(g)
+            if g + 1 < G:
+                first_layer(g + 1)
+            second_layer(g)
+            if g + 1 < G:
+                turn_h(g + 1)
+            turn_y(g)
+            scatter(0, g)
+        finish(0)
+        for g in range(G):
+            scatter(1, g)
+        finish(1)

@@ -16,11 +16,13 @@ FP8X4 = mybir.dt.float8_e4m3fn_x4
 FP4X4 = mybir.dt.float4_e2m1fn_x4
 ACT = mybir.ActivationFunctionType
 ADD = mybir.AluOpType.add
+MULT = mybir.AluOpType.mult
 
 P = 128
-PAIR = 2
-G = E // PAIR
-GS = PAIR * C
+PAIRS = E // 2
+PS = 2 * C
+PIECES = [(0, 256), (256, 640), (640, 1024), (1024, 1280)]
+EARLY = 2
 TOKEN_CHUNKS = [(0, 512), (512, 1024), (1024, 1280)]
 
 
@@ -30,190 +32,219 @@ def tile_moe_adp_gelu_kernel(
     nc = tc.nc
     with ExitStack() as ctx:
         keep = ctx.enter_context(tc.tile_pool(name="keep", bufs=1))
-        ring = ctx.enter_context(tc.tile_pool(name="ring", bufs=3))
+        shared = ctx.enter_context(tc.tile_pool(name="shared", bufs=1))
+        late = ctx.enter_context(tc.tile_pool(name="late", bufs=1))
         psum = ctx.enter_context(tc.psum_pool(name="psum", bufs=1))
 
         offsets = keep.tile([P, T // 16], U16, name="offsets")
         xw = keep.tile([P, T], I32, name="xw", align_bytes=64)
         xs = keep.tile([P, T], U8, name="xs", align_bytes=64)
-        xwg = keep.tile([P, T], U32, name="xwg", align_bytes=64)
-        xsg = keep.tile([P, T], U8, name="xsg", align_bytes=64)
-        ww = keep.tile([P, 2 * N], U8, name="ww", align_bytes=64)
-        ws = keep.tile([P, N], U8, name="ws", align_bytes=64)
-        wa = keep.tile([P, E, 2 * H], U8, name="wa", align_bytes=64)
+        word_at = [0, 2048, 0, 5120]
+        byte_at = [3584, 4096, 3584, 4608]
+        xwg = [
+            shared.tile([P, b - a], U32, name="xwg%d" % i, align_bytes=64, offset=word_at[i])
+            for i, (a, b) in enumerate(PIECES)
+        ]
+        xsg = [
+            shared.tile([P, b - a], U8, name="xsg%d" % i, align_bytes=64, offset=byte_at[i])
+            for i, (a, b) in enumerate(PIECES)
+        ]
+        warm = late.tile([P, 4800], F32, name="warm", align_bytes=64, offset=0)
+        wa_late = late.tile([P, E - EARLY, 2 * H], U8, name="wa_late", align_bytes=64, offset=0)
+        wb = late.tile([P, E, 2 * N], U8, name="wb", align_bytes=64, offset=8192)
+        gates = late.tile([P, T], F32, name="gates", align_bytes=64, offset=13312)
+        ww = late.tile([P, 2 * N], U8, name="ww", align_bytes=64, offset=18432)
+        ws = late.tile([P, N], U8, name="ws", align_bytes=64, offset=18944)
+        wa = keep.tile([P, EARLY, 2 * H], U8, name="wa", align_bytes=64)
         was = keep.tile([P, E, H], U8, name="was", align_bytes=64)
-        wb = keep.tile([P, E, 2 * N], U8, name="wb", align_bytes=64)
         wbs = keep.tile([P, E, N], U8, name="wbs", align_bytes=64)
-        grow = keep.tile([P, P], F32, name="grow")
-        gcol = keep.tile([P, E], F32, name="gcol")
         ident = keep.tile([P, P], F32, name="ident")
-        warm = keep.tile([P, 8], F32, name="warm")
-        warm_out = keep.tile([P, 8], F32, name="warm_out")
+        hb = keep.tile([P, E, H], BF16, name="hb", align_bytes=64)
+        hin = keep.tile([P, E, 4 * C], BF16, name="hin", align_bytes=64)
+        hin1 = shared.tile([P, 4 * C], BF16, name="hin1", align_bytes=64, offset=4608)
+        hcodes = keep.tile([P, T], U32, name="hcodes", align_bytes=64)
+        hscales = keep.tile([P, T], U8, name="hscales", align_bytes=64)
+        ys = keep.tile([P, 2, T], F32, name="ys")
         win = [keep.tile([P, T], F32, name="win%d" % t) for t in range(2)]
         res = [keep.tile([P, T], F32, name="res%d" % t) for t in range(2)]
-        ys = [keep.tile([P, 2, GS], F32, name="ys%d" % g) for g in range(G)]
+        base0 = keep.tile([P, T], F32, name="base0")
+        half = keep.tile([P, T], F32, name="half")
+        bank = [psum.tile([P, 512], F32, name="bank%d" % b) for b in range(8)]
+        wide, alt, spare = bank[0:3], bank[3:5], bank[5:8]
 
         nc.vector.memset(xs[:].bitcast(I32), 0)
-        nc.vector.memset(was[:].bitcast(I32), 0)
+        nc.vector.memset(warm[:, 0:8], 0.0)
+        nc.vector.memset(was[:, 0:4, :].bitcast(I32), 0)
         nc.vector.memset(wbs[:].bitcast(I32), 0)
-        nc.vector.memset(ws[:].bitcast(I32), 0)
-        nc.gpsimd.memset(warm[:], 0.0)
-        nc.scalar.activation(out=warm_out[:], in_=warm[:], func=ACT.Gelu_apprx_tanh)
+        nc.vector.memset(was[:, 4:E, :].bitcast(I32), 0)
+        nc.gpsimd.dma_start(out=wa[:].bitcast(I32), in_=wa_words.bitcast(I32)[0:EARLY, 0].rearrange("e p n -> p e n"))
         make_identity(nc, ident[:])
 
-        def load_plane(plane, rows):
+        def load_plane(queue, plane, rows):
             src = rows.bitcast(I32).rearrange("(q r) n -> r q n", r=4)
             for r in range(4):
-                nc.sync.dma_start(out=plane[r:P:32, :].bitcast(I32), in_=src[r])
+                queue.dma_start(out=plane[r:P:32, :].bitcast(I32), in_=src[r])
 
         def load_planes(planes, rows, e0, e1):
             src = rows.bitcast(I32)[e0:e1, 0].rearrange("e (q r) n -> r q e n", r=4)
             for r in range(4):
                 nc.sync.dma_start(out=planes[r:P:32, e0:e1, :].bitcast(I32), in_=src[r])
 
-        def load_words(words, src, e0, e1):
-            nc.sync.dma_start(
-                out=words[:, e0:e1, :].bitcast(I32), in_=src.bitcast(I32)[e0:e1, 0].rearrange("e p n -> p e n")
+        def load_words(words, src, e0, e1, first=0, queue=nc.sync):
+            queue.dma_start(
+                out=words[:, e0 - first : e1 - first, :].bitcast(I32), in_=src.bitcast(I32)[e0:e1, 0].rearrange("e p n -> p e n")
             )
 
         nc.sync.dma_start(offsets[:], offs)
-        load_plane(xs, x_scales[0])
         nc.sync.dma_start(out=xw[:], in_=x_words[0].rearrange("p t d -> p (t d)").bitcast(I32))
-        load_planes(was, wa_scales, 0, 2)
-        load_words(wa, wa_words, 0, 2)
-        nc.sync.dma_start(out=grow[:], in_=gate.rearrange("r (e j) -> (r e) j", j=C)[0:P, :])
+        load_plane(nc.scalar, xs, x_scales[0])
+        nc.scalar.activation(out=warm[:, 8:16], in_=warm[:, 0:8], func=ACT.Gelu_apprx_tanh)
+        load_planes(was, wa_scales, 0, 4)
+        load_words(wa_late, wa_words, 2, 4, EARLY)
         load_planes(wbs, wb_scales, 0, E)
         load_words(wb, wb_words, 0, 2)
-        load_planes(was, wa_scales, 2, E)
-        load_words(wa, wa_words, 2, 4)
-        load_words(wb, wb_words, 2, 4)
-        load_words(wa, wa_words, 4, 6)
-        load_words(wb, wb_words, 4, E)
-        load_words(wa, wa_words, 6, E)
-        load_plane(ws, w_scales[0])
+        load_planes(was, wa_scales, 4, E)
+        load_words(wa_late, wa_words, 4, 6, EARLY)
+        nc.sync.dma_start(out=gates[:, 0:PS], in_=gate[:, 0:PS])
+        load_words(wa_late, wa_words, 6, 8, EARLY)
+        load_words(wb, wb_words, 2, 6)
+        nc.sync.dma_start(out=gates[:, PS:T], in_=gate[:, PS:T])
+        load_words(wa_late, wa_words, 8, E, EARLY)
+        load_words(wb, wb_words, 6, E)
+        nc.gpsimd.memset(ws[:].bitcast(I32), 0)
+        load_plane(nc.sync, ws, w_scales[0])
         nc.sync.dma_start(out=ww[:].bitcast(I32), in_=w_words[0].bitcast(I32))
 
-        def gather_bytes(a, b):
-            nc.vector.tensor_copy(out=xsg[:, a:b], in_=xs[:].indirect(offsets[:, a // 16 : b // 16]))
+        def gather_bytes(dst, a, b):
+            nc.vector.tensor_copy(out=dst, in_=xs[:].indirect(offsets[:, a // 16 : b // 16]))
 
-        def gather_words(a, b):
-            nc.vector.tensor_copy(out=xwg[:, a:b], in_=xw[:].bitcast(U32).indirect(offsets[:, a // 16 : b // 16]))
+        def gather_words(dst, a, b):
+            nc.vector.tensor_copy(out=dst, in_=xw[:].bitcast(U32).indirect(offsets[:, a // 16 : b // 16]))
 
-        gather_bytes(0, 512)
-        gather_words(0, 256)
-        gather_words(256, 512)
-        gather_bytes(512, 1280)
-        gather_words(512, 768)
-        gather_words(768, 1280)
+        def gather(i):
+            gather_bytes(xsg[i][:], *PIECES[i])
+            gather_words(xwg[i][:], *PIECES[i])
 
-        hb = {}
-        hin = {}
-        hq = {}
-        yt = {}
+        def first_layer(e):
+            a, b = e * C, (e + 1) * C
+            i = [j for j, (lo, hi) in enumerate(PIECES) if lo <= a < hi][0]
+            words = xwg[i][:, a - PIECES[i][0] : b - PIECES[i][0]]
+            scales = xsg[i][:, a - PIECES[i][0] : b - PIECES[i][0]]
+            moving = wa[:, e, :] if e < EARLY else wa_late[:, e - EARLY, :]
+            acc = wide[e % 3]
+            nc.tensor.matmul_mx(
+                out=acc[:],
+                lhsT=words.bitcast(FP8X4),
+                lhsT_scale=scales,
+                rhs=moving.bitcast(FP4X4),
+                rhs_scale=was[:, e, :],
+                start=True,
+                stop=True,
+            )
+            nc.scalar.activation(
+                out=hb[:, e, :].rearrange("j (u p d) -> j u p d", u=2, d=2),
+                in_=acc[:].rearrange("j (p u d) -> j u p d", u=2, d=2),
+                func=ACT.Gelu_apprx_tanh,
+            )
 
-        def first_layer(g):
-            hb[g] = ring.tile([P, PAIR, H], BF16, name="hb", align_bytes=64)
-            for x in range(PAIR):
-                e = PAIR * g + x
-                slots = slice(e * C, (e + 1) * C)
-                acc = psum.tile([P, H], F32, name="l1", bufs=2)
-                nc.tensor.matmul_mx(
-                    out=acc[:],
-                    lhsT=xwg[:, slots].bitcast(FP8X4),
-                    lhsT_scale=xsg[:, slots],
-                    rhs=wa[:, e, :].bitcast(FP4X4),
-                    rhs_scale=was[:, e, :],
-                    start=True,
-                    stop=True,
-                )
-                nc.scalar.activation(
-                    out=hb[g][:, x, :].rearrange("j (u p d) -> j u p d", u=2, d=2),
-                    in_=acc[:].rearrange("j (p u d) -> j u p d", u=2, d=2),
-                    func=ACT.Gelu_apprx_tanh,
-                )
-
-        def turn_h(g):
-            turned = psum.tile([P, PAIR, 2, C], F32, name="t1")
-            for x in range(PAIR):
-                words = hb[g][:, x, :].bitcast(F32)
+        def turn_and_quantise(e0, e1, acc, grouped):
+            m = e1 - e0
+            turned = acc[:, 0 : m * 2 * C].rearrange("p (x u j) -> p x u j", x=m, u=2)
+            for x in range(m):
+                words = hb[:, e0 + x, :].bitcast(F32)
                 for u in range(2):
                     nc.tensor.transpose(turned[:, x, u, :], words[:, u * P : (u + 1) * P], ident[:])
-            hin[g] = ring.tile([P, GS * 4], BF16, name="hin", align_bytes=64)
             nc.scalar.copy(
-                out=hin[g][:].bitcast(F32).rearrange("p (x j u) -> p x j u", x=PAIR, u=2),
-                in_=turned[:].rearrange("p x u j -> p x j u"),
+                out=grouped.bitcast(F32).rearrange("p (x j u) -> p x j u", x=m, u=2),
+                in_=turned.rearrange("p x u j -> p x j u"),
+            )
+            nc.vector.quantize_mx(
+                out=hcodes[:, e0 * C : e1 * C].bitcast(FP8X4), scales=hscales[:, e0 * C : e1 * C], in_=grouped
             )
 
-        def quantise(g):
-            codes = ring.tile([P, GS], U32, name="hcodes", align_bytes=64)
-            scales = ring.tile([P, GS], U8, name="hscales", align_bytes=64)
-            nc.vector.quantize_mx(out=codes[:].bitcast(FP8X4), scales=scales[:], in_=hin[g][:])
-            hq[g] = (codes, scales)
+        def pair_stage(g):
+            first_layer(2 * g)
+            first_layer(2 * g + 1)
+            turn_and_quantise(2 * g, 2 * g + 2, alt[g % 2], hin[:, 2 * g : 2 * g + 2, :].rearrange("p x c -> p (x c)"))
 
-        def second_layer(g):
-            codes, scales = hq[g]
-            acc = psum.tile([P, PAIR, N], F32, name="l2")
-            yt[g] = ring.tile([P, PAIR, N], F32, name="yt")
-            for x in range(PAIR):
-                e = PAIR * g + x
+        def second_layer(t, e0, e1, acc):
+            for e in range(e0, e1):
                 nc.tensor.matmul_mx(
-                    out=acc[:, x, :],
-                    lhsT=codes[:, x * C : (x + 1) * C].bitcast(FP8X4),
-                    lhsT_scale=scales[:, x * C : (x + 1) * C],
-                    rhs=wb[:, e, :].bitcast(FP4X4),
-                    rhs_scale=wbs[:, e, :],
+                    out=acc[:, (e - e0) * C : (e - e0 + 1) * C],
+                    lhsT=wb[:, e, t * 2 * P : (t + 1) * 2 * P].bitcast(FP4X4),
+                    lhsT_scale=wbs[:, e, t * P : (t + 1) * P],
+                    rhs=hcodes[:, e * C : (e + 1) * C].bitcast(FP8X4),
+                    rhs_scale=hscales[:, e * C : (e + 1) * C],
                     start=True,
                     stop=True,
                 )
-            for x in range(PAIR):
-                e = PAIR * g + x
-                nc.scalar.activation(out=yt[g][:, x, :], in_=acc[:, x, :], func=ACT.Copy, scale=gcol[:, e : e + 1])
+            nc.scalar.copy(out=ys[:, t, e0 * C : e1 * C], in_=acc[:, 0 : (e1 - e0) * C])
 
-        def turn_y(g):
-            turned = psum.tile([P, 2, PAIR, C], F32, name="t2")
-            for t in range(2):
-                for x in range(PAIR):
-                    nc.tensor.transpose(turned[:, t, x, :], yt[g][:, x, t * P : (t + 1) * P], ident[:])
-            nc.scalar.copy(out=ys[g][:], in_=turned[:].rearrange("p t x j -> p t (x j)"))
-
-        def scatter(t, g):
-            nc.vector.tensor_copy(
-                out=win[t][:].indirect(offsets[:, g * GS // 16 : (g + 1) * GS // 16]), in_=ys[g][:, t, :]
+        def scatter(t, e0, e1):
+            a, b = e0 * C, e1 * C
+            nc.vector.tensor_tensor(
+                out=win[t][:].indirect(offsets[:, a // 16 : b // 16]), in0=ys[:, t, a:b], in1=gates[:, a:b], op=MULT
             )
 
-        def gate_columns():
-            turned = psum.tile([P, 2, PAIR, C], F32, name="t2")
-            nc.tensor.transpose(turned[:, 0, 0, :], grow[:], ident[:])
-            nc.scalar.copy(out=gcol[:], in_=turned[:, 0, 0, 0:E])
+        def frozen(t, i):
+            a, b = TOKEN_CHUNKS[i]
+            nc.tensor.matmul_mx(
+                out=wide[(E + i) % 3][:, 0 : b - a],
+                lhsT=ww[:, t * 2 * P : (t + 1) * 2 * P].bitcast(FP4X4),
+                lhsT_scale=ws[:, t * P : (t + 1) * P],
+                rhs=xw[:, a:b].bitcast(FP8X4),
+                rhs_scale=xs[:, a:b],
+                start=True,
+                stop=True,
+            )
+            return wide[(E + i) % 3][:, 0 : b - a]
 
-        def finish(t):
-            for a, b in TOKEN_CHUNKS:
-                acc = psum.tile([P, 512], F32, name="base", bufs=3)
-                nc.tensor.matmul_mx(
-                    out=acc[:, 0 : b - a],
-                    lhsT=ww[:, t * 2 * P : (t + 1) * 2 * P].bitcast(FP4X4),
-                    lhsT_scale=ws[:, t * P : (t + 1) * P],
-                    rhs=xw[:, a:b].bitcast(FP8X4),
-                    rhs_scale=xs[:, a:b],
-                    start=True,
-                    stop=True,
-                )
-                nc.vector.tensor_tensor(out=res[t][:, a:b], in0=acc[:, 0 : b - a], in1=win[t][:, a:b], op=ADD)
+        def finish_direct(t):
+            for i, (a, b) in enumerate(TOKEN_CHUNKS):
+                acc = frozen(t, i)
+                nc.vector.tensor_tensor(out=res[t][:, a:b], in0=acc, in1=win[t][:, a:b], op=ADD)
                 nc.sync.dma_start(out=out[t * P : (t + 1) * P, a:b], in_=res[t][:, a:b])
 
+        def finish_turned():
+            for i, (a, b) in enumerate(TOKEN_CHUNKS):
+                for c in range(a, b, P):
+                    o = spare[i][:, c - a : c - a + P]
+                    nc.tensor.matmul(o, lhsT=base0[:, c : c + P], rhs=ident[:], start=True, stop=False, is_transpose=True)
+                    nc.tensor.matmul(o, lhsT=win[0][:, c : c + P], rhs=ident[:], start=False, stop=True, is_transpose=True)
+                nc.scalar.copy(out=half[:, a:b], in_=spare[i][:, 0 : b - a])
+            for i, (a, b) in enumerate(TOKEN_CHUNKS):
+                for c in range(a, b, P):
+                    nc.tensor.transpose(spare[i][:, c - a : c - a + P], half[:, c : c + P], ident[:])
+                nc.scalar.copy(out=res[0][:, a:b], in_=spare[i][:, 0 : b - a])
+                nc.sync.dma_start(out=out[0:P, a:b], in_=res[0][:, a:b])
+
+        gather(0)
+        gather(1)
         first_layer(0)
-        gate_columns()
-        turn_h(0)
-        for g in range(G):
-            quantise(g)
-            if g + 1 < G:
-                first_layer(g + 1)
-            second_layer(g)
-            if g + 1 < G:
-                turn_h(g + 1)
-            turn_y(g)
-            scatter(0, g)
-        finish(0)
-        for g in range(G):
-            scatter(1, g)
-        finish(1)
+        first_layer(1)
+        gather(2)
+        turn_and_quantise(0, 1, spare[0], hin[:, 0, :])
+        turn_and_quantise(1, 2, spare[1], hin1[:])
+        second_layer(0, 0, 2, spare[2])
+        gather(3)
+        pair_stage(1)
+        scatter(0, 0, 2)
+        second_layer(1, 0, 2, alt[1])
+        for g in range(2, PAIRS):
+            pair_stage(g)
+            if g == 2:
+                scatter(1, 0, 2)
+            else:
+                scatter(0, 2 * g - 4, 2 * g - 2)
+            second_layer(0, 2 * g - 2, 2 * g, alt[g % 2])
+        scatter(0, E - 4, E - 2)
+        second_layer(0, E - 2, E, alt[1])
+        scatter(0, E - 2, E)
+        second_layer(1, 2, 6, alt[1])
+        second_layer(1, 6, E, alt[0])
+        for i, (a, b) in enumerate(TOKEN_CHUNKS):
+            nc.scalar.copy(out=base0[:, a:b], in_=frozen(0, i))
+        finish_turned()
+        scatter(1, 2, 6)
+        scatter(1, 6, E)
+        finish_direct(1)

@@ -21,8 +21,11 @@ MULT = mybir.AluOpType.mult
 P = 128
 PAIRS = E // 2
 PS = 2 * C
-PIECES = [(0, 256), (256, 640), (640, 1024), (1024, 1280)]
-EARLY = 2
+WA_CUTS = [(0, 2), (2, 4), (4, 6), (6, 10)]
+WAS_CUTS = [(0, 4), (4, 10)]
+WB_CUTS = [(0, 4), (4, 10)]
+GATE_CUTS = [(0, 2), (2, 5)]
+QUANT_CUTS = [(0, 1), (1, 2), (2, 4), (4, 6), (6, 8), (8, 10)]
 TOKEN_CHUNKS = [(0, 512), (512, 1024), (1024, 1280)]
 
 
@@ -36,160 +39,179 @@ def tile_moe_adp_gelu_kernel(
         late = ctx.enter_context(tc.tile_pool(name="late", bufs=1))
         psum = ctx.enter_context(tc.psum_pool(name="psum", bufs=1))
 
+        def placed(pool, name, shape, dtype, at):
+            return pool.tile(shape, dtype, name=name, align_bytes=64, offset=at)
+
         offsets = keep.tile([P, T // 16], U16, name="offsets")
         xw = keep.tile([P, T], I32, name="xw", align_bytes=64)
         xs = keep.tile([P, T], U8, name="xs", align_bytes=64)
-        word_at = [0, 2048, 0, 5120]
-        byte_at = [3584, 4096, 3584, 4608]
-        xwg = [
-            shared.tile([P, b - a], U32, name="xwg%d" % i, align_bytes=64, offset=word_at[i])
-            for i, (a, b) in enumerate(PIECES)
-        ]
-        xsg = [
-            shared.tile([P, b - a], U8, name="xsg%d" % i, align_bytes=64, offset=byte_at[i])
-            for i, (a, b) in enumerate(PIECES)
-        ]
-        warm = late.tile([P, 4800], F32, name="warm", align_bytes=64, offset=0)
-        wa_late = late.tile([P, E - EARLY, 2 * H], U8, name="wa_late", align_bytes=64, offset=0)
-        wb = late.tile([P, E, 2 * N], U8, name="wb", align_bytes=64, offset=8192)
-        gates = late.tile([P, T], F32, name="gates", align_bytes=64, offset=13312)
-        ww = late.tile([P, 2 * N], U8, name="ww", align_bytes=64, offset=18432)
-        ws = late.tile([P, N], U8, name="ws", align_bytes=64, offset=18944)
-        wa = keep.tile([P, EARLY, 2 * H], U8, name="wa", align_bytes=64)
-        was = keep.tile([P, E, H], U8, name="was", align_bytes=64)
+        was = [keep.tile([P, b - a, H], U8, name="was%d" % a, align_bytes=64) for a, b in WAS_CUTS]
         wbs = keep.tile([P, E, N], U8, name="wbs", align_bytes=64)
         ident = keep.tile([P, P], F32, name="ident")
-        hb = keep.tile([P, E, H], BF16, name="hb", align_bytes=64)
-        hin = keep.tile([P, E, 4 * C], BF16, name="hin", align_bytes=64)
-        hin1 = shared.tile([P, 4 * C], BF16, name="hin1", align_bytes=64, offset=4608)
-        hcodes = keep.tile([P, T], U32, name="hcodes", align_bytes=64)
-        hscales = keep.tile([P, T], U8, name="hscales", align_bytes=64)
-        ys = keep.tile([P, 2, T], F32, name="ys")
+        hcodes = [keep.tile([P, b - a, C], U32, name="hcodes%d" % a, align_bytes=64) for a, b in QUANT_CUTS]
+        hscales = [keep.tile([P, b - a, C], U8, name="hscales%d" % a, align_bytes=64) for a, b in QUANT_CUTS]
+        ys0 = [keep.tile([P, PS], F32, name="ys0_%d" % g) for g in range(PAIRS)]
         win = [keep.tile([P, T], F32, name="win%d" % t) for t in range(2)]
         res = [keep.tile([P, T], F32, name="res%d" % t) for t in range(2)]
         base0 = keep.tile([P, T], F32, name="base0")
         half = keep.tile([P, T], F32, name="half")
-        bank = [psum.tile([P, 512], F32, name="bank%d" % b) for b in range(8)]
-        wide, alt, spare = bank[0:3], bank[3:5], bank[5:8]
 
-        nc.vector.memset(xs[:].bitcast(I32), 0)
-        nc.vector.memset(warm[:, 0:8], 0.0)
-        nc.vector.memset(was[:, 0:4, :].bitcast(I32), 0)
-        nc.vector.memset(wbs[:].bitcast(I32), 0)
-        nc.vector.memset(was[:, 4:E, :].bitcast(I32), 0)
-        nc.gpsimd.dma_start(out=wa[:].bitcast(I32), in_=wa_words.bitcast(I32)[0:EARLY, 0].rearrange("e p n -> p e n"))
-        make_identity(nc, ident[:])
+        warm = placed(late, "warm", [P, 4800], F32, 2048)
+        wa = [placed(late, "wa%d" % a, [P, b - a, 2 * H], U8, a * 2 * H) for a, b in WA_CUTS]
+        wb = [placed(late, "wb%d" % a, [P, b - a, 2 * N], U8, 10240 + a * 2 * N) for a, b in WB_CUTS]
+        gates = [placed(late, "gates%d" % a, [P, b - a, PS], F32, 15360 + a * 4 * PS) for a, b in GATE_CUTS]
+        ww = placed(late, "ww", [P, 2 * N], U8, 20480)
+        ws = placed(late, "ws", [P, N], U8, 20992)
+
+        def pick(tiles, cuts, e):
+            i = [j for j, (a, b) in enumerate(cuts) if a <= e < b][0]
+            return tiles[i][:, e - cuts[i][0], :]
+
+        step = 2048
+        hb = [placed(shared, "hb%d" % g, [P, 2, H], BF16, g * step) for g in range(PAIRS)]
+        hin = [placed(shared, "hin%d" % g, [P, 8 * C], BF16, (PAIRS + g) * step) for g in range(PAIRS)]
+        own = 2 * PAIRS * step
+        ys1_at = [2 * step, 3 * step, 4 * step, own, own + 1024]
+        ys1 = [placed(shared, "ys1_%d" % g, [P, PS], F32, ys1_at[g]) for g in range(PAIRS)]
+        gather_at = [own + step, own + 2 * step, own + step, PAIRS * step, (PAIRS + 1) * step]
+        xwg = [placed(shared, "xwg%d" % g, [P, PS], U32, gather_at[g]) for g in range(PAIRS)]
+        xsg = [placed(shared, "xsg%d" % g, [P, PS], U8, gather_at[g] + 1024) for g in range(PAIRS)]
+
+        bank = [psum.tile([P, 512], F32, name="bank%d" % b) for b in range(8)]
+        wide, turn, second, route = bank[0:3], bank[3:5], bank[5:7], [bank[3], bank[4], bank[7]]
 
         def load_plane(queue, plane, rows):
             src = rows.bitcast(I32).rearrange("(q r) n -> r q n", r=4)
             for r in range(4):
                 queue.dma_start(out=plane[r:P:32, :].bitcast(I32), in_=src[r])
 
-        def load_planes(planes, rows, e0, e1):
+        def load_planes(planes, rows, cut):
+            e0, e1 = cut
             src = rows.bitcast(I32)[e0:e1, 0].rearrange("e (q r) n -> r q e n", r=4)
             for r in range(4):
-                nc.sync.dma_start(out=planes[r:P:32, e0:e1, :].bitcast(I32), in_=src[r])
+                nc.sync.dma_start(out=planes[r:P:32, :, :].bitcast(I32), in_=src[r])
 
-        def load_words(words, src, e0, e1, first=0, queue=nc.sync):
+        def load_gates(i):
+            a, b = GATE_CUTS[i]
+            nc.sync.dma_start(out=gates[i][:].rearrange("p g j -> p (g j)"), in_=gate[:, a * PS : b * PS])
+
+        def load_words(queue, words, src, cut):
+            e0, e1 = cut
             queue.dma_start(
-                out=words[:, e0 - first : e1 - first, :].bitcast(I32), in_=src.bitcast(I32)[e0:e1, 0].rearrange("e p n -> p e n")
+                out=words[:].bitcast(I32),
+                in_=src.bitcast(I32)[e0:e1, 0].rearrange("e p n -> p e n"),
             )
+
+        nc.vector.memset(xs[:].bitcast(I32), 0)
+        nc.vector.memset(was[0][:].bitcast(I32), 0)
+        nc.vector.memset(warm[:, 0:8], 0.0)
+        nc.vector.memset(wbs[:].bitcast(I32), 0)
+        nc.vector.memset(was[1][:].bitcast(I32), 0)
 
         nc.sync.dma_start(offsets[:], offs)
         nc.sync.dma_start(out=xw[:], in_=x_words[0].rearrange("p t d -> p (t d)").bitcast(I32))
+        load_words(nc.gpsimd, wa[0], wa_words, WA_CUTS[0])
         load_plane(nc.scalar, xs, x_scales[0])
+        load_planes(was[0], wa_scales, WAS_CUTS[0])
         nc.scalar.activation(out=warm[:, 8:16], in_=warm[:, 0:8], func=ACT.Gelu_apprx_tanh)
-        load_planes(was, wa_scales, 0, 4)
-        load_words(wa_late, wa_words, 2, 4, EARLY)
-        load_planes(wbs, wb_scales, 0, E)
-        load_words(wb, wb_words, 0, 2)
-        load_planes(was, wa_scales, 4, E)
-        load_words(wa_late, wa_words, 4, 6, EARLY)
-        nc.sync.dma_start(out=gates[:, 0:PS], in_=gate[:, 0:PS])
-        load_words(wa_late, wa_words, 6, 8, EARLY)
-        load_words(wb, wb_words, 2, 6)
-        nc.sync.dma_start(out=gates[:, PS:T], in_=gate[:, PS:T])
-        load_words(wa_late, wa_words, 8, E, EARLY)
-        load_words(wb, wb_words, 6, E)
+        make_identity(nc, ident[:])
+        load_words(nc.sync, wa[1], wa_words, WA_CUTS[1])
+        load_planes(wbs, wb_scales, (0, E))
+        load_words(nc.sync, wb[0], wb_words, WB_CUTS[0])
+        load_words(nc.sync, wa[2], wa_words, WA_CUTS[2])
+        load_planes(was[1], wa_scales, WAS_CUTS[1])
+        load_gates(0)
+        load_words(nc.sync, wa[3], wa_words, WA_CUTS[3])
+        load_words(nc.sync, wb[1], wb_words, WB_CUTS[1])
+        load_gates(1)
         nc.gpsimd.memset(ws[:].bitcast(I32), 0)
         load_plane(nc.sync, ws, w_scales[0])
         nc.sync.dma_start(out=ww[:].bitcast(I32), in_=w_words[0].bitcast(I32))
 
-        def gather_bytes(dst, a, b):
-            nc.vector.tensor_copy(out=dst, in_=xs[:].indirect(offsets[:, a // 16 : b // 16]))
-
-        def gather_words(dst, a, b):
-            nc.vector.tensor_copy(out=dst, in_=xw[:].bitcast(U32).indirect(offsets[:, a // 16 : b // 16]))
-
-        def gather(i):
-            gather_bytes(xsg[i][:], *PIECES[i])
-            gather_words(xwg[i][:], *PIECES[i])
+        def gather(g):
+            cols = offsets[:, g * PS // 16 : (g + 1) * PS // 16]
+            nc.vector.tensor_copy(out=xsg[g][:], in_=xs[:].indirect(cols))
+            nc.vector.tensor_copy(out=xwg[g][:], in_=xw[:].bitcast(U32).indirect(cols))
 
         def first_layer(e):
-            a, b = e * C, (e + 1) * C
-            i = [j for j, (lo, hi) in enumerate(PIECES) if lo <= a < hi][0]
-            words = xwg[i][:, a - PIECES[i][0] : b - PIECES[i][0]]
-            scales = xsg[i][:, a - PIECES[i][0] : b - PIECES[i][0]]
-            moving = wa[:, e, :] if e < EARLY else wa_late[:, e - EARLY, :]
+            slots = slice((e % 2) * C, (e % 2 + 1) * C)
             acc = wide[e % 3]
             nc.tensor.matmul_mx(
                 out=acc[:],
-                lhsT=words.bitcast(FP8X4),
-                lhsT_scale=scales,
-                rhs=moving.bitcast(FP4X4),
-                rhs_scale=was[:, e, :],
+                lhsT=xwg[e // 2][:, slots].bitcast(FP8X4),
+                lhsT_scale=xsg[e // 2][:, slots],
+                rhs=pick(wa, WA_CUTS, e).bitcast(FP4X4),
+                rhs_scale=pick(was, WAS_CUTS, e),
                 start=True,
                 stop=True,
             )
             nc.scalar.activation(
-                out=hb[:, e, :].rearrange("j (u p d) -> j u p d", u=2, d=2),
+                out=hb[e // 2][:, e % 2, :].rearrange("j (u p d) -> j u p d", u=2, d=2),
                 in_=acc[:].rearrange("j (p u d) -> j u p d", u=2, d=2),
                 func=ACT.Gelu_apprx_tanh,
             )
 
-        def turn_and_quantise(e0, e1, acc, grouped):
+        def turn_and_quantise(e0, e1, acc):
             m = e1 - e0
+            g, x0 = e0 // 2, e0 % 2
+            grouped = hin[g][:, x0 * 4 * C : (x0 + m) * 4 * C]
             turned = acc[:, 0 : m * 2 * C].rearrange("p (x u j) -> p x u j", x=m, u=2)
             for x in range(m):
-                words = hb[:, e0 + x, :].bitcast(F32)
+                words = hb[g][:, x0 + x, :].bitcast(F32)
                 for u in range(2):
                     nc.tensor.transpose(turned[:, x, u, :], words[:, u * P : (u + 1) * P], ident[:])
             nc.scalar.copy(
                 out=grouped.bitcast(F32).rearrange("p (x j u) -> p x j u", x=m, u=2),
                 in_=turned.rearrange("p x u j -> p x j u"),
             )
+            i = QUANT_CUTS.index((e0, e1))
             nc.vector.quantize_mx(
-                out=hcodes[:, e0 * C : e1 * C].bitcast(FP8X4), scales=hscales[:, e0 * C : e1 * C], in_=grouped
+                out=hcodes[i][:].rearrange("p x j -> p (x j)").bitcast(FP8X4),
+                scales=hscales[i][:].rearrange("p x j -> p (x j)"),
+                in_=grouped,
             )
 
         def pair_stage(g):
             first_layer(2 * g)
             first_layer(2 * g + 1)
-            turn_and_quantise(2 * g, 2 * g + 2, alt[g % 2], hin[:, 2 * g : 2 * g + 2, :].rearrange("p x c -> p (x c)"))
+            turn_and_quantise(2 * g, 2 * g + 2, turn[g % 2])
 
-        def second_layer(t, e0, e1, acc):
-            for e in range(e0, e1):
+        def second_layer(t, g, acc):
+            for x in range(2):
+                e = 2 * g + x
                 nc.tensor.matmul_mx(
-                    out=acc[:, (e - e0) * C : (e - e0 + 1) * C],
-                    lhsT=wb[:, e, t * 2 * P : (t + 1) * 2 * P].bitcast(FP4X4),
+                    out=acc[:, x * C : (x + 1) * C],
+                    lhsT=pick(wb, WB_CUTS, e)[:, t * 2 * P : (t + 1) * 2 * P].bitcast(FP4X4),
                     lhsT_scale=wbs[:, e, t * P : (t + 1) * P],
-                    rhs=hcodes[:, e * C : (e + 1) * C].bitcast(FP8X4),
-                    rhs_scale=hscales[:, e * C : (e + 1) * C],
+                    rhs=pick(hcodes, QUANT_CUTS, e).bitcast(FP8X4),
+                    rhs_scale=pick(hscales, QUANT_CUTS, e),
                     start=True,
                     stop=True,
                 )
-            nc.scalar.copy(out=ys[:, t, e0 * C : e1 * C], in_=acc[:, 0 : (e1 - e0) * C])
 
-        def scatter(t, e0, e1):
-            a, b = e0 * C, e1 * C
+        def scatter(t, g, values):
+            a, b = g * PS, (g + 1) * PS
             nc.vector.tensor_tensor(
-                out=win[t][:].indirect(offsets[:, a // 16 : b // 16]), in0=ys[:, t, a:b], in1=gates[:, a:b], op=MULT
+                out=win[t][:].indirect(offsets[:, a // 16 : b // 16]), in0=values, in1=pick(gates, GATE_CUTS, g), op=MULT
             )
+
+        def upper(g):
+            acc = second[g % 2]
+            second_layer(0, g, acc[:, 0:PS])
+            if g > 0:
+                second_layer(1, g - 1, acc[:, PS : 2 * PS])
+            nc.scalar.copy(out=ys0[g][:], in_=acc[:, 0:PS])
+            scatter(0, g, ys0[g][:])
+
+        def lower(g):
+            nc.scalar.copy(out=ys1[g][:], in_=second[(g + 1) % 2][:, PS : 2 * PS])
+            scatter(1, g, ys1[g][:])
 
         def frozen(t, i):
             a, b = TOKEN_CHUNKS[i]
+            acc = wide[(E + i) % 3][:, 0 : b - a]
             nc.tensor.matmul_mx(
-                out=wide[(E + i) % 3][:, 0 : b - a],
+                out=acc,
                 lhsT=ww[:, t * 2 * P : (t + 1) * 2 * P].bitcast(FP4X4),
                 lhsT_scale=ws[:, t * P : (t + 1) * P],
                 rhs=xw[:, a:b].bitcast(FP8X4),
@@ -197,54 +219,54 @@ def tile_moe_adp_gelu_kernel(
                 start=True,
                 stop=True,
             )
-            return wide[(E + i) % 3][:, 0 : b - a]
+            return acc
 
-        def finish_direct(t):
-            for i, (a, b) in enumerate(TOKEN_CHUNKS):
-                acc = frozen(t, i)
-                nc.vector.tensor_tensor(out=res[t][:, a:b], in0=acc, in1=win[t][:, a:b], op=ADD)
-                nc.sync.dma_start(out=out[t * P : (t + 1) * P, a:b], in_=res[t][:, a:b])
-
-        def finish_turned():
-            for i, (a, b) in enumerate(TOKEN_CHUNKS):
-                for c in range(a, b, P):
-                    o = spare[i][:, c - a : c - a + P]
-                    nc.tensor.matmul(o, lhsT=base0[:, c : c + P], rhs=ident[:], start=True, stop=False, is_transpose=True)
-                    nc.tensor.matmul(o, lhsT=win[0][:, c : c + P], rhs=ident[:], start=False, stop=True, is_transpose=True)
-                nc.scalar.copy(out=half[:, a:b], in_=spare[i][:, 0 : b - a])
-            for i, (a, b) in enumerate(TOKEN_CHUNKS):
-                for c in range(a, b, P):
-                    nc.tensor.transpose(spare[i][:, c - a : c - a + P], half[:, c : c + P], ident[:])
-                nc.scalar.copy(out=res[0][:, a:b], in_=spare[i][:, 0 : b - a])
-                nc.sync.dma_start(out=out[0:P, a:b], in_=res[0][:, a:b])
+        def turn_into(i, src, start, stop):
+            a, b = TOKEN_CHUNKS[i]
+            for c in range(a, b, P):
+                nc.tensor.matmul(
+                    route[i][:, c - a : c - a + P],
+                    lhsT=src[:, c : c + P],
+                    rhs=ident[:],
+                    start=start and c == a,
+                    stop=stop and c == b - P,
+                    is_transpose=True,
+                )
 
         gather(0)
         gather(1)
         first_layer(0)
         first_layer(1)
+        turn_and_quantise(0, 1, turn[0])
+        turn_and_quantise(1, 2, turn[1])
         gather(2)
-        turn_and_quantise(0, 1, spare[0], hin[:, 0, :])
-        turn_and_quantise(1, 2, spare[1], hin1[:])
-        second_layer(0, 0, 2, spare[2])
         gather(3)
-        pair_stage(1)
-        scatter(0, 0, 2)
-        second_layer(1, 0, 2, alt[1])
-        for g in range(2, PAIRS):
+        upper(0)
+        for g in range(1, PAIRS):
             pair_stage(g)
-            if g == 2:
-                scatter(1, 0, 2)
+            if g == 1:
+                gather(4)
             else:
-                scatter(0, 2 * g - 4, 2 * g - 2)
-            second_layer(0, 2 * g - 2, 2 * g, alt[g % 2])
-        scatter(0, E - 4, E - 2)
-        second_layer(0, E - 2, E, alt[1])
-        scatter(0, E - 2, E)
-        second_layer(1, 2, 6, alt[1])
-        second_layer(1, 6, E, alt[0])
+                lower(g - 2)
+            upper(g)
+        second_layer(1, PAIRS - 1, second[PAIRS % 2][:, PS : 2 * PS])
         for i, (a, b) in enumerate(TOKEN_CHUNKS):
             nc.scalar.copy(out=base0[:, a:b], in_=frozen(0, i))
-        finish_turned()
-        scatter(1, 2, 6)
-        scatter(1, 6, E)
-        finish_direct(1)
+            turn_into(i, base0, True, False)
+        lower(PAIRS - 2)
+        lower(PAIRS - 1)
+        for i, (a, b) in enumerate(TOKEN_CHUNKS):
+            turn_into(i, win[0], False, True)
+            nc.scalar.copy(out=half[:, a:b], in_=route[i][:, 0 : b - a])
+        for i, (a, b) in enumerate(TOKEN_CHUNKS):
+            for c in range(a, b, P):
+                nc.tensor.transpose(route[i][:, c - a : c - a + P], half[:, c : c + P], ident[:])
+            nc.scalar.copy(out=res[0][:, a:b], in_=route[i][:, 0 : b - a])
+            nc.sync.dma_start(out=out[0:P, a:b], in_=res[0][:, a:b])
+        for i, (a, b) in enumerate(TOKEN_CHUNKS):
+            acc = frozen(1, i)
+            for c in range(a, b, PS):
+                nc.vector.tensor_tensor(
+                    out=res[1][:, c : c + PS], in0=acc[:, c - a : c - a + PS], in1=win[1][:, c : c + PS], op=ADD
+                )
+                nc.sync.dma_start(out=out[P : 2 * P, c : c + PS], in_=res[1][:, c : c + PS])

@@ -48,9 +48,7 @@ def tile_moe_adp_gelu_kernel(
         was = [keep.tile([P, b - a, H], U8, name="was%d" % a, align_bytes=64) for a, b in WAS_CUTS]
         wbs = keep.tile([P, E, N], U8, name="wbs", align_bytes=64)
         ident = keep.tile([P, P], F32, name="ident")
-        hcodes = [keep.tile([P, b - a, C], U32, name="hcodes%d" % a, align_bytes=64) for a, b in QUANT_CUTS]
         hscales = [keep.tile([P, b - a, C], U8, name="hscales%d" % a, align_bytes=64) for a, b in QUANT_CUTS]
-        ys0 = [keep.tile([P, PS], F32, name="ys0_%d" % g) for g in range(PAIRS)]
         win = [keep.tile([P, T], F32, name="win%d" % t) for t in range(2)]
         res = [keep.tile([P, T], F32, name="res%d" % t) for t in range(2)]
         base0 = keep.tile([P, T], F32, name="base0")
@@ -71,19 +69,28 @@ def tile_moe_adp_gelu_kernel(
         hb = [placed(shared, "hb%d" % g, [P, 2, H], BF16, g * step) for g in range(PAIRS)]
         hin = [placed(shared, "hin%d" % g, [P, 8 * C], BF16, (PAIRS + g) * step) for g in range(PAIRS)]
         own = 2 * PAIRS * step
-        ys1_at = [2 * step, 3 * step, 4 * step, own, own + 1024]
-        ys1 = [placed(shared, "ys1_%d" % g, [P, PS], F32, ys1_at[g]) for g in range(PAIRS)]
-        gather_at = [own + step, own + 2 * step, own + step, PAIRS * step, (PAIRS + 1) * step]
-        xwg = [placed(shared, "xwg%d" % g, [P, PS], U32, gather_at[g]) for g in range(PAIRS)]
-        xsg = [placed(shared, "xsg%d" % g, [P, PS], U8, gather_at[g] + 1024) for g in range(PAIRS)]
+        codes_at = own + 3 * step
+        hcodes = [placed(shared, "hcodes%d" % a, [P, b - a, C], U32, codes_at + a * 4 * C) for a, b in QUANT_CUTS]
+        ys0_at = [codes_at + 4 * step + g * 1024 for g in range(PAIRS)]
+        ys0 = [placed(shared, "ys0_%d" % g, [P, PS], F32, ys0_at[g]) for g in range(PAIRS)]
+        ys1 = [placed(shared, "ys1_%d" % g, [P, PS], F32, (g + 1) * step) for g in range(2)]
+        ys1_rest = placed(shared, "ys1_rest", [P, 3, PS], F32, codes_at + 8 * 4 * C)
+        free_at = codes_at + 7 * step
+        words_at = [free_at, free_at + step, free_at, free_at + 1024, PAIRS * step]
+        bytes_at = [free_at + 1024, free_at + step + 1024, free_at + step + 1280, free_at + step + 1536, PAIRS * step + 1024]
+        xwg = [placed(shared, "xwg%d" % g, [P, PS], U32, words_at[g]) for g in range(PAIRS)]
+        xsg = [placed(shared, "xsg%d" % g, [P, PS], U8, bytes_at[g]) for g in range(PAIRS)]
 
         bank = [psum.tile([P, 512], F32, name="bank%d" % b) for b in range(8)]
-        wide, turn, second, route = bank[0:3], bank[3:5], bank[5:7], [bank[3], bank[4], bank[7]]
+        wide, turn, second, spare = bank[0:3], bank[3:5], bank[5:7], bank[7]
+        route = [turn[0], turn[1], spare]
+        upper_acc = [second[0][:, 0:PS], second[1][:, 0:PS], wide[1][:, 0:PS], wide[0][:, 0:PS], second[0][:, 0:PS]]
+        lower_acc = [second[0][:, PS:], second[1][:, PS:], turn[0][:, 0:PS], turn[0][:, PS:], second[0][:, PS:]]
 
-        def load_plane(queue, plane, rows):
+        def load_plane(queues, plane, rows):
             src = rows.bitcast(I32).rearrange("(q r) n -> r q n", r=4)
             for r in range(4):
-                queue.dma_start(out=plane[r:P:32, :].bitcast(I32), in_=src[r])
+                queues[r].dma_start(out=plane[r:P:32, :].bitcast(I32), in_=src[r])
 
         def load_planes(planes, rows, cut):
             e0, e1 = cut
@@ -111,7 +118,7 @@ def tile_moe_adp_gelu_kernel(
         nc.sync.dma_start(offsets[:], offs)
         nc.sync.dma_start(out=xw[:], in_=x_words[0].rearrange("p t d -> p (t d)").bitcast(I32))
         load_words(nc.gpsimd, wa[0], wa_words, WA_CUTS[0])
-        load_plane(nc.scalar, xs, x_scales[0])
+        load_plane([nc.sync, nc.scalar, nc.sync, nc.scalar], xs, x_scales[0])
         load_planes(was[0], wa_scales, WAS_CUTS[0])
         nc.scalar.activation(out=warm[:, 8:16], in_=warm[:, 0:8], func=ACT.Gelu_apprx_tanh)
         make_identity(nc, ident[:])
@@ -125,13 +132,16 @@ def tile_moe_adp_gelu_kernel(
         load_words(nc.sync, wb[1], wb_words, WB_CUTS[1])
         load_gates(1)
         nc.gpsimd.memset(ws[:].bitcast(I32), 0)
-        load_plane(nc.sync, ws, w_scales[0])
+        load_plane([nc.sync] * 4, ws, w_scales[0])
         nc.sync.dma_start(out=ww[:].bitcast(I32), in_=w_words[0].bitcast(I32))
 
-        def gather(g):
+        def gather_words(g):
+            cols = offsets[:, g * PS // 16 : (g + 1) * PS // 16]
+            nc.vector.tensor_copy(out=xwg[g][:], in_=xw[:].bitcast(U32).indirect(cols))
+
+        def gather_bytes(g):
             cols = offsets[:, g * PS // 16 : (g + 1) * PS // 16]
             nc.vector.tensor_copy(out=xsg[g][:], in_=xs[:].indirect(cols))
-            nc.vector.tensor_copy(out=xwg[g][:], in_=xw[:].bitcast(U32).indirect(cols))
 
         def first_layer(e):
             slots = slice((e % 2) * C, (e % 2 + 1) * C)
@@ -196,15 +206,11 @@ def tile_moe_adp_gelu_kernel(
             )
 
         def upper(g):
-            acc = second[g % 2]
-            second_layer(0, g, acc[:, 0:PS])
-            if g > 0:
-                second_layer(1, g - 1, acc[:, PS : 2 * PS])
-            nc.scalar.copy(out=ys0[g][:], in_=acc[:, 0:PS])
+            nc.scalar.copy(out=ys0[g][:], in_=upper_acc[g])
             scatter(0, g, ys0[g][:])
 
         def lower(g):
-            nc.scalar.copy(out=ys1[g][:], in_=second[(g + 1) % 2][:, PS : 2 * PS])
+            nc.scalar.copy(out=ys1[g][:], in_=lower_acc[g])
             scatter(1, g, ys1[g][:])
 
         def frozen(t, i):
@@ -233,32 +239,54 @@ def tile_moe_adp_gelu_kernel(
                     is_transpose=True,
                 )
 
-        gather(0)
-        gather(1)
+        gather_words(0)
+        gather_words(1)
+        for g in range(4):
+            gather_bytes(g)
         first_layer(0)
         first_layer(1)
+        gather_words(2)
+        gather_words(3)
         turn_and_quantise(0, 1, turn[0])
         turn_and_quantise(1, 2, turn[1])
-        gather(2)
-        gather(3)
-        upper(0)
-        for g in range(1, PAIRS):
-            pair_stage(g)
-            if g == 1:
-                gather(4)
-            else:
-                lower(g - 2)
+        gather_words(4)
+        gather_bytes(4)
+        for g in (0, 1):
+            second_layer(0, g, upper_acc[g])
+            second_layer(1, g, lower_acc[g])
             upper(g)
-        second_layer(1, PAIRS - 1, second[PAIRS % 2][:, PS : 2 * PS])
+            pair_stage(g + 1)
+            lower(g)
+        pair_stage(3)
+        first_layer(8)
+        second_layer(0, 2, upper_acc[2])
+        upper(2)
+        first_layer(9)
+        turn_and_quantise(8, 10, turn[0])
+        second_layer(0, 3, upper_acc[3])
+        upper(3)
+        second_layer(0, 4, upper_acc[4])
+        second_layer(1, 4, lower_acc[4])
+        upper(4)
+        second_layer(1, 2, lower_acc[2])
+        second_layer(1, 3, lower_acc[3])
+        nc.scalar.copy(out=ys1_rest[:, 0:2, :].rearrange("p g j -> p (g j)"), in_=turn[0][:])
+        nc.scalar.copy(out=ys1_rest[:, 2, :], in_=lower_acc[4])
+        rest = ys1_rest[:].rearrange("p g j -> p (g j)")
+        rest_gates = gates[1][:].rearrange("p g j -> p (g j)")
+        for a, b in ((0, 3 * C), (3 * C, 6 * C)):
+            nc.vector.tensor_tensor(
+                out=win[1][:].indirect(offsets[:, (2 * PS + a) // 16 : (2 * PS + b) // 16]),
+                in0=rest[:, a:b],
+                in1=rest_gates[:, a:b],
+                op=MULT,
+            )
         for i, (a, b) in enumerate(TOKEN_CHUNKS):
             nc.scalar.copy(out=base0[:, a:b], in_=frozen(0, i))
             turn_into(i, base0, True, False)
-        lower(PAIRS - 2)
-        lower(PAIRS - 1)
         for i, (a, b) in enumerate(TOKEN_CHUNKS):
             turn_into(i, win[0], False, True)
             nc.scalar.copy(out=half[:, a:b], in_=route[i][:, 0 : b - a])
-        for i, (a, b) in enumerate(TOKEN_CHUNKS):
             for c in range(a, b, P):
                 nc.tensor.transpose(route[i][:, c - a : c - a + P], half[:, c : c + P], ident[:])
             nc.scalar.copy(out=res[0][:, a:b], in_=route[i][:, 0 : b - a])

@@ -14,19 +14,27 @@ U16 = mybir.dt.uint16
 U8 = mybir.dt.uint8
 FP8X4 = mybir.dt.float8_e4m3fn_x4
 FP4X4 = mybir.dt.float4_e2m1fn_x4
-ACT = mybir.ActivationFunctionType
+GELU = mybir.ActivationFunctionType.Gelu_apprx_tanh
 ADD = mybir.AluOpType.add
 MULT = mybir.AluOpType.mult
 
 P = 128
+BANK = 512
 PAIRS = E // 2
 PS = 2 * C
+PER_COLUMN = 16
+UPPER, LOWER = 0, 1
+FP4_BYTES = 2
+
 WA_CUTS = [(0, 2), (2, 4), (4, 6), (6, 10)]
-WAS_CUTS = [(0, 4), (4, 10)]
+WA_SCALE_CUTS = [(0, 4), (4, 10)]
 WB_CUTS = [(0, 4), (4, 10)]
 GATE_CUTS = [(0, 2), (2, 5)]
 QUANT_CUTS = [(0, 1), (1, 2), (2, 4), (4, 6), (6, 8), (8, 10)]
 TOKEN_CHUNKS = [(0, 512), (512, 1024), (1024, 1280)]
+FILL_PAIRS = 3
+REGION = 2048
+HALF_REGION = REGION // 2
 
 
 def tile_moe_adp_gelu_kernel(
@@ -39,53 +47,81 @@ def tile_moe_adp_gelu_kernel(
         late = ctx.enter_context(tc.tile_pool(name="late", bufs=1))
         psum = ctx.enter_context(tc.psum_pool(name="psum", bufs=1))
 
+        def own(name, shape, dtype):
+            return keep.tile(shape, dtype, name=name, align_bytes=64)
+
         def placed(pool, name, shape, dtype, at):
             return pool.tile(shape, dtype, name=name, align_bytes=64, offset=at)
 
-        offsets = keep.tile([P, T // 16], U16, name="offsets")
-        xw = keep.tile([P, T], I32, name="xw", align_bytes=64)
-        xs = keep.tile([P, T], U8, name="xs", align_bytes=64)
-        was = [keep.tile([P, b - a, H], U8, name="was%d" % a, align_bytes=64) for a, b in WAS_CUTS]
-        wbs = keep.tile([P, E, N], U8, name="wbs", align_bytes=64)
-        ident = keep.tile([P, P], F32, name="ident")
-        hscales = [keep.tile([P, b - a, C], U8, name="hscales%d" % a, align_bytes=64) for a, b in QUANT_CUTS]
-        win = [keep.tile([P, T], F32, name="win%d" % t) for t in range(2)]
-        res = [keep.tile([P, T], F32, name="res%d" % t) for t in range(2)]
-        base0 = keep.tile([P, T], F32, name="base0")
-        half = keep.tile([P, T], F32, name="half")
+        def pick(tiles, cuts, index):
+            i = [j for j, (a, b) in enumerate(cuts) if a <= index < b][0]
+            return tiles[i][:, index - cuts[i][0], :]
 
-        warm = placed(late, "warm", [P, 4800], F32, 2048)
-        wa = [placed(late, "wa%d" % a, [P, b - a, 2 * H], U8, a * 2 * H) for a, b in WA_CUTS]
-        wb = [placed(late, "wb%d" % a, [P, b - a, 2 * N], U8, 10240 + a * 2 * N) for a, b in WB_CUTS]
-        gates = [placed(late, "gates%d" % a, [P, b - a, PS], F32, 15360 + a * 4 * PS) for a, b in GATE_CUTS]
-        ww = placed(late, "ww", [P, 2 * N], U8, 20480)
-        ws = placed(late, "ws", [P, N], U8, 20992)
+        offsets = keep.tile([P, T // PER_COLUMN], U16, name="offsets")
+        xw = own("xw", [P, T], I32)
+        xs = own("xs", [P, T], U8)
+        wa_first = own("wa0", [P, WA_CUTS[0][1], FP4_BYTES * H], U8)
+        was = [own("was%d" % a, [P, b - a, H], U8) for a, b in WA_SCALE_CUTS]
+        wbs = own("wbs", [P, E, N], U8)
+        ident = own("ident", [P, P], F32)
+        hscales = [own("hscales%d" % a, [P, b - a, C], U8) for a, b in QUANT_CUTS]
+        y_upper = [own("y_upper%d" % g, [P, PS], F32) for g in range(PAIRS)]
+        window = [own("window%d" % half, [P, T], F32) for half in (UPPER, LOWER)]
+        result = [own("result%d" % half, [P, T], F32) for half in (UPPER, LOWER)]
+        base_upper = own("base_upper", [P, T], F32)
+        sum_turned = own("sum_turned", [P, T], F32)
 
-        def pick(tiles, cuts, e):
-            i = [j for j, (a, b) in enumerate(cuts) if a <= e < b][0]
-            return tiles[i][:, e - cuts[i][0], :]
+        wa_at = [(a - WA_CUTS[1][0]) * FP4_BYTES * H for a, b in WA_CUTS[1:]]
+        wb_at = (E - WA_CUTS[1][0]) * FP4_BYTES * H
+        gates_at = wb_at + E * FP4_BYTES * N
+        ww_at = gates_at + 4 * T
+        ws_at = ww_at + FP4_BYTES * N
+        warm = placed(late, "warm", [P, (ws_at + N) // 4], F32, 0)
+        wa = [wa_first] + [
+            placed(late, "wa%d" % a, [P, b - a, FP4_BYTES * H], U8, at) for (a, b), at in zip(WA_CUTS[1:], wa_at)
+        ]
+        wb = [placed(late, "wb%d" % a, [P, b - a, FP4_BYTES * N], U8, wb_at + a * FP4_BYTES * N) for a, b in WB_CUTS]
+        gates = [placed(late, "gates%d" % a, [P, b - a, PS], F32, gates_at + a * 4 * PS) for a, b in GATE_CUTS]
+        ww = placed(late, "ww", [P, FP4_BYTES * N], U8, ww_at)
+        ws = placed(late, "ws", [P, N], U8, ws_at)
 
-        step = 2048
-        hb = [placed(shared, "hb%d" % g, [P, 2, H], BF16, g * step) for g in range(PAIRS)]
-        hin = [placed(shared, "hin%d" % g, [P, 8 * C], BF16, (PAIRS + g) * step) for g in range(PAIRS)]
-        own = 2 * PAIRS * step
-        codes_at = own + 3 * step
-        hcodes = [placed(shared, "hcodes%d" % a, [P, b - a, C], U32, codes_at + a * 4 * C) for a, b in QUANT_CUTS]
-        ys0_at = [codes_at + 4 * step + g * 1024 for g in range(PAIRS)]
-        ys0 = [placed(shared, "ys0_%d" % g, [P, PS], F32, ys0_at[g]) for g in range(PAIRS)]
-        ys1 = [placed(shared, "ys1_%d" % g, [P, PS], F32, (g + 1) * step) for g in range(2)]
-        ys1_rest = placed(shared, "ys1_rest", [P, 3, PS], F32, codes_at + 8 * 4 * C)
-        free_at = codes_at + 7 * step
-        words_at = [free_at, free_at + step, free_at, free_at + 1024, PAIRS * step]
-        bytes_at = [free_at + 1024, free_at + step + 1024, free_at + step + 1280, free_at + step + 1536, PAIRS * step + 1024]
-        xwg = [placed(shared, "xwg%d" % g, [P, PS], U32, words_at[g]) for g in range(PAIRS)]
-        xsg = [placed(shared, "xsg%d" % g, [P, PS], U8, bytes_at[g]) for g in range(PAIRS)]
+        h_rows = []
+        for g in range(PAIRS):
+            if 1 <= g <= FILL_PAIRS:
+                h_rows.append(placed(shared, "h_rows%d" % g, [P, 2, H], BF16, (g - 1) * REGION))
+            else:
+                h_rows.append(own("h_rows%d" % g, [P, 2, H], BF16))
+        y_lower = [placed(shared, "y_lower%d" % g, [P, PS], F32, g * REGION) for g in range(FILL_PAIRS)]
+        first_at = FILL_PAIRS * REGION
+        last_at = first_at + REGION
+        xwg = [
+            placed(shared, "xwg0", [P, PS], U32, first_at),
+            own("xwg1", [P, PS], U32),
+            placed(shared, "xwg2", [P, PS], U32, first_at),
+            placed(shared, "xwg3", [P, PS], U32, first_at + HALF_REGION),
+            placed(shared, "xwg4", [P, PS], U32, last_at),
+        ]
+        xsg = [placed(shared, "xsg0", [P, PS], U8, first_at + HALF_REGION)]
+        xsg += [own("xsg%d" % g, [P, PS], U8) for g in range(1, PAIRS - 1)]
+        xsg += [placed(shared, "xsg4", [P, PS], U8, last_at + HALF_REGION)]
+        h_cols = [placed(shared, "h_cols0", [P, 4 * PS], BF16, last_at)]
+        h_cols += [own("h_cols%d" % g, [P, 4 * PS], BF16) for g in range(1, PAIRS)]
+        rest_at = last_at + REGION
+        hcodes = [own("hcodes%d" % a, [P, b - a, C], U32) for a, b in QUANT_CUTS[:-1]]
+        hcodes += [placed(shared, "hcodes_last", [P, 2, C], U32, rest_at)]
+        y_rest = placed(shared, "y_rest", [P, PAIRS - FILL_PAIRS, PS], F32, rest_at)
 
-        bank = [psum.tile([P, 512], F32, name="bank%d" % b) for b in range(8)]
-        wide, turn, second, spare = bank[0:3], bank[3:5], bank[5:7], bank[7]
-        route = [turn[0], turn[1], spare]
-        upper_acc = [second[0][:, 0:PS], second[1][:, 0:PS], wide[1][:, 0:PS], wide[0][:, 0:PS], second[0][:, 0:PS]]
-        lower_acc = [second[0][:, PS:], second[1][:, PS:], turn[0][:, 0:PS], turn[0][:, PS:], second[0][:, PS:]]
+        bank = [psum.tile([P, BANK], F32, name="bank%d" % b) for b in range(8)]
+        wide = bank[0:3]
+        turn = bank[3:5]
+        second = bank[5:7]
+        summing = [bank[3], bank[4], bank[7]]
+        upper_acc = [second[g % 2][:, 0:PS] for g in range(PAIRS)]
+        lower_acc = [second[g % 2][:, PS:] for g in range(PAIRS)]
+        upper_acc[3] = wide[(E - 1) % 3][:, 0:PS]
+        lower_acc[3] = turn[(PAIRS - 1) % 2][:, 0:PS]
+        upper_acc[4] = second[1][:, 0:PS]
+        lower_acc[4] = second[1][:, PS:]
 
         def load_plane(queues, plane, rows):
             src = rows.bitcast(I32).rearrange("(q r) n -> r q n", r=4)
@@ -93,21 +129,18 @@ def tile_moe_adp_gelu_kernel(
                 queues[r].dma_start(out=plane[r:P:32, :].bitcast(I32), in_=src[r])
 
         def load_planes(planes, rows, cut):
-            e0, e1 = cut
-            src = rows.bitcast(I32)[e0:e1, 0].rearrange("e (q r) n -> r q e n", r=4)
+            src = rows.bitcast(I32)[cut[0] : cut[1], 0].rearrange("e (q r) n -> r q e n", r=4)
             for r in range(4):
                 nc.sync.dma_start(out=planes[r:P:32, :, :].bitcast(I32), in_=src[r])
+
+        def load_words(queue, words, src, cut):
+            queue.dma_start(
+                out=words[:].bitcast(I32), in_=src.bitcast(I32)[cut[0] : cut[1], 0].rearrange("e p n -> p e n")
+            )
 
         def load_gates(i):
             a, b = GATE_CUTS[i]
             nc.sync.dma_start(out=gates[i][:].rearrange("p g j -> p (g j)"), in_=gate[:, a * PS : b * PS])
-
-        def load_words(queue, words, src, cut):
-            e0, e1 = cut
-            queue.dma_start(
-                out=words[:].bitcast(I32),
-                in_=src.bitcast(I32)[e0:e1, 0].rearrange("e p n -> p e n"),
-            )
 
         nc.vector.memset(xs[:].bitcast(I32), 0)
         nc.vector.memset(was[0][:].bitcast(I32), 0)
@@ -119,14 +152,14 @@ def tile_moe_adp_gelu_kernel(
         nc.sync.dma_start(out=xw[:], in_=x_words[0].rearrange("p t d -> p (t d)").bitcast(I32))
         load_words(nc.gpsimd, wa[0], wa_words, WA_CUTS[0])
         load_plane([nc.sync, nc.scalar, nc.sync, nc.scalar], xs, x_scales[0])
-        load_planes(was[0], wa_scales, WAS_CUTS[0])
-        nc.scalar.activation(out=warm[:, 8:16], in_=warm[:, 0:8], func=ACT.Gelu_apprx_tanh)
+        load_planes(was[0], wa_scales, WA_SCALE_CUTS[0])
+        nc.scalar.activation(out=warm[:, 8:16], in_=warm[:, 0:8], func=GELU)
         make_identity(nc, ident[:])
         load_words(nc.sync, wa[1], wa_words, WA_CUTS[1])
         load_planes(wbs, wb_scales, (0, E))
         load_words(nc.sync, wb[0], wb_words, WB_CUTS[0])
         load_words(nc.sync, wa[2], wa_words, WA_CUTS[2])
-        load_planes(was[1], wa_scales, WAS_CUTS[1])
+        load_planes(was[1], wa_scales, WA_SCALE_CUTS[1])
         load_gates(0)
         load_words(nc.sync, wa[3], wa_words, WA_CUTS[3])
         load_words(nc.sync, wb[1], wb_words, WB_CUTS[1])
@@ -135,39 +168,41 @@ def tile_moe_adp_gelu_kernel(
         load_plane([nc.sync] * 4, ws, w_scales[0])
         nc.sync.dma_start(out=ww[:].bitcast(I32), in_=w_words[0].bitcast(I32))
 
+        def entries(first_pair, end_pair):
+            return offsets[:, first_pair * PS // PER_COLUMN : end_pair * PS // PER_COLUMN]
+
         def gather_words(g):
-            cols = offsets[:, g * PS // 16 : (g + 1) * PS // 16]
-            nc.vector.tensor_copy(out=xwg[g][:], in_=xw[:].bitcast(U32).indirect(cols))
+            nc.vector.tensor_copy(out=xwg[g][:], in_=xw[:].bitcast(U32).indirect(entries(g, g + 1)))
 
         def gather_bytes(g):
-            cols = offsets[:, g * PS // 16 : (g + 1) * PS // 16]
-            nc.vector.tensor_copy(out=xsg[g][:], in_=xs[:].indirect(cols))
+            nc.vector.tensor_copy(out=xsg[g][:], in_=xs[:].indirect(entries(g, g + 1)))
 
         def first_layer(e):
-            slots = slice((e % 2) * C, (e % 2 + 1) * C)
+            g, x = divmod(e, 2)
+            slots = slice(x * C, (x + 1) * C)
             acc = wide[e % 3]
             nc.tensor.matmul_mx(
                 out=acc[:],
-                lhsT=xwg[e // 2][:, slots].bitcast(FP8X4),
-                lhsT_scale=xsg[e // 2][:, slots],
+                lhsT=xwg[g][:, slots].bitcast(FP8X4),
+                lhsT_scale=xsg[g][:, slots],
                 rhs=pick(wa, WA_CUTS, e).bitcast(FP4X4),
-                rhs_scale=pick(was, WAS_CUTS, e),
+                rhs_scale=pick(was, WA_SCALE_CUTS, e),
                 start=True,
                 stop=True,
             )
             nc.scalar.activation(
-                out=hb[e // 2][:, e % 2, :].rearrange("j (u p d) -> j u p d", u=2, d=2),
+                out=h_rows[g][:, x, :].rearrange("j (u p d) -> j u p d", u=2, d=2),
                 in_=acc[:].rearrange("j (p u d) -> j u p d", u=2, d=2),
-                func=ACT.Gelu_apprx_tanh,
+                func=GELU,
             )
 
         def turn_and_quantise(e0, e1, acc):
             m = e1 - e0
-            g, x0 = e0 // 2, e0 % 2
-            grouped = hin[g][:, x0 * 4 * C : (x0 + m) * 4 * C]
+            g, x0 = divmod(e0, 2)
+            grouped = h_cols[g][:, x0 * 4 * C : (x0 + m) * 4 * C]
             turned = acc[:, 0 : m * 2 * C].rearrange("p (x u j) -> p x u j", x=m, u=2)
             for x in range(m):
-                words = hb[g][:, x0 + x, :].bitcast(F32)
+                words = h_rows[g][:, x0 + x, :].bitcast(F32)
                 for u in range(2):
                     nc.tensor.transpose(turned[:, x, u, :], words[:, u * P : (u + 1) * P], ident[:])
             nc.scalar.copy(
@@ -181,45 +216,44 @@ def tile_moe_adp_gelu_kernel(
                 in_=grouped,
             )
 
-        def pair_stage(g):
+        def pair_to_codes(g):
             first_layer(2 * g)
             first_layer(2 * g + 1)
             turn_and_quantise(2 * g, 2 * g + 2, turn[g % 2])
 
-        def second_layer(t, g, acc):
+        def second_layer(half, g, acc):
             for x in range(2):
                 e = 2 * g + x
                 nc.tensor.matmul_mx(
                     out=acc[:, x * C : (x + 1) * C],
-                    lhsT=pick(wb, WB_CUTS, e)[:, t * 2 * P : (t + 1) * 2 * P].bitcast(FP4X4),
-                    lhsT_scale=wbs[:, e, t * P : (t + 1) * P],
+                    lhsT=pick(wb, WB_CUTS, e)[:, half * FP4_BYTES * P : (half + 1) * FP4_BYTES * P].bitcast(FP4X4),
+                    lhsT_scale=wbs[:, e, half * P : (half + 1) * P],
                     rhs=pick(hcodes, QUANT_CUTS, e).bitcast(FP8X4),
                     rhs_scale=pick(hscales, QUANT_CUTS, e),
                     start=True,
                     stop=True,
                 )
 
-        def scatter(t, g, values):
-            a, b = g * PS, (g + 1) * PS
+        def scatter(half, first_pair, end_pair, values, weights):
             nc.vector.tensor_tensor(
-                out=win[t][:].indirect(offsets[:, a // 16 : b // 16]), in0=values, in1=pick(gates, GATE_CUTS, g), op=MULT
+                out=window[half][:].indirect(entries(first_pair, end_pair)), in0=values, in1=weights, op=MULT
             )
 
         def upper(g):
-            nc.scalar.copy(out=ys0[g][:], in_=upper_acc[g])
-            scatter(0, g, ys0[g][:])
+            nc.scalar.copy(out=y_upper[g][:], in_=upper_acc[g])
+            scatter(UPPER, g, g + 1, y_upper[g][:], pick(gates, GATE_CUTS, g))
 
         def lower(g):
-            nc.scalar.copy(out=ys1[g][:], in_=lower_acc[g])
-            scatter(1, g, ys1[g][:])
+            nc.scalar.copy(out=y_lower[g][:], in_=lower_acc[g])
+            scatter(LOWER, g, g + 1, y_lower[g][:], pick(gates, GATE_CUTS, g))
 
-        def frozen(t, i):
+        def frozen(half, i):
             a, b = TOKEN_CHUNKS[i]
             acc = wide[(E + i) % 3][:, 0 : b - a]
             nc.tensor.matmul_mx(
                 out=acc,
-                lhsT=ww[:, t * 2 * P : (t + 1) * 2 * P].bitcast(FP4X4),
-                lhsT_scale=ws[:, t * P : (t + 1) * P],
+                lhsT=ww[:, half * FP4_BYTES * P : (half + 1) * FP4_BYTES * P].bitcast(FP4X4),
+                lhsT_scale=ws[:, half * P : (half + 1) * P],
                 rhs=xw[:, a:b].bitcast(FP8X4),
                 rhs_scale=xs[:, a:b],
                 start=True,
@@ -227,21 +261,21 @@ def tile_moe_adp_gelu_kernel(
             )
             return acc
 
-        def turn_into(i, src, start, stop):
+        def turn_into_sum(i, src, opens, closes):
             a, b = TOKEN_CHUNKS[i]
             for c in range(a, b, P):
                 nc.tensor.matmul(
-                    route[i][:, c - a : c - a + P],
+                    summing[i][:, c - a : c - a + P],
                     lhsT=src[:, c : c + P],
                     rhs=ident[:],
-                    start=start and c == a,
-                    stop=stop and c == b - P,
+                    start=opens and c == a,
+                    stop=closes and c == b - P,
                     is_transpose=True,
                 )
 
         gather_words(0)
         gather_words(1)
-        for g in range(4):
+        for g in range(PAIRS - 1):
             gather_bytes(g)
         first_layer(0)
         first_layer(1)
@@ -249,52 +283,49 @@ def tile_moe_adp_gelu_kernel(
         gather_words(3)
         turn_and_quantise(0, 1, turn[0])
         turn_and_quantise(1, 2, turn[1])
-        gather_words(4)
-        gather_bytes(4)
-        for g in (0, 1):
-            second_layer(0, g, upper_acc[g])
-            second_layer(1, g, lower_acc[g])
+        gather_words(PAIRS - 1)
+        gather_bytes(PAIRS - 1)
+        for g in range(FILL_PAIRS):
+            second_layer(UPPER, g, upper_acc[g])
+            second_layer(LOWER, g, lower_acc[g])
             upper(g)
-            pair_stage(g + 1)
+            pair_to_codes(g + 1)
             lower(g)
-        pair_stage(3)
-        first_layer(8)
-        second_layer(0, 2, upper_acc[2])
-        upper(2)
-        first_layer(9)
-        turn_and_quantise(8, 10, turn[0])
-        second_layer(0, 3, upper_acc[3])
+        pair_to_codes(4)
+        second_layer(UPPER, 3, upper_acc[3])
         upper(3)
-        second_layer(0, 4, upper_acc[4])
-        second_layer(1, 4, lower_acc[4])
+        second_layer(UPPER, 4, upper_acc[4])
+        second_layer(LOWER, 4, lower_acc[4])
         upper(4)
-        second_layer(1, 2, lower_acc[2])
-        second_layer(1, 3, lower_acc[3])
-        nc.scalar.copy(out=ys1_rest[:, 0:2, :].rearrange("p g j -> p (g j)"), in_=turn[0][:])
-        nc.scalar.copy(out=ys1_rest[:, 2, :], in_=lower_acc[4])
-        rest = ys1_rest[:].rearrange("p g j -> p (g j)")
-        rest_gates = gates[1][:].rearrange("p g j -> p (g j)")
-        for a, b in ((0, 3 * C), (3 * C, 6 * C)):
-            nc.vector.tensor_tensor(
-                out=win[1][:].indirect(offsets[:, (2 * PS + a) // 16 : (2 * PS + b) // 16]),
-                in0=rest[:, a:b],
-                in1=rest_gates[:, a:b],
-                op=MULT,
-            )
+        second_layer(LOWER, 3, lower_acc[3])
+        for g in range(FILL_PAIRS, PAIRS):
+            nc.scalar.copy(out=y_rest[:, g - FILL_PAIRS, :], in_=lower_acc[g])
+        scatter(
+            LOWER,
+            FILL_PAIRS,
+            PAIRS,
+            y_rest[:].rearrange("p g j -> p (g j)"),
+            gates[1][:, FILL_PAIRS - GATE_CUTS[1][0] :, :].rearrange("p g j -> p (g j)"),
+        )
+
         for i, (a, b) in enumerate(TOKEN_CHUNKS):
-            nc.scalar.copy(out=base0[:, a:b], in_=frozen(0, i))
-            turn_into(i, base0, True, False)
+            nc.scalar.copy(out=base_upper[:, a:b], in_=frozen(UPPER, i))
+            turn_into_sum(i, base_upper, True, False)
         for i, (a, b) in enumerate(TOKEN_CHUNKS):
-            turn_into(i, win[0], False, True)
-            nc.scalar.copy(out=half[:, a:b], in_=route[i][:, 0 : b - a])
+            turn_into_sum(i, window[UPPER], False, True)
+            nc.scalar.copy(out=sum_turned[:, a:b], in_=summing[i][:, 0 : b - a])
             for c in range(a, b, P):
-                nc.tensor.transpose(route[i][:, c - a : c - a + P], half[:, c : c + P], ident[:])
-            nc.scalar.copy(out=res[0][:, a:b], in_=route[i][:, 0 : b - a])
-            nc.sync.dma_start(out=out[0:P, a:b], in_=res[0][:, a:b])
+                nc.tensor.transpose(summing[i][:, c - a : c - a + P], sum_turned[:, c : c + P], ident[:])
+            nc.scalar.copy(out=result[UPPER][:, a:b], in_=summing[i][:, 0 : b - a])
+            nc.scalar.dma_start(out=out[0:P, a:b], in_=result[UPPER][:, a:b])
+
         for i, (a, b) in enumerate(TOKEN_CHUNKS):
-            acc = frozen(1, i)
+            acc = frozen(LOWER, i)
             for c in range(a, b, PS):
                 nc.vector.tensor_tensor(
-                    out=res[1][:, c : c + PS], in0=acc[:, c - a : c - a + PS], in1=win[1][:, c : c + PS], op=ADD
+                    out=result[LOWER][:, c : c + PS],
+                    in0=acc[:, c - a : c - a + PS],
+                    in1=window[LOWER][:, c : c + PS],
+                    op=ADD,
                 )
-                nc.sync.dma_start(out=out[P : 2 * P, c : c + PS], in_=res[1][:, c : c + PS])
+                nc.sync.dma_start(out=out[P : 2 * P, c : c + PS], in_=result[LOWER][:, c : c + PS])

@@ -26,13 +26,14 @@ PER_COLUMN = 16
 UPPER, LOWER = 0, 1
 FP4_BYTES = 2
 
-WA_CUTS = [(0, 2), (2, 4), (4, 6), (6, 10)]
+WA_CUTS = [(0, 2), (2, 4), (4, 6), (6, 8), (8, 10)]
 WA_SCALE_CUTS = [(0, 4), (4, 10)]
 WB_CUTS = [(0, 4), (4, 10)]
 GATE_CUTS = [(0, 2), (2, 5)]
-QUANT_CUTS = [(0, 1), (1, 2), (2, 4), (4, 6), (6, 8), (8, 10)]
+WORD_CUTS = [(0, 1), (1, 3), (3, 5)]
+BYTE_CUTS = [(0, 1), (1, 3), (3, 5)]
 TOKEN_CHUNKS = [(0, 512), (512, 1024), (1024, 1280)]
-FILL_PAIRS = 3
+WINDOW = 2048
 REGION = 2048
 HALF_REGION = REGION // 2
 
@@ -44,6 +45,7 @@ def tile_moe_adp_gelu_kernel(
     with ExitStack() as ctx:
         keep = ctx.enter_context(tc.tile_pool(name="keep", bufs=1))
         shared = ctx.enter_context(tc.tile_pool(name="shared", bufs=1))
+        soon = ctx.enter_context(tc.tile_pool(name="soon", bufs=1))
         late = ctx.enter_context(tc.tile_pool(name="late", bufs=1))
         psum = ctx.enter_context(tc.psum_pool(name="psum", bufs=1))
 
@@ -60,143 +62,188 @@ def tile_moe_adp_gelu_kernel(
         offsets = keep.tile([P, T // PER_COLUMN], U16, name="offsets")
         xw = own("xw", [P, T], I32)
         xs = own("xs", [P, T], U8)
-        wa_first = own("wa0", [P, WA_CUTS[0][1], FP4_BYTES * H], U8)
         was = [own("was%d" % a, [P, b - a, H], U8) for a, b in WA_SCALE_CUTS]
         wbs = own("wbs", [P, E, N], U8)
         ident = own("ident", [P, P], F32)
-        hscales = [own("hscales%d" % a, [P, b - a, C], U8) for a, b in QUANT_CUTS]
-        y_upper = [own("y_upper%d" % g, [P, PS], F32) for g in range(PAIRS)]
-        window = [own("window%d" % half, [P, T], F32) for half in (UPPER, LOWER)]
+        hscales = [own("hscales%d" % g, [P, PS], U8) for g in range(PAIRS)]
+        window = [own("window%d" % half, [P, WINDOW], F32) for half in (UPPER, LOWER)]
         result = [own("result%d" % half, [P, T], F32) for half in (UPPER, LOWER)]
-        base_upper = own("base_upper", [P, T], F32)
-        sum_turned = own("sum_turned", [P, T], F32)
 
-        wa_at = [(a - WA_CUTS[1][0]) * FP4_BYTES * H for a, b in WA_CUTS[1:]]
-        wb_at = (E - WA_CUTS[1][0]) * FP4_BYTES * H
-        gates_at = wb_at + E * FP4_BYTES * N
-        ww_at = gates_at + 4 * T
-        ws_at = ww_at + FP4_BYTES * N
-        warm = placed(late, "warm", [P, (ws_at + N) // 4], F32, 0)
-        wa = [wa_first] + [
-            placed(late, "wa%d" % a, [P, b - a, FP4_BYTES * H], U8, at) for (a, b), at in zip(WA_CUTS[1:], wa_at)
+        wa_bytes = FP4_BYTES * H
+        wb_bytes = FP4_BYTES * N
+
+        def laid_out(pool, specs):
+            tiles, at = [], 0
+            for name, shape, dtype, size in specs:
+                tiles.append(placed(pool, name, shape, dtype, at))
+                at = at + size
+            return tiles, at
+
+        soon_specs = [
+            ("wa2", [P, 2, wa_bytes], U8, 2 * wa_bytes),
+            ("wb0", [P, 4, wb_bytes], U8, 4 * wb_bytes),
+            ("gates0", [P, 2 * PS], F32, 8 * PS),
+            ("wa4", [P, 2, wa_bytes], U8, 2 * wa_bytes),
         ]
-        wb = [placed(late, "wb%d" % a, [P, b - a, FP4_BYTES * N], U8, wb_at + a * FP4_BYTES * N) for a, b in WB_CUTS]
-        gates = [placed(late, "gates%d" % a, [P, b - a, PS], F32, gates_at + a * 4 * PS) for a, b in GATE_CUTS]
-        ww = placed(late, "ww", [P, FP4_BYTES * N], U8, ww_at)
-        ws = placed(late, "ws", [P, N], U8, ws_at)
+        warm = placed(soon, "warm", [P, sum([s[3] for s in soon_specs]) // 4], F32, 0)
+        (wa2, wb0, gates0, wa4), soon_end = laid_out(soon, soon_specs)
 
-        h_rows = []
-        for g in range(PAIRS):
-            if 1 <= g <= FILL_PAIRS:
-                h_rows.append(placed(shared, "h_rows%d" % g, [P, 2, H], BF16, (g - 1) * REGION))
-            else:
-                h_rows.append(own("h_rows%d" % g, [P, 2, H], BF16))
-        y_lower = [placed(shared, "y_lower%d" % g, [P, PS], F32, g * REGION) for g in range(FILL_PAIRS)]
-        first_at = FILL_PAIRS * REGION
-        last_at = first_at + REGION
+        late_specs = [
+            ("xwg2", [P, 2, PS], U32, 8 * PS),
+            ("xsg3", [P, 2, PS], U8, 2 * PS),
+            ("wb4", [P, 6, wb_bytes], U8, 6 * wb_bytes),
+            ("gates2", [P, 3 * PS], F32, 12 * PS),
+            ("ww", [P, wb_bytes], U8, wb_bytes),
+            ("ws", [P, N], U8, N),
+            ("wa6", [P, 3, wa_bytes], U8, 3 * wa_bytes),
+            ("h_rows2", [P, 2, H], BF16, 4 * H),
+            ("wa8", [P, 3, wa_bytes], U8, 3 * wa_bytes),
+        ]
+        first_bytes = placed(late, "first_bytes", [P, sum([s[3] for s in late_specs])], U8, 0)
+        (xwg2, xsg3, wb4, gates2, ww, ws, wa6, h_rows2, wa8), late_end = laid_out(late, late_specs)
+        rows2_at = late_end - 3 * wa_bytes - 4 * H
+        wa = [own("wa0", [P, 2, wa_bytes], U8), wa2, wa4, wa6, wa8]
+        wb = [wb0, wb4]
+        gates = [gates0, gates2]
+        xsg = [
+            first_bytes[:, 0:PS].rearrange("p (g j) -> p g j", g=1),
+            own("xsg1", [P, 2, PS], U8)[:],
+            xsg3[:],
+        ]
+
+        h_rows = [own("h_rows0", [P, 2, H], BF16)]
+        h_rows += [
+            placed(shared, "h_rows1", [P, 2, H], BF16, 0),
+            h_rows2,
+            placed(late, "h_rows3", [P, 2, H], BF16, late_end),
+            placed(shared, "h_rows4", [P, 2, H], BF16, 3 * REGION),
+        ]
+        y_upper = [own("y_upper0", [P, PS], F32)]
+        y_upper += [
+            own("y_upper1", [P, PS], F32),
+            placed(late, "y_upper2", [P, PS], F32, late_end - 2 * PS),
+            placed(shared, "y_upper3", [P, PS], F32, 3 * REGION),
+        ]
+        y_upper += [own("y_upper4", [P, PS], F32)]
+        y_lower = [
+            placed(shared, "y_lower0", [P, PS], F32, 0),
+            placed(late, "y_lower1", [P, PS], F32, rows2_at - 2 * PS),
+        ]
+        cols_at = 4 * REGION
+        h_cols = [placed(shared, "h_cols0", [P, 4 * PS], BF16, cols_at)]
+        h_cols += [
+            own("h_cols1", [P, 4 * PS], BF16),
+            placed(late, "h_cols2", [P, 4 * PS], BF16, rows2_at - 3 * wa_bytes),
+            placed(late, "h_cols3", [P, 4 * PS], BF16, late_end - 3 * wa_bytes),
+            own("h_cols4", [P, 4 * PS], BF16),
+        ]
         xwg = [
-            placed(shared, "xwg0", [P, PS], U32, first_at),
-            own("xwg1", [P, PS], U32),
-            placed(shared, "xwg2", [P, PS], U32, first_at),
-            placed(shared, "xwg3", [P, PS], U32, first_at + HALF_REGION),
-            placed(shared, "xwg4", [P, PS], U32, last_at),
+            own("xwg0", [P, 1, PS], U32)[:],
+            xwg2[:],
+            placed(shared, "xwg3", [P, 2, PS], U32, cols_at)[:],
         ]
-        xsg = [placed(shared, "xsg0", [P, PS], U8, first_at + HALF_REGION)]
-        xsg += [own("xsg%d" % g, [P, PS], U8) for g in range(1, PAIRS - 1)]
-        xsg += [placed(shared, "xsg4", [P, PS], U8, last_at + HALF_REGION)]
-        h_cols = [placed(shared, "h_cols0", [P, 4 * PS], BF16, last_at)]
-        h_cols += [own("h_cols%d" % g, [P, 4 * PS], BF16) for g in range(1, PAIRS)]
-        rest_at = last_at + REGION
-        hcodes = [own("hcodes%d" % a, [P, b - a, C], U32) for a, b in QUANT_CUTS[:-1]]
-        hcodes += [placed(shared, "hcodes_last", [P, 2, C], U32, rest_at)]
-        y_rest = placed(shared, "y_rest", [P, PAIRS - FILL_PAIRS, PS], F32, rest_at)
+        hcodes = [own("hcodes%d" % g, [P, PS], U32) for g in range(PAIRS)]
+        y_rest = own("y_rest", [P, 3 * PS], F32)
+        base_at = 3 * REGION + HALF_REGION
+        base_upper = placed(shared, "base_upper", [P, T], F32, base_at)
+        sum_turned = placed(shared, "sum_turned", [P, T], F32, base_at)
 
         bank = [psum.tile([P, BANK], F32, name="bank%d" % b) for b in range(8)]
-        wide = bank[0:3]
+        first_acc = [bank[b] for b in (0, 1, 1, 2, 0, 5, 1, 2, 0, 5)]
+        turn_first = [bank[2], bank[0]]
         turn = bank[3:5]
-        second = bank[5:7]
-        summing = [bank[3], bank[4], bank[7]]
-        upper_acc = [second[g % 2][:, 0:PS] for g in range(PAIRS)]
-        lower_acc = [second[g % 2][:, PS:] for g in range(PAIRS)]
-        upper_acc[3] = wide[(E - 1) % 3][:, 0:PS]
-        lower_acc[3] = turn[(PAIRS - 1) % 2][:, 0:PS]
-        upper_acc[4] = second[1][:, 0:PS]
-        lower_acc[4] = second[1][:, PS:]
+        second = [bank[6]] + [first_acc[2 * g + 3] for g in range(1, PAIRS - 1)]
+        upper_acc = [second[g][:, 0:PS] for g in range(PAIRS - 1)] + [second[3][:, PS:]]
+        lower_acc = [second[g][:, PS:] for g in range(PAIRS - 2)] + [turn[1][:, 0:PS], turn[1][:, PS:]]
+        frozen_acc = bank[0:3]
+        summing = [bank[6], bank[7], bank[3]]
 
-        def load_plane(queues, plane, rows):
+        def load_plane(queue, plane, rows):
             src = rows.bitcast(I32).rearrange("(q r) n -> r q n", r=4)
             for r in range(4):
-                queues[r].dma_start(out=plane[r:P:32, :].bitcast(I32), in_=src[r])
+                queue.dma_start(out=plane[r:P:32, :].bitcast(I32), in_=src[r])
 
-        def load_planes(planes, rows, cut):
+        def load_planes(queues, planes, rows, cut):
             src = rows.bitcast(I32)[cut[0] : cut[1], 0].rearrange("e (q r) n -> r q e n", r=4)
             for r in range(4):
-                nc.sync.dma_start(out=planes[r:P:32, :, :].bitcast(I32), in_=src[r])
+                queues[r].dma_start(out=planes[r:P:32, :, :].bitcast(I32), in_=src[r])
 
         def load_words(queue, words, src, cut):
             queue.dma_start(
-                out=words[:].bitcast(I32), in_=src.bitcast(I32)[cut[0] : cut[1], 0].rearrange("e p n -> p e n")
+                out=words[:, 0 : cut[1] - cut[0], :].bitcast(I32), in_=src.bitcast(I32)[cut[0] : cut[1], 0].rearrange("e p n -> p e n")
             )
 
         def load_gates(i):
             a, b = GATE_CUTS[i]
-            nc.sync.dma_start(out=gates[i][:].rearrange("p g j -> p (g j)"), in_=gate[:, a * PS : b * PS])
+            nc.sync.dma_start(out=gates[i][:], in_=gate[:, a * PS : b * PS])
 
         nc.vector.memset(xs[:].bitcast(I32), 0)
-        nc.vector.memset(was[0][:].bitcast(I32), 0)
         nc.vector.memset(warm[:, 0:8], 0.0)
+        nc.vector.memset(was[0][:].bitcast(I32), 0)
+        nc.vector.memset(ident[:], 0.0)
         nc.vector.memset(wbs[:].bitcast(I32), 0)
-        nc.vector.memset(was[1][:].bitcast(I32), 0)
 
         nc.sync.dma_start(offsets[:], offs)
         nc.sync.dma_start(out=xw[:], in_=x_words[0].rearrange("p t d -> p (t d)").bitcast(I32))
         load_words(nc.gpsimd, wa[0], wa_words, WA_CUTS[0])
-        load_plane([nc.sync, nc.scalar, nc.sync, nc.scalar], xs, x_scales[0])
-        load_planes(was[0], wa_scales, WA_SCALE_CUTS[0])
+        load_plane(nc.sync, xs, x_scales[0])
+        load_planes([nc.sync, nc.sync, nc.sync, nc.gpsimd], was[0], wa_scales, WA_SCALE_CUTS[0])
+        make_identity(nc, ident[:], nomemset=True)
         nc.scalar.activation(out=warm[:, 8:16], in_=warm[:, 0:8], func=GELU)
-        make_identity(nc, ident[:])
+        load_planes([nc.sync] * 4, wbs, wb_scales, (0, E))
         load_words(nc.sync, wa[1], wa_words, WA_CUTS[1])
-        load_planes(wbs, wb_scales, (0, E))
         load_words(nc.sync, wb[0], wb_words, WB_CUTS[0])
-        load_words(nc.sync, wa[2], wa_words, WA_CUTS[2])
-        load_planes(was[1], wa_scales, WA_SCALE_CUTS[1])
         load_gates(0)
-        load_words(nc.sync, wa[3], wa_words, WA_CUTS[3])
-        load_words(nc.sync, wb[1], wb_words, WB_CUTS[1])
-        load_gates(1)
-        nc.gpsimd.memset(ws[:].bitcast(I32), 0)
-        load_plane([nc.sync] * 4, ws, w_scales[0])
-        nc.sync.dma_start(out=ww[:].bitcast(I32), in_=w_words[0].bitcast(I32))
+        load_words(nc.sync, wa[2], wa_words, WA_CUTS[2])
+        nc.vector.memset(was[1][:].bitcast(I32), 0)
+        load_planes([nc.sync] * 4, was[1], wa_scales, WA_SCALE_CUTS[1])
+
+        def late_loads():
+            load_words(nc.sync, wa[3], wa_words, WA_CUTS[3])
+            load_words(nc.sync, wb[1], wb_words, WB_CUTS[1])
+            load_words(nc.sync, wa[4], wa_words, WA_CUTS[4])
+            load_gates(1)
+            nc.gpsimd.memset(ws[:].bitcast(I32), 0)
+            load_plane(nc.sync, ws, w_scales[0])
+            nc.sync.dma_start(out=ww[:].bitcast(I32), in_=w_words[0].bitcast(I32))
 
         def entries(first_pair, end_pair):
             return offsets[:, first_pair * PS // PER_COLUMN : end_pair * PS // PER_COLUMN]
 
-        def gather_words(g):
-            nc.vector.tensor_copy(out=xwg[g][:], in_=xw[:].bitcast(U32).indirect(entries(g, g + 1)))
+        def gather_words(i):
+            nc.vector.tensor_copy(
+                out=xwg[i].rearrange("p g j -> p (g j)"), in_=xw[:].bitcast(U32).indirect(entries(*WORD_CUTS[i]))
+            )
 
-        def gather_bytes(g):
-            nc.vector.tensor_copy(out=xsg[g][:], in_=xs[:].indirect(entries(g, g + 1)))
+        def gather_bytes(i):
+            nc.vector.tensor_copy(
+                out=xsg[i].rearrange("p g j -> p (g j)"), in_=xs[:].indirect(entries(*BYTE_CUTS[i]))
+            )
 
-        def first_layer(e):
+        def first_product(e):
             g, x = divmod(e, 2)
             slots = slice(x * C, (x + 1) * C)
-            acc = wide[e % 3]
+            acc = first_acc[e]
             nc.tensor.matmul_mx(
                 out=acc[:],
-                lhsT=xwg[g][:, slots].bitcast(FP8X4),
-                lhsT_scale=xsg[g][:, slots],
+                lhsT=pick(xwg, WORD_CUTS, g)[:, slots].bitcast(FP8X4),
+                lhsT_scale=pick(xsg, BYTE_CUTS, g)[:, slots],
                 rhs=pick(wa, WA_CUTS, e).bitcast(FP4X4),
                 rhs_scale=pick(was, WA_SCALE_CUTS, e),
                 start=True,
                 stop=True,
             )
+
+        def gelu(e):
+            g, x = divmod(e, 2)
+            acc = first_acc[e]
             nc.scalar.activation(
                 out=h_rows[g][:, x, :].rearrange("j (u p d) -> j u p d", u=2, d=2),
                 in_=acc[:].rearrange("j (p u d) -> j u p d", u=2, d=2),
                 func=GELU,
             )
 
-        def turn_and_quantise(e0, e1, acc):
+        def turn_h(e0, e1, acc):
             m = e1 - e0
             g, x0 = divmod(e0, 2)
             grouped = h_cols[g][:, x0 * 4 * C : (x0 + m) * 4 * C]
@@ -209,47 +256,56 @@ def tile_moe_adp_gelu_kernel(
                 out=grouped.bitcast(F32).rearrange("p (x j u) -> p x j u", x=m, u=2),
                 in_=turned.rearrange("p x u j -> p x j u"),
             )
-            i = QUANT_CUTS.index((e0, e1))
-            nc.vector.quantize_mx(
-                out=hcodes[i][:].rearrange("p x j -> p (x j)").bitcast(FP8X4),
-                scales=hscales[i][:].rearrange("p x j -> p (x j)"),
-                in_=grouped,
-            )
 
-        def pair_to_codes(g):
-            first_layer(2 * g)
-            first_layer(2 * g + 1)
-            turn_and_quantise(2 * g, 2 * g + 2, turn[g % 2])
+        def quantise(g):
+            nc.vector.quantize_mx(out=hcodes[g][:].bitcast(FP8X4), scales=hscales[g][:], in_=h_cols[g][:])
 
         def second_layer(half, g, acc):
             for x in range(2):
                 e = 2 * g + x
+                slots = slice(x * C, (x + 1) * C)
                 nc.tensor.matmul_mx(
-                    out=acc[:, x * C : (x + 1) * C],
+                    out=acc[:, slots],
                     lhsT=pick(wb, WB_CUTS, e)[:, half * FP4_BYTES * P : (half + 1) * FP4_BYTES * P].bitcast(FP4X4),
                     lhsT_scale=wbs[:, e, half * P : (half + 1) * P],
-                    rhs=pick(hcodes, QUANT_CUTS, e).bitcast(FP8X4),
-                    rhs_scale=pick(hscales, QUANT_CUTS, e),
+                    rhs=hcodes[g][:, slots].bitcast(FP8X4),
+                    rhs_scale=hscales[g][:, slots],
                     start=True,
                     stop=True,
                 )
 
-        def scatter(half, first_pair, end_pair, values, weights):
+        def first_layers(g):
+            first_product(2 * g)
+            first_product(2 * g + 1)
+            gelu(2 * g)
+
+        def to_codes(g):
+            turn_h(2 * g, 2 * g + 2, turn[(g + 1) % 2])
+            quantise(g)
+
+        def second_layers(g):
+            second_layer(UPPER, g, upper_acc[g])
+            second_layer(LOWER, g, lower_acc[g])
+
+        def scatter(half, first_pair, end_pair, values):
+            i = [j for j, (a, b) in enumerate(GATE_CUTS) if a <= first_pair < b][0]
+            at = GATE_CUTS[i][0]
+            weights = gates[i][:, (first_pair - at) * PS : (end_pair - at) * PS]
             nc.vector.tensor_tensor(
                 out=window[half][:].indirect(entries(first_pair, end_pair)), in0=values, in1=weights, op=MULT
             )
 
         def upper(g):
             nc.scalar.copy(out=y_upper[g][:], in_=upper_acc[g])
-            scatter(UPPER, g, g + 1, y_upper[g][:], pick(gates, GATE_CUTS, g))
+            scatter(UPPER, g, g + 1, y_upper[g][:])
 
         def lower(g):
             nc.scalar.copy(out=y_lower[g][:], in_=lower_acc[g])
-            scatter(LOWER, g, g + 1, y_lower[g][:], pick(gates, GATE_CUTS, g))
+            scatter(LOWER, g, g + 1, y_lower[g][:])
 
         def frozen(half, i):
             a, b = TOKEN_CHUNKS[i]
-            acc = wide[(E + i) % 3][:, 0 : b - a]
+            acc = frozen_acc[i][:, 0 : b - a]
             nc.tensor.matmul_mx(
                 out=acc,
                 lhsT=ww[:, half * FP4_BYTES * P : (half + 1) * FP4_BYTES * P].bitcast(FP4X4),
@@ -274,39 +330,49 @@ def tile_moe_adp_gelu_kernel(
                 )
 
         gather_words(0)
+        gather_bytes(0)
+        gather_bytes(1)
+        first_layers(0)
+        gelu(1)
         gather_words(1)
-        for g in range(PAIRS - 1):
-            gather_bytes(g)
-        first_layer(0)
-        first_layer(1)
+        gather_bytes(2)
+        late_loads()
+        turn_h(0, 1, turn_first[0])
+        turn_h(1, 2, turn_first[1])
+        quantise(0)
         gather_words(2)
-        gather_words(3)
-        turn_and_quantise(0, 1, turn[0])
-        turn_and_quantise(1, 2, turn[1])
-        gather_words(PAIRS - 1)
-        gather_bytes(PAIRS - 1)
-        for g in range(FILL_PAIRS):
-            second_layer(UPPER, g, upper_acc[g])
-            second_layer(LOWER, g, lower_acc[g])
-            upper(g)
-            pair_to_codes(g + 1)
-            lower(g)
-        pair_to_codes(4)
+        second_layer(UPPER, 0, upper_acc[0])
+        upper(0)
+        first_layers(1)
+        gelu(3)
+        second_layer(LOWER, 0, lower_acc[0])
+        to_codes(1)
+        lower(0)
+        first_layers(2)
+        gelu(5)
+        second_layers(1)
+        upper(1)
+        first_layers(3)
+        to_codes(2)
+        lower(1)
+        gelu(7)
+        first_product(8)
+        gelu(8)
+        first_product(9)
+        to_codes(3)
+        second_layers(2)
+        upper(2)
+        gelu(9)
+        to_codes(4)
         second_layer(UPPER, 3, upper_acc[3])
         upper(3)
         second_layer(UPPER, 4, upper_acc[4])
-        second_layer(LOWER, 4, lower_acc[4])
         upper(4)
         second_layer(LOWER, 3, lower_acc[3])
-        for g in range(FILL_PAIRS, PAIRS):
-            nc.scalar.copy(out=y_rest[:, g - FILL_PAIRS, :], in_=lower_acc[g])
-        scatter(
-            LOWER,
-            FILL_PAIRS,
-            PAIRS,
-            y_rest[:].rearrange("p g j -> p (g j)"),
-            gates[1][:, FILL_PAIRS - GATE_CUTS[1][0] :, :].rearrange("p g j -> p (g j)"),
-        )
+        second_layer(LOWER, 4, lower_acc[4])
+        nc.scalar.copy(out=y_rest[:, 0:PS], in_=lower_acc[2])
+        nc.scalar.copy(out=y_rest[:, PS:], in_=turn[1][:])
+        scatter(LOWER, 2, 5, y_rest[:])
 
         for i, (a, b) in enumerate(TOKEN_CHUNKS):
             nc.scalar.copy(out=base_upper[:, a:b], in_=frozen(UPPER, i))

@@ -31,7 +31,7 @@ WA_SCALE_CUTS = [(0, 4), (4, 10)]
 WB_CUTS = [(0, 4), (4, 10)]
 GATE_CUTS = [(0, 2), (2, 5)]
 WORD_CUTS = [(0, 1), (1, 3), (3, 5)]
-BYTE_CUTS = [(0, 1), (1, 3), (3, 5)]
+BYTE_CUTS = [(0, 1), (1, 4), (4, 5)]
 TOKEN_CHUNKS = [(0, 512), (512, 1024), (1024, 1280)]
 WINDOW = 2048
 REGION = 2048
@@ -90,7 +90,7 @@ def tile_moe_adp_gelu_kernel(
 
         late_specs = [
             ("xwg2", [P, 2, PS], U32, 8 * PS),
-            ("xsg3", [P, 2, PS], U8, 2 * PS),
+            ("xsg3", [P, 1, PS], U8, PS),
             ("wb4", [P, 6, wb_bytes], U8, 6 * wb_bytes),
             ("gates2", [P, 3 * PS], F32, 12 * PS),
             ("ww", [P, wb_bytes], U8, wb_bytes),
@@ -107,7 +107,7 @@ def tile_moe_adp_gelu_kernel(
         gates = [gates0, gates2]
         xsg = [
             first_bytes[:, 0:PS].rearrange("p (g j) -> p g j", g=1),
-            own("xsg1", [P, 2, PS], U8)[:],
+            own("xsg1", [P, 3, PS], U8)[:],
             xsg3[:],
         ]
 
@@ -143,6 +143,8 @@ def tile_moe_adp_gelu_kernel(
             placed(shared, "xwg3", [P, 2, PS], U32, cols_at)[:],
         ]
         hcodes = [own("hcodes%d" % g, [P, PS], U32) for g in range(PAIRS)]
+        base_last = own("base_last", [P, PS], F32)
+        result_last = own("result_last", [P, PS], F32)
         y_rest = own("y_rest", [P, 3 * PS], F32)
         base_at = 3 * REGION + HALF_REGION
         base_upper = placed(shared, "base_upper", [P, T], F32, base_at)
@@ -385,7 +387,14 @@ def tile_moe_adp_gelu_kernel(
             nc.scalar.copy(out=result[UPPER][:, a:b], in_=summing[i][:, 0 : b - a])
             nc.scalar.dma_start(out=out[0:P, a:b], in_=result[UPPER][:, a:b])
 
-        for i, (a, b) in enumerate(TOKEN_CHUNKS):
+        def store_lower(c):
+            nc.sync.dma_start(out=out[P : 2 * P, c : c + PS], in_=result[LOWER][:, c : c + PS])
+
+        a, b = TOKEN_CHUNKS[-1]
+        nc.scalar.copy(out=base_last[:], in_=frozen(LOWER, len(TOKEN_CHUNKS) - 1))
+        nc.gpsimd.tensor_tensor(out=result_last[:], in0=base_last[:], in1=window[LOWER][:, a:b], op=ADD)
+        nc.scalar.dma_start(out=out[P : 2 * P, a:b], in_=result_last[:])
+        for i, (a, b) in enumerate(TOKEN_CHUNKS[:-1]):
             acc = frozen(LOWER, i)
             for c in range(a, b, PS):
                 nc.vector.tensor_tensor(
@@ -394,4 +403,4 @@ def tile_moe_adp_gelu_kernel(
                     in1=window[LOWER][:, c : c + PS],
                     op=ADD,
                 )
-                nc.sync.dma_start(out=out[P : 2 * P, c : c + PS], in_=result[LOWER][:, c : c + PS])
+                store_lower(c)

@@ -33,6 +33,7 @@ GATE_CUTS = [(0, 2), (2, 5)]
 WORD_CUTS = [(0, 1), (1, 3), (3, 5)]
 BYTE_CUTS = [(0, 1), (1, 4), (4, 5)]
 TOKEN_CHUNKS = [(0, 512), (512, 1024), (1024, 1280)]
+SIDE = 384
 WINDOW = 2048
 REGION = 2048
 HALF_REGION = REGION // 2
@@ -61,10 +62,15 @@ def tile_moe_adp_gelu_kernel(
 
         offsets = keep.tile([P, T // PER_COLUMN], U16, name="offsets")
         xw = own("xw", [P, T], I32)
-        xs = own("xs", [P, T], U8)
-        was = [own("was%d" % a, [P, b - a, H], U8) for a, b in WA_SCALE_CUTS]
-        wbs = own("wbs", [P, E, N], U8)
-        ident = own("ident", [P, P], F32)
+        xs = own("xs", [P, T + 4], U8)
+        was_tiles = [own("was%d" % a, [P, (b - a) * H + 4], U8) for a, b in WA_SCALE_CUTS]
+        wbs_tile = own("wbs", [P, E * N + 4], U8)
+        was = [
+            t[:, 0 : (b - a) * H].rearrange("p (e i) -> p e i", i=H) for t, (a, b) in zip(was_tiles, WA_SCALE_CUTS)
+        ]
+        wbs = wbs_tile[:, 0 : E * N].rearrange("p (e n) -> p e n", n=N)
+        ident_tile = own("ident", [P, P + 1], F32)
+        ident = ident_tile[:, 0:P]
         hscales = [own("hscales%d" % g, [P, PS], U8) for g in range(PAIRS)]
         window = [own("window%d" % half, [P, WINDOW], F32) for half in (UPPER, LOWER)]
         result = [own("result%d" % half, [P, T], F32) for half in (UPPER, LOWER)]
@@ -143,8 +149,8 @@ def tile_moe_adp_gelu_kernel(
             placed(shared, "xwg3", [P, 2, PS], U32, cols_at)[:],
         ]
         hcodes = [own("hcodes%d" % g, [P, PS], U32) for g in range(PAIRS)]
-        base_last = own("base_last", [P, PS], F32)
-        result_last = own("result_last", [P, PS], F32)
+        base_last = own("base_last", [P, SIDE], F32)
+        result_last = own("result_last", [P, SIDE], F32)
         y_rest = own("y_rest", [P, 3 * PS], F32)
         base_at = 3 * REGION + HALF_REGION
         base_upper = placed(shared, "base_upper", [P, T], F32, base_at)
@@ -163,7 +169,7 @@ def tile_moe_adp_gelu_kernel(
         def load_plane(queue, plane, rows):
             src = rows.bitcast(I32).rearrange("(q r) n -> r q n", r=4)
             for r in range(4):
-                queue.dma_start(out=plane[r:P:32, :].bitcast(I32), in_=src[r])
+                queue.dma_start(out=plane[r:P:32, 0 : rows.shape[1]].bitcast(I32), in_=src[r])
 
         def load_planes(queues, planes, rows, cut):
             src = rows.bitcast(I32)[cut[0] : cut[1], 0].rearrange("e (q r) n -> r q e n", r=4)
@@ -180,10 +186,10 @@ def tile_moe_adp_gelu_kernel(
             nc.sync.dma_start(out=gates[i][:], in_=gate[:, a * PS : b * PS])
 
         nc.vector.memset(xs[:].bitcast(I32), 0)
-        nc.vector.memset(warm[:, 0:8], 0.0)
-        nc.vector.memset(was[0][:].bitcast(I32), 0)
-        nc.vector.memset(ident[:], 0.0)
-        nc.vector.memset(wbs[:].bitcast(I32), 0)
+        nc.vector.memset(warm[:, 0:7], 0.0)
+        nc.vector.memset(was_tiles[0][:].bitcast(I32), 0)
+        nc.vector.memset(ident_tile[:], 0.0)
+        nc.vector.memset(wbs_tile[:].bitcast(I32), 0)
 
         nc.sync.dma_start(offsets[:], offs)
         nc.sync.dma_start(out=xw[:], in_=x_words[0].rearrange("p t d -> p (t d)").bitcast(I32))
@@ -191,13 +197,13 @@ def tile_moe_adp_gelu_kernel(
         load_plane(nc.sync, xs, x_scales[0])
         load_planes([nc.sync, nc.sync, nc.sync, nc.gpsimd], was[0], wa_scales, WA_SCALE_CUTS[0])
         make_identity(nc, ident[:], nomemset=True)
-        nc.scalar.activation(out=warm[:, 8:16], in_=warm[:, 0:8], func=GELU)
+        nc.scalar.activation(out=warm[:, 8:15], in_=warm[:, 0:7], func=GELU)
         load_planes([nc.sync] * 4, wbs, wb_scales, (0, E))
         load_words(nc.sync, wa[1], wa_words, WA_CUTS[1])
         load_words(nc.sync, wb[0], wb_words, WB_CUTS[0])
         load_gates(0)
         load_words(nc.sync, wa[2], wa_words, WA_CUTS[2])
-        nc.vector.memset(was[1][:].bitcast(I32), 0)
+        nc.vector.memset(was_tiles[1][:].bitcast(I32), 0)
         load_planes([nc.sync] * 4, was[1], wa_scales, WA_SCALE_CUTS[1])
 
         def late_loads():
@@ -379,6 +385,10 @@ def tile_moe_adp_gelu_kernel(
         for i, (a, b) in enumerate(TOKEN_CHUNKS):
             nc.scalar.copy(out=base_upper[:, a:b], in_=frozen(UPPER, i))
             turn_into_sum(i, base_upper, True, False)
+        accs = [frozen(LOWER, i) for i in range(len(TOKEN_CHUNKS))]
+        split = T - SIDE
+        nc.scalar.copy(out=base_last[:, 0 : 2 * BANK - split], in_=accs[1][:, split - BANK :])
+        nc.scalar.copy(out=base_last[:, 2 * BANK - split :], in_=accs[2])
         for i, (a, b) in enumerate(TOKEN_CHUNKS):
             turn_into_sum(i, window[UPPER], False, True)
             nc.scalar.copy(out=sum_turned[:, a:b], in_=summing[i][:, 0 : b - a])
@@ -387,20 +397,13 @@ def tile_moe_adp_gelu_kernel(
             nc.scalar.copy(out=result[UPPER][:, a:b], in_=summing[i][:, 0 : b - a])
             nc.scalar.dma_start(out=out[0:P, a:b], in_=result[UPPER][:, a:b])
 
-        def store_lower(c):
-            nc.sync.dma_start(out=out[P : 2 * P, c : c + PS], in_=result[LOWER][:, c : c + PS])
-
-        a, b = TOKEN_CHUNKS[-1]
-        nc.scalar.copy(out=base_last[:], in_=frozen(LOWER, len(TOKEN_CHUNKS) - 1))
-        nc.gpsimd.tensor_tensor(out=result_last[:], in0=base_last[:], in1=window[LOWER][:, a:b], op=ADD)
-        nc.scalar.dma_start(out=out[P : 2 * P, a:b], in_=result_last[:])
-        for i, (a, b) in enumerate(TOKEN_CHUNKS[:-1]):
-            acc = frozen(LOWER, i)
-            for c in range(a, b, PS):
-                nc.vector.tensor_tensor(
-                    out=result[LOWER][:, c : c + PS],
-                    in0=acc[:, c - a : c - a + PS],
-                    in1=window[LOWER][:, c : c + PS],
-                    op=ADD,
-                )
-                store_lower(c)
+        nc.gpsimd.tensor_tensor(out=result_last[:], in0=base_last[:], in1=window[LOWER][:, split:T], op=ADD)
+        for a, b in [(0, PS), (PS, BANK), (BANK, split)]:
+            nc.vector.tensor_tensor(
+                out=result[LOWER][:, a:b],
+                in0=accs[a // BANK][:, a % BANK : a % BANK + b - a],
+                in1=window[LOWER][:, a:b],
+                op=ADD,
+            )
+            nc.sync.dma_start(out=out[P : 2 * P, a:b], in_=result[LOWER][:, a:b])
+        nc.sync.dma_start(out=out[P : 2 * P, split:T], in_=result_last[:])

@@ -1,7 +1,6 @@
 from contextlib import ExitStack
 
 import concourse.mybir as mybir
-from concourse.masks import make_identity
 
 K, T, E, C, H, N = 512, 1280, 10, 128, 512, 256
 FLOPS = 2 * K * N * T + 2 * K * H * E * C + 2 * H * N * E * C
@@ -27,7 +26,7 @@ UPPER, LOWER = 0, 1
 FP4_BYTES = 2
 
 WA_CUTS = [(0, 2), (2, 4), (4, 6), (6, 8), (8, 10)]
-WA_SCALE_CUTS = [(0, 4), (4, 10)]
+WA_SCALE_CUTS = [(0, 2), (2, 10)]
 WB_CUTS = [(0, 4), (4, 10)]
 GATE_CUTS = [(0, 2), (2, 5)]
 WORD_CUTS = [(0, 1), (1, 3), (3, 5)]
@@ -62,15 +61,10 @@ def tile_moe_adp_gelu_kernel(
 
         offsets = keep.tile([P, T // PER_COLUMN], U16, name="offsets")
         xw = own("xw", [P, T], I32)
-        xs = own("xs", [P, T + 4], U8)
-        was_tiles = [own("was%d" % a, [P, (b - a) * H + 4], U8) for a, b in WA_SCALE_CUTS]
-        wbs_tile = own("wbs", [P, E * N + 4], U8)
-        was = [
-            t[:, 0 : (b - a) * H].rearrange("p (e i) -> p e i", i=H) for t, (a, b) in zip(was_tiles, WA_SCALE_CUTS)
-        ]
-        wbs = wbs_tile[:, 0 : E * N].rearrange("p (e n) -> p e n", n=N)
-        ident_tile = own("ident", [P, P + 1], F32)
-        ident = ident_tile[:, 0:P]
+        xs = own("xs", [P, T], U8)
+        was = [own("was%d" % a, [P, b - a, H], U8) for a, b in WA_SCALE_CUTS]
+        wbs = own("wbs", [P, E, N], U8)
+        ident = own("ident", [P, P], F32)
         hscales = [own("hscales%d" % g, [P, PS], U8) for g in range(PAIRS)]
         window = [own("window%d" % half, [P, WINDOW], F32) for half in (UPPER, LOWER)]
         result = [own("result%d" % half, [P, T], F32) for half in (UPPER, LOWER)]
@@ -91,7 +85,7 @@ def tile_moe_adp_gelu_kernel(
             ("gates0", [P, 2 * PS], F32, 8 * PS),
             ("wa4", [P, 2, wa_bytes], U8, 2 * wa_bytes),
         ]
-        warm = placed(soon, "warm", [P, sum([s[3] for s in soon_specs]) // 4], F32, 0)
+        zeros = placed(soon, "zeros", [P, sum([s[3] for s in soon_specs]) // 4], F32, 0)
         (wa2, wb0, gates0, wa4), soon_end = laid_out(soon, soon_specs)
 
         late_specs = [
@@ -185,26 +179,32 @@ def tile_moe_adp_gelu_kernel(
             a, b = GATE_CUTS[i]
             nc.sync.dma_start(out=gates[i][:], in_=gate[:, a * PS : b * PS])
 
+        nc.gpsimd.memset(was[0][:].bitcast(I32), 0)
         nc.vector.memset(xs[:].bitcast(I32), 0)
-        nc.vector.memset(warm[:, 0:7], 0.0)
-        nc.vector.memset(was_tiles[0][:].bitcast(I32), 0)
-        nc.vector.memset(ident_tile[:], 0.0)
-        nc.vector.memset(wbs_tile[:].bitcast(I32), 0)
+        nc.vector.memset(was[1][:].bitcast(I32), 0)
+        nc.vector.memset(wbs[:].bitcast(I32), 0)
+        nc.vector.memset(zeros[:, 0:P], 0.0)
 
         nc.sync.dma_start(offsets[:], offs)
         nc.sync.dma_start(out=xw[:], in_=x_words[0].rearrange("p t d -> p (t d)").bitcast(I32))
-        load_words(nc.gpsimd, wa[0], wa_words, WA_CUTS[0])
         load_plane(nc.sync, xs, x_scales[0])
         load_planes([nc.sync, nc.sync, nc.sync, nc.gpsimd], was[0], wa_scales, WA_SCALE_CUTS[0])
-        make_identity(nc, ident[:], nomemset=True)
-        nc.scalar.activation(out=warm[:, 8:15], in_=warm[:, 0:7], func=GELU)
+        load_words(nc.gpsimd, wa[0], wa_words, WA_CUTS[0])
+        load_planes([nc.sync] * 4, was[1], wa_scales, WA_SCALE_CUTS[1])
         load_planes([nc.sync] * 4, wbs, wb_scales, (0, E))
+        nc.gpsimd.affine_select(
+            out=ident[:],
+            in_=zeros[:, 0:P],
+            compare_op=mybir.AluOpType.not_equal,
+            fill=1.0,
+            base=0,
+            pattern=[[-1, P]],
+            channel_multiplier=1,
+        )
         load_words(nc.sync, wa[1], wa_words, WA_CUTS[1])
         load_words(nc.sync, wb[0], wb_words, WB_CUTS[0])
         load_gates(0)
         load_words(nc.sync, wa[2], wa_words, WA_CUTS[2])
-        nc.vector.memset(was_tiles[1][:].bitcast(I32), 0)
-        load_planes([nc.sync] * 4, was[1], wa_scales, WA_SCALE_CUTS[1])
 
         def late_loads():
             load_words(nc.sync, wa[3], wa_words, WA_CUTS[3])

@@ -25,16 +25,19 @@ PER_COLUMN = 16
 UPPER, LOWER = 0, 1
 FP4_BYTES = 2
 
-WA_CUTS = [(0, 2), (2, 4), (4, 6), (6, 8), (8, 10)]
-WA_SCALE_CUTS = [(0, 2), (2, 10)]
-WB_CUTS = [(0, 4), (4, 10)]
-GATE_CUTS = [(0, 2), (2, 5)]
-WORD_CUTS = [(0, 1), (1, 3), (3, 5)]
-BYTE_CUTS = [(0, 1), (1, 4), (4, 5)]
-TOKEN_CHUNKS = [(0, 512), (512, 1024), (1024, 1280)]
-SIDE = 384
+WA_BYTES = FP4_BYTES * H
+WB_BYTES = FP4_BYTES * N
+
+WA_CUTS = [(2 * g, 2 * g + 2) for g in range(PAIRS)]
+WA_SCALE_CUTS = [(0, 4), (4, E)]
+WB_CUTS = [(0, 4), (4, E)]
+GATE_CUTS = [(0, 2), (2, PAIRS)]
+WORD_CUTS = [(0, 1), (1, 3), (3, PAIRS)]
+BYTE_CUTS = [(0, 1), (1, 4), (4, PAIRS)]
+TOKEN_CHUNKS = [(0, BANK), (BANK, 2 * BANK), (2 * BANK, T)]
+FILLERS = 2
 WINDOW = 2048
-REGION = 2048
+REGION = 4 * H
 HALF_REGION = REGION // 2
 
 
@@ -55,6 +58,13 @@ def tile_moe_adp_gelu_kernel(
         def placed(pool, name, shape, dtype, at):
             return pool.tile(shape, dtype, name=name, align_bytes=64, offset=at)
 
+        def laid_out(pool, specs):
+            tiles, at = [], 0
+            for name, shape, dtype, size in specs:
+                tiles.append(placed(pool, name, shape, dtype, at))
+                at = at + size
+            return tiles
+
         def pick(tiles, cuts, index):
             i = [j for j, (a, b) in enumerate(cuts) if a <= index < b][0]
             return tiles[i][:, index - cuts[i][0], :]
@@ -62,108 +72,104 @@ def tile_moe_adp_gelu_kernel(
         offsets = keep.tile([P, T // PER_COLUMN], U16, name="offsets")
         xw = own("xw", [P, T], I32)
         xs = own("xs", [P, T], U8)
-        was = [own("was%d" % a, [P, b - a, H], U8) for a, b in WA_SCALE_CUTS]
         wbs = own("wbs", [P, E, N], U8)
         ident = own("ident", [P, P], F32)
         hscales = [own("hscales%d" % g, [P, PS], U8) for g in range(PAIRS)]
         window = [own("window%d" % half, [P, WINDOW], F32) for half in (UPPER, LOWER)]
         result = [own("result%d" % half, [P, T], F32) for half in (UPPER, LOWER)]
 
-        wa_bytes = FP4_BYTES * H
-        wb_bytes = FP4_BYTES * N
-
-        def laid_out(pool, specs):
-            tiles, at = [], 0
-            for name, shape, dtype, size in specs:
-                tiles.append(placed(pool, name, shape, dtype, at))
-                at = at + size
-            return tiles, at
-
         soon_specs = [
-            ("wa2", [P, 2, wa_bytes], U8, 2 * wa_bytes),
-            ("wb0", [P, 4, wb_bytes], U8, 4 * wb_bytes),
-            ("gates0", [P, 2 * PS], F32, 8 * PS),
-            ("wa4", [P, 2, wa_bytes], U8, 2 * wa_bytes),
+            ("wa2", [P, 2, WA_BYTES], U8, 2 * WA_BYTES),
+            ("wb0", [P, 4, WB_BYTES], U8, 4 * WB_BYTES),
+            ("gates0", [P, 2 * PS], F32, 4 * 2 * PS),
+            ("wa4", [P, 2, WA_BYTES], U8, 2 * WA_BYTES),
+            ("was4", [P, 6, H], U8, 6 * H),
         ]
         zeros = placed(soon, "zeros", [P, sum([s[3] for s in soon_specs]) // 4], F32, 0)
-        (wa2, wb0, gates0, wa4), soon_end = laid_out(soon, soon_specs)
+        wa2, wb0, gates0, wa4, was4 = laid_out(soon, soon_specs)
+        was = [own("was0", [P, 4, H], U8), was4]
 
         late_specs = [
-            ("xwg2", [P, 2, PS], U32, 8 * PS),
-            ("xsg3", [P, 1, PS], U8, PS),
-            ("wb4", [P, 6, wb_bytes], U8, 6 * wb_bytes),
-            ("gates2", [P, 3 * PS], F32, 12 * PS),
-            ("ww", [P, wb_bytes], U8, wb_bytes),
+            ("xwg1", [P, 2, PS], U32, 4 * 2 * PS),
+            ("xsg4", [P, 1, PS], U8, PS),
+            ("wb4", [P, 6, WB_BYTES], U8, 6 * WB_BYTES),
+            ("gates2", [P, 3 * PS], F32, 4 * 3 * PS),
+            ("ww", [P, WB_BYTES], U8, WB_BYTES),
             ("ws", [P, N], U8, N),
-            ("wa6", [P, 3, wa_bytes], U8, 3 * wa_bytes),
-            ("h_rows2", [P, 2, H], BF16, 4 * H),
-            ("wa8", [P, 3, wa_bytes], U8, 3 * wa_bytes),
+            ("wa6", [P, 3, WA_BYTES], U8, 3 * WA_BYTES),
+            ("h_rows2", [P, 2, H], BF16, REGION),
+            ("wa8", [P, 3, WA_BYTES], U8, 3 * WA_BYTES),
         ]
-        first_bytes = placed(late, "first_bytes", [P, sum([s[3] for s in late_specs])], U8, 0)
-        (xwg2, xsg3, wb4, gates2, ww, ws, wa6, h_rows2, wa8), late_end = laid_out(late, late_specs)
-        rows2_at = late_end - 3 * wa_bytes - 4 * H
-        wa = [own("wa0", [P, 2, wa_bytes], U8), wa2, wa4, wa6, wa8]
+        rows3_at = sum([s[3] for s in late_specs])
+        wa8_at = rows3_at - 3 * WA_BYTES
+        rows2_at = wa8_at - REGION
+        wa6_at = rows2_at - 3 * WA_BYTES
+        first_bytes = placed(late, "first_bytes", [P, rows3_at], U8, 0)
+        xwg1, xsg4, wb4, gates2, ww, ws, wa6, h_rows2, wa8 = laid_out(late, late_specs)
+        wa = [own("wa0", [P, 2, WA_BYTES], U8), wa2, wa4, wa6, wa8]
         wb = [wb0, wb4]
         gates = [gates0, gates2]
         xsg = [
             first_bytes[:, 0:PS].rearrange("p (g j) -> p g j", g=1),
             own("xsg1", [P, 3, PS], U8)[:],
-            xsg3[:],
+            xsg4[:],
         ]
 
-        h_rows = [own("h_rows0", [P, 2, H], BF16)]
-        h_rows += [
+        rows4_at = 3 * REGION
+        cols0_at = rows4_at + REGION
+        h_rows = [
+            own("h_rows0", [P, 2, H], BF16),
             placed(shared, "h_rows1", [P, 2, H], BF16, 0),
             h_rows2,
-            placed(late, "h_rows3", [P, 2, H], BF16, late_end),
-            placed(shared, "h_rows4", [P, 2, H], BF16, 3 * REGION),
+            placed(late, "h_rows3", [P, 2, H], BF16, rows3_at),
+            placed(shared, "h_rows4", [P, 2, H], BF16, rows4_at),
         ]
-        y_upper = [own("y_upper0", [P, PS], F32)]
-        y_upper += [
+        straddle = HALF_REGION // 2
+        y_upper = [
+            own("y_upper0", [P, PS], F32),
             own("y_upper1", [P, PS], F32),
-            placed(late, "y_upper2", [P, PS], F32, late_end - 2 * PS),
-            placed(shared, "y_upper3", [P, PS], F32, 3 * REGION),
+            placed(late, "y_upper2", [P, PS], F32, rows3_at - straddle),
+            placed(shared, "y_upper3", [P, PS], F32, rows4_at),
+            own("y_upper4", [P, PS], F32),
         ]
-        y_upper += [own("y_upper4", [P, PS], F32)]
         y_lower = [
             placed(shared, "y_lower0", [P, PS], F32, 0),
-            placed(late, "y_lower1", [P, PS], F32, rows2_at - 2 * PS),
+            placed(late, "y_lower1", [P, PS], F32, rows2_at - straddle),
         ]
-        cols_at = 4 * REGION
-        h_cols = [placed(shared, "h_cols0", [P, 4 * PS], BF16, cols_at)]
-        h_cols += [
+        h_cols = [
+            placed(shared, "h_cols0", [P, 4 * PS], BF16, cols0_at),
             own("h_cols1", [P, 4 * PS], BF16),
-            placed(late, "h_cols2", [P, 4 * PS], BF16, rows2_at - 3 * wa_bytes),
-            placed(late, "h_cols3", [P, 4 * PS], BF16, late_end - 3 * wa_bytes),
+            placed(late, "h_cols2", [P, 4 * PS], BF16, wa6_at),
+            placed(late, "h_cols3", [P, 4 * PS], BF16, wa8_at),
             own("h_cols4", [P, 4 * PS], BF16),
         ]
-        xwg = [
-            own("xwg0", [P, 1, PS], U32)[:],
-            xwg2[:],
-            placed(shared, "xwg3", [P, 2, PS], U32, cols_at)[:],
-        ]
+        xwg = [own("xwg0", [P, 1, PS], U32)[:], xwg1[:], placed(shared, "xwg3", [P, 2, PS], U32, cols0_at)[:]]
         hcodes = [own("hcodes%d" % g, [P, PS], U32) for g in range(PAIRS)]
-        base_last = own("base_last", [P, SIDE], F32)
-        result_last = own("result_last", [P, SIDE], F32)
-        y_rest = own("y_rest", [P, 3 * PS], F32)
-        base_at = 3 * REGION + HALF_REGION
+        side_first, side_end = TOKEN_CHUNKS[-1]
+        base_side = own("base_side", [P, side_end - side_first], F32)
+        result_side = own("result_side", [P, side_end - side_first], F32)
+        y_rest = own("y_rest", [P, (PAIRS - FILLERS) * PS], F32)
+        base_at = rows4_at + HALF_REGION
         base_upper = placed(shared, "base_upper", [P, T], F32, base_at)
         sum_turned = placed(shared, "sum_turned", [P, T], F32, base_at)
 
         bank = [psum.tile([P, BANK], F32, name="bank%d" % b) for b in range(8)]
-        first_acc = [bank[b] for b in (0, 1, 1, 2, 0, 5, 1, 2, 0, 5)]
+        first_acc = [bank[0], bank[1]]
+        for g in range(1, PAIRS):
+            first_acc += [bank[g % 2], [bank[5], bank[2]][g % 2]]
         turn_first = [bank[2], bank[0]]
         turn = bank[3:5]
         second = [bank[6]] + [first_acc[2 * g + 3] for g in range(1, PAIRS - 1)]
-        upper_acc = [second[g][:, 0:PS] for g in range(PAIRS - 1)] + [second[3][:, PS:]]
-        lower_acc = [second[g][:, PS:] for g in range(PAIRS - 2)] + [turn[1][:, 0:PS], turn[1][:, PS:]]
+        last_lower = turn[1]
+        upper_acc = [second[g][:, 0:PS] for g in range(PAIRS - 1)] + [second[PAIRS - 2][:, PS:]]
+        lower_acc = [second[g][:, PS:] for g in range(PAIRS - 2)] + [last_lower[:, 0:PS], last_lower[:, PS:]]
         frozen_acc = bank[0:3]
         summing = [bank[6], bank[7], bank[3]]
 
-        def load_plane(queue, plane, rows):
+        def load_plane(plane, rows):
             src = rows.bitcast(I32).rearrange("(q r) n -> r q n", r=4)
             for r in range(4):
-                queue.dma_start(out=plane[r:P:32, 0 : rows.shape[1]].bitcast(I32), in_=src[r])
+                nc.sync.dma_start(out=plane[r:P:32, :].bitcast(I32), in_=src[r])
 
         def load_planes(queues, planes, rows, cut):
             src = rows.bitcast(I32)[cut[0] : cut[1], 0].rearrange("e (q r) n -> r q e n", r=4)
@@ -172,25 +178,24 @@ def tile_moe_adp_gelu_kernel(
 
         def load_words(queue, words, src, cut):
             queue.dma_start(
-                out=words[:, 0 : cut[1] - cut[0], :].bitcast(I32), in_=src.bitcast(I32)[cut[0] : cut[1], 0].rearrange("e p n -> p e n")
+                out=words[:, 0 : cut[1] - cut[0], :].bitcast(I32),
+                in_=src.bitcast(I32)[cut[0] : cut[1], 0].rearrange("e p n -> p e n"),
             )
 
         def load_gates(i):
             a, b = GATE_CUTS[i]
             nc.sync.dma_start(out=gates[i][:], in_=gate[:, a * PS : b * PS])
 
-        nc.gpsimd.memset(was[0][:].bitcast(I32), 0)
         nc.vector.memset(xs[:].bitcast(I32), 0)
-        nc.vector.memset(was[1][:].bitcast(I32), 0)
-        nc.vector.memset(wbs[:].bitcast(I32), 0)
+        nc.vector.memset(was[0][:].bitcast(I32), 0)
         nc.vector.memset(zeros[:, 0:P], 0.0)
+        nc.vector.memset(wbs[:].bitcast(I32), 0)
 
         nc.sync.dma_start(offsets[:], offs)
         nc.sync.dma_start(out=xw[:], in_=x_words[0].rearrange("p t d -> p (t d)").bitcast(I32))
-        load_plane(nc.sync, xs, x_scales[0])
-        load_planes([nc.sync, nc.sync, nc.sync, nc.gpsimd], was[0], wa_scales, WA_SCALE_CUTS[0])
         load_words(nc.gpsimd, wa[0], wa_words, WA_CUTS[0])
-        load_planes([nc.sync] * 4, was[1], wa_scales, WA_SCALE_CUTS[1])
+        load_plane(xs, x_scales[0])
+        load_planes([nc.sync, nc.sync, nc.sync, nc.gpsimd], was[0], wa_scales, WA_SCALE_CUTS[0])
         load_planes([nc.sync] * 4, wbs, wb_scales, (0, E))
         nc.gpsimd.affine_select(
             out=ident[:],
@@ -205,6 +210,8 @@ def tile_moe_adp_gelu_kernel(
         load_words(nc.sync, wb[0], wb_words, WB_CUTS[0])
         load_gates(0)
         load_words(nc.sync, wa[2], wa_words, WA_CUTS[2])
+        nc.gpsimd.memset(was[1][:].bitcast(I32), 0)
+        load_planes([nc.sync] * 4, was[1], wa_scales, WA_SCALE_CUTS[1])
 
         def late_loads():
             load_words(nc.sync, wa[3], wa_words, WA_CUTS[3])
@@ -212,7 +219,7 @@ def tile_moe_adp_gelu_kernel(
             load_words(nc.sync, wa[4], wa_words, WA_CUTS[4])
             load_gates(1)
             nc.gpsimd.memset(ws[:].bitcast(I32), 0)
-            load_plane(nc.sync, ws, w_scales[0])
+            load_plane(ws, w_scales[0])
             nc.sync.dma_start(out=ww[:].bitcast(I32), in_=w_words[0].bitcast(I32))
 
         def entries(first_pair, end_pair):
@@ -231,9 +238,8 @@ def tile_moe_adp_gelu_kernel(
         def first_product(e):
             g, x = divmod(e, 2)
             slots = slice(x * C, (x + 1) * C)
-            acc = first_acc[e]
             nc.tensor.matmul_mx(
-                out=acc[:],
+                out=first_acc[e][:],
                 lhsT=pick(xwg, WORD_CUTS, g)[:, slots].bitcast(FP8X4),
                 lhsT_scale=pick(xsg, BYTE_CUTS, g)[:, slots],
                 rhs=pick(wa, WA_CUTS, e).bitcast(FP4X4),
@@ -244,10 +250,9 @@ def tile_moe_adp_gelu_kernel(
 
         def gelu(e):
             g, x = divmod(e, 2)
-            acc = first_acc[e]
             nc.scalar.activation(
                 out=h_rows[g][:, x, :].rearrange("j (u p d) -> j u p d", u=2, d=2),
-                in_=acc[:].rearrange("j (p u d) -> j u p d", u=2, d=2),
+                in_=first_acc[e][:].rearrange("j (p u d) -> j u p d", u=2, d=2),
                 func=GELU,
             )
 
@@ -282,7 +287,7 @@ def tile_moe_adp_gelu_kernel(
                     stop=True,
                 )
 
-        def first_layers(g):
+        def open_pair(g):
             first_product(2 * g)
             first_product(2 * g + 1)
             gelu(2 * g)
@@ -340,7 +345,7 @@ def tile_moe_adp_gelu_kernel(
         gather_words(0)
         gather_bytes(0)
         gather_bytes(1)
-        first_layers(0)
+        open_pair(0)
         gelu(1)
         gather_words(1)
         gather_bytes(2)
@@ -351,16 +356,16 @@ def tile_moe_adp_gelu_kernel(
         gather_words(2)
         second_layer(UPPER, 0, upper_acc[0])
         upper(0)
-        first_layers(1)
+        open_pair(1)
         gelu(3)
         second_layer(LOWER, 0, lower_acc[0])
         to_codes(1)
         lower(0)
-        first_layers(2)
+        open_pair(2)
         gelu(5)
         second_layers(1)
         upper(1)
-        first_layers(3)
+        open_pair(3)
         to_codes(2)
         lower(1)
         gelu(7)
@@ -378,17 +383,15 @@ def tile_moe_adp_gelu_kernel(
         upper(4)
         second_layer(LOWER, 3, lower_acc[3])
         second_layer(LOWER, 4, lower_acc[4])
-        nc.scalar.copy(out=y_rest[:, 0:PS], in_=lower_acc[2])
-        nc.scalar.copy(out=y_rest[:, PS:], in_=turn[1][:])
-        scatter(LOWER, 2, 5, y_rest[:])
+        nc.scalar.copy(out=y_rest[:, 0:PS], in_=lower_acc[FILLERS])
+        nc.scalar.copy(out=y_rest[:, PS:], in_=last_lower[:])
+        scatter(LOWER, FILLERS, PAIRS, y_rest[:])
 
         for i, (a, b) in enumerate(TOKEN_CHUNKS):
             nc.scalar.copy(out=base_upper[:, a:b], in_=frozen(UPPER, i))
             turn_into_sum(i, base_upper, True, False)
-        accs = [frozen(LOWER, i) for i in range(len(TOKEN_CHUNKS))]
-        split = T - SIDE
-        nc.scalar.copy(out=base_last[:, 0 : 2 * BANK - split], in_=accs[1][:, split - BANK :])
-        nc.scalar.copy(out=base_last[:, 2 * BANK - split :], in_=accs[2])
+        base_lower = [frozen(LOWER, i) for i in range(len(TOKEN_CHUNKS))]
+        nc.scalar.copy(out=base_side[:], in_=base_lower[-1])
         for i, (a, b) in enumerate(TOKEN_CHUNKS):
             turn_into_sum(i, window[UPPER], False, True)
             nc.scalar.copy(out=sum_turned[:, a:b], in_=summing[i][:, 0 : b - a])
@@ -397,13 +400,15 @@ def tile_moe_adp_gelu_kernel(
             nc.scalar.copy(out=result[UPPER][:, a:b], in_=summing[i][:, 0 : b - a])
             nc.scalar.dma_start(out=out[0:P, a:b], in_=result[UPPER][:, a:b])
 
-        nc.gpsimd.tensor_tensor(out=result_last[:], in0=base_last[:], in1=window[LOWER][:, split:T], op=ADD)
-        for a, b in [(0, PS), (PS, BANK), (BANK, split)]:
+        nc.gpsimd.tensor_tensor(
+            out=result_side[:], in0=base_side[:], in1=window[LOWER][:, side_first:side_end], op=ADD
+        )
+        for a in range(0, side_first, PS):
             nc.vector.tensor_tensor(
-                out=result[LOWER][:, a:b],
-                in0=accs[a // BANK][:, a % BANK : a % BANK + b - a],
-                in1=window[LOWER][:, a:b],
+                out=result[LOWER][:, a : a + PS],
+                in0=base_lower[a // BANK][:, a % BANK : a % BANK + PS],
+                in1=window[LOWER][:, a : a + PS],
                 op=ADD,
             )
-            nc.sync.dma_start(out=out[P : 2 * P, a:b], in_=result[LOWER][:, a:b])
-        nc.sync.dma_start(out=out[P : 2 * P, split:T], in_=result_last[:])
+            nc.sync.dma_start(out=out[P : 2 * P, a : a + PS], in_=result[LOWER][:, a : a + PS])
+        nc.sync.dma_start(out=out[P : 2 * P, side_first:side_end], in_=result_side[:])

@@ -32,8 +32,9 @@ WA_CUTS = [(2 * g, 2 * g + 2) for g in range(PAIRS)]
 WA_SCALE_CUTS = [(0, 4), (4, E)]
 WB_CUTS = [(0, 4), (4, E)]
 GATE_CUTS = [(0, 2), (2, PAIRS)]
-WORD_CUTS = [(0, 1), (1, 3), (3, PAIRS)]
-BYTE_CUTS = [(0, 1), (1, 4), (4, PAIRS)]
+WORD_CUTS = [(0, 1), (1, 2), (2, 8), (8, E)]
+FEWEST = T // 8
+BYTE_CUTS = [(0, 3), (3, PAIRS)]
 TOKEN_CHUNKS = [(0, BANK), (BANK, 2 * BANK), (2 * BANK, T)]
 FILLERS = 2
 WINDOW = 2048
@@ -70,28 +71,31 @@ def tile_moe_adp_gelu_kernel(
             return tiles[i][:, index - cuts[i][0], :]
 
         offsets = keep.tile([P, T // PER_COLUMN], U16, name="offsets")
-        xw = own("xw", [P, T], I32)
         xs = own("xs", [P, T], U8)
-        wbs = own("wbs", [P, E, N], U8)
         ident = own("ident", [P, P], F32)
         hscales = [own("hscales%d" % g, [P, PS], U8) for g in range(PAIRS)]
         window = [own("window%d" % half, [P, WINDOW], F32) for half in (UPPER, LOWER)]
         result = [own("result%d" % half, [P, T], F32) for half in (UPPER, LOWER)]
 
         soon_specs = [
+            ("xw", [P, T], I32, 4 * T),
             ("wa2", [P, 2, WA_BYTES], U8, 2 * WA_BYTES),
+            ("wa4", [P, 2, WA_BYTES], U8, 2 * WA_BYTES),
             ("wb0", [P, 4, WB_BYTES], U8, 4 * WB_BYTES),
             ("gates0", [P, 2 * PS], F32, 4 * 2 * PS),
-            ("wa4", [P, 2, WA_BYTES], U8, 2 * WA_BYTES),
+            ("was0", [P, 4, H], U8, 4 * H),
+            ("wbs0", [P, 4, N], U8, 4 * N),
+            ("wbs4", [P, 6, N], U8, 6 * N),
             ("was4", [P, 6, H], U8, 6 * H),
+            ("xsg0", [P, 3, PS], U8, 3 * PS),
         ]
         zeros = placed(soon, "zeros", [P, sum([s[3] for s in soon_specs]) // 4], F32, 0)
-        wa2, wb0, gates0, wa4, was4 = laid_out(soon, soon_specs)
-        was = [own("was0", [P, 4, H], U8), was4]
+        xw, wa2, wa4, wb0, gates0, was0, wbs0, wbs4, was4, xsg0 = laid_out(soon, soon_specs)
+        wbs = [wbs0, wbs4]
+        was = [was0, was4]
 
         late_specs = [
-            ("xwg1", [P, 2, PS], U32, 4 * 2 * PS),
-            ("xsg4", [P, 1, PS], U8, PS),
+            ("xsg3", [P, 2, PS], U8, 2 * PS),
             ("wb4", [P, 6, WB_BYTES], U8, 6 * WB_BYTES),
             ("gates2", [P, 3 * PS], F32, 4 * 3 * PS),
             ("ww", [P, WB_BYTES], U8, WB_BYTES),
@@ -104,16 +108,12 @@ def tile_moe_adp_gelu_kernel(
         wa8_at = rows3_at - 3 * WA_BYTES
         rows2_at = wa8_at - REGION
         wa6_at = rows2_at - 3 * WA_BYTES
-        first_bytes = placed(late, "first_bytes", [P, rows3_at], U8, 0)
-        xwg1, xsg4, wb4, gates2, ww, ws, wa6, h_rows2, wa8 = laid_out(late, late_specs)
+        first_words = placed(late, "first_words", [P, rows3_at // 4], U32, 0)
+        xsg3, wb4, gates2, ww, ws, wa6, h_rows2, wa8 = laid_out(late, late_specs)
         wa = [own("wa0", [P, 2, WA_BYTES], U8), wa2, wa4, wa6, wa8]
         wb = [wb0, wb4]
         gates = [gates0, gates2]
-        xsg = [
-            first_bytes[:, 0:PS].rearrange("p (g j) -> p g j", g=1),
-            own("xsg1", [P, 3, PS], U8)[:],
-            xsg4[:],
-        ]
+        xsg = [xsg0[:], xsg3[:]]
 
         rows4_at = 3 * REGION
         cols0_at = rows4_at + REGION
@@ -143,7 +143,12 @@ def tile_moe_adp_gelu_kernel(
             placed(late, "h_cols3", [P, 4 * PS], BF16, wa8_at),
             own("h_cols4", [P, 4 * PS], BF16),
         ]
-        xwg = [own("xwg0", [P, 1, PS], U32)[:], xwg1[:], placed(shared, "xwg3", [P, 2, PS], U32, cols0_at)[:]]
+        xwg = [
+            first_words[:, 0:FEWEST],
+            own("xwg1", [P, FEWEST], U32)[:],
+            own("xwg2", [P, 6 * C], U32)[:],
+            placed(shared, "xwg8", [P, 2 * C], U32, cols0_at)[:],
+        ]
         hcodes = [own("hcodes%d" % g, [P, PS], U32) for g in range(PAIRS)]
         side_first, side_end = TOKEN_CHUNKS[-1]
         base_side = own("base_side", [P, side_end - side_first], F32)
@@ -160,9 +165,9 @@ def tile_moe_adp_gelu_kernel(
         turn_first = [bank[2], bank[0]]
         turn = bank[3:5]
         second = [bank[6]] + [first_acc[2 * g + 3] for g in range(1, PAIRS - 1)]
-        last_lower = turn[1]
-        upper_acc = [second[g][:, 0:PS] for g in range(PAIRS - 1)] + [second[PAIRS - 2][:, PS:]]
-        lower_acc = [second[g][:, PS:] for g in range(PAIRS - 2)] + [last_lower[:, 0:PS], last_lower[:, PS:]]
+        second.append(turn[1])
+        upper_acc = [acc[:, 0:PS] for acc in second]
+        lower_acc = [acc[:, PS:] for acc in second]
         frozen_acc = bank[0:3]
         summing = [bank[6], bank[7], bank[3]]
 
@@ -182,21 +187,12 @@ def tile_moe_adp_gelu_kernel(
                 in_=src.bitcast(I32)[cut[0] : cut[1], 0].rearrange("e p n -> p e n"),
             )
 
-        def load_gates(i):
+        def load_gates(queue, i):
             a, b = GATE_CUTS[i]
-            nc.sync.dma_start(out=gates[i][:], in_=gate[:, a * PS : b * PS])
+            queue.dma_start(out=gates[i][:], in_=gate[:, a * PS : b * PS])
 
-        nc.vector.memset(xs[:].bitcast(I32), 0)
-        nc.vector.memset(was[0][:].bitcast(I32), 0)
+        nc.gpsimd.memset(xs[:].bitcast(I32), 0)
         nc.vector.memset(zeros[:, 0:P], 0.0)
-        nc.vector.memset(wbs[:].bitcast(I32), 0)
-
-        nc.sync.dma_start(offsets[:], offs)
-        nc.sync.dma_start(out=xw[:], in_=x_words[0].rearrange("p t d -> p (t d)").bitcast(I32))
-        load_words(nc.gpsimd, wa[0], wa_words, WA_CUTS[0])
-        load_plane(xs, x_scales[0])
-        load_planes([nc.sync, nc.sync, nc.sync, nc.gpsimd], was[0], wa_scales, WA_SCALE_CUTS[0])
-        load_planes([nc.sync] * 4, wbs, wb_scales, (0, E))
         nc.gpsimd.affine_select(
             out=ident[:],
             in_=zeros[:, 0:P],
@@ -206,18 +202,27 @@ def tile_moe_adp_gelu_kernel(
             pattern=[[-1, P]],
             channel_multiplier=1,
         )
-        load_words(nc.sync, wa[1], wa_words, WA_CUTS[1])
-        load_words(nc.sync, wb[0], wb_words, WB_CUTS[0])
-        load_gates(0)
-        load_words(nc.sync, wa[2], wa_words, WA_CUTS[2])
-        nc.gpsimd.memset(was[1][:].bitcast(I32), 0)
+        for plane in (was[0], wbs[0], was[1], wbs[1]):
+            nc.vector.memset(plane[:].bitcast(I32), 0)
+
+        nc.sync.dma_start(offsets[:], offs)
+        load_words(nc.sync, wa[0], wa_words, WA_CUTS[0])
+        load_plane(xs, x_scales[0])
+        nc.sync.dma_start(out=xw[:], in_=x_words[0].rearrange("p t d -> p (t d)").bitcast(I32))
+        load_planes([nc.sync] * 4, was[0], wa_scales, WA_SCALE_CUTS[0])
+        load_words(nc.gpsimd, wb[0], wb_words, WB_CUTS[0])
+        load_gates(nc.gpsimd, 0)
+        load_words(nc.gpsimd, wa[1], wa_words, WA_CUTS[1])
+        load_words(nc.gpsimd, wa[2], wa_words, WA_CUTS[2])
+        load_planes([nc.sync] * 4, wbs[0], wb_scales, WB_CUTS[0])
         load_planes([nc.sync] * 4, was[1], wa_scales, WA_SCALE_CUTS[1])
+        load_planes([nc.sync] * 4, wbs[1], wb_scales, WB_CUTS[1])
 
         def late_loads():
             load_words(nc.sync, wa[3], wa_words, WA_CUTS[3])
             load_words(nc.sync, wb[1], wb_words, WB_CUTS[1])
             load_words(nc.sync, wa[4], wa_words, WA_CUTS[4])
-            load_gates(1)
+            load_gates(nc.sync, 1)
             nc.gpsimd.memset(ws[:].bitcast(I32), 0)
             load_plane(ws, w_scales[0])
             nc.sync.dma_start(out=ww[:].bitcast(I32), in_=w_words[0].bitcast(I32))
@@ -226,9 +231,14 @@ def tile_moe_adp_gelu_kernel(
             return offsets[:, first_pair * PS // PER_COLUMN : end_pair * PS // PER_COLUMN]
 
         def gather_words(i):
-            nc.vector.tensor_copy(
-                out=xwg[i].rearrange("p g j -> p (g j)"), in_=xw[:].bitcast(U32).indirect(entries(*WORD_CUTS[i]))
-            )
+            first = WORD_CUTS[i][0] * C // PER_COLUMN
+            listed = offsets[:, first : first + xwg[i].shape[1] // PER_COLUMN]
+            nc.vector.tensor_copy(out=xwg[i], in_=xw[:].bitcast(U32).indirect(listed))
+
+        def slot_words(e):
+            i = [j for j, (a, b) in enumerate(WORD_CUTS) if a <= e < b][0]
+            at = (e - WORD_CUTS[i][0]) * C
+            return xwg[i][:, at : at + C]
 
         def gather_bytes(i):
             nc.vector.tensor_copy(
@@ -240,7 +250,7 @@ def tile_moe_adp_gelu_kernel(
             slots = slice(x * C, (x + 1) * C)
             nc.tensor.matmul_mx(
                 out=first_acc[e][:],
-                lhsT=pick(xwg, WORD_CUTS, g)[:, slots].bitcast(FP8X4),
+                lhsT=slot_words(e).bitcast(FP8X4),
                 lhsT_scale=pick(xsg, BYTE_CUTS, g)[:, slots],
                 rhs=pick(wa, WA_CUTS, e).bitcast(FP4X4),
                 rhs_scale=pick(was, WA_SCALE_CUTS, e),
@@ -280,7 +290,7 @@ def tile_moe_adp_gelu_kernel(
                 nc.tensor.matmul_mx(
                     out=acc[:, slots],
                     lhsT=pick(wb, WB_CUTS, e)[:, half * FP4_BYTES * P : (half + 1) * FP4_BYTES * P].bitcast(FP4X4),
-                    lhsT_scale=wbs[:, e, half * P : (half + 1) * P],
+                    lhsT_scale=pick(wbs, WB_CUTS, e)[:, half * P : (half + 1) * P],
                     rhs=hcodes[g][:, slots].bitcast(FP8X4),
                     rhs_scale=hscales[g][:, slots],
                     start=True,
@@ -342,18 +352,18 @@ def tile_moe_adp_gelu_kernel(
                     is_transpose=True,
                 )
 
-        gather_words(0)
         gather_bytes(0)
-        gather_bytes(1)
+        gather_words(0)
+        gather_words(1)
+        gather_words(2)
         open_pair(0)
         gelu(1)
-        gather_words(1)
-        gather_bytes(2)
+        gather_bytes(1)
         late_loads()
         turn_h(0, 1, turn_first[0])
         turn_h(1, 2, turn_first[1])
         quantise(0)
-        gather_words(2)
+        gather_words(3)
         second_layer(UPPER, 0, upper_acc[0])
         upper(0)
         open_pair(1)
@@ -383,8 +393,8 @@ def tile_moe_adp_gelu_kernel(
         upper(4)
         second_layer(LOWER, 3, lower_acc[3])
         second_layer(LOWER, 4, lower_acc[4])
-        nc.scalar.copy(out=y_rest[:, 0:PS], in_=lower_acc[FILLERS])
-        nc.scalar.copy(out=y_rest[:, PS:], in_=last_lower[:])
+        for g in range(FILLERS, PAIRS):
+            nc.scalar.copy(out=y_rest[:, (g - FILLERS) * PS : (g - FILLERS + 1) * PS], in_=lower_acc[g])
         scatter(LOWER, FILLERS, PAIRS, y_rest[:])
 
         for i, (a, b) in enumerate(TOKEN_CHUNKS):

@@ -79,18 +79,25 @@ def tile_moe_adp_gelu_kernel(
 
         soon_specs = [
             ("xw", [P, T], I32, 4 * T),
+            ("was0", [P, 4, H], U8, 4 * H),
+            ("wbs0", [P, 4, N], U8, 4 * N),
+            ("xsg0", [P, 3, PS], U8, 3 * PS),
+        ]
+        next_specs = [
             ("wa2", [P, 2, WA_BYTES], U8, 2 * WA_BYTES),
             ("wa4", [P, 2, WA_BYTES], U8, 2 * WA_BYTES),
             ("wb0", [P, 4, WB_BYTES], U8, 4 * WB_BYTES),
             ("gates0", [P, 2 * PS], F32, 4 * 2 * PS),
-            ("was0", [P, 4, H], U8, 4 * H),
-            ("wbs0", [P, 4, N], U8, 4 * N),
             ("wbs4", [P, 6, N], U8, 6 * N),
             ("was4", [P, 6, H], U8, 6 * H),
-            ("xsg0", [P, 3, PS], U8, 3 * PS),
         ]
-        zeros = placed(soon, "zeros", [P, sum([s[3] for s in soon_specs]) // 4], F32, 0)
-        xw, wa2, wa4, wb0, gates0, was0, wbs0, wbs4, was4, xsg0 = laid_out(soon, soon_specs)
+        next_at = sum([s[3] for s in soon_specs])
+        next_size = sum([s[3] for s in next_specs])
+        zeros = [
+            placed(soon, "zeros0", [P, (next_at + next_size) // 4], F32, 0),
+            placed(soon, "zeros1", [P, next_size // 4], F32, next_at),
+        ]
+        xw, was0, wbs0, xsg0, wa2, wa4, wb0, gates0, wbs4, was4 = laid_out(soon, soon_specs + next_specs)
         wbs = [wbs0, wbs4]
         was = [was0, was4]
 
@@ -191,30 +198,36 @@ def tile_moe_adp_gelu_kernel(
             a, b = GATE_CUTS[i]
             queue.dma_start(out=gates[i][:], in_=gate[:, a * PS : b * PS])
 
+        def identity_half(i):
+            nc.vector.memset(zeros[i][:, 0 : P // 2], 0.0)
+            nc.gpsimd.affine_select(
+                out=ident[:, i * P // 2 : (i + 1) * P // 2],
+                in_=zeros[i][:, 0 : P // 2],
+                compare_op=mybir.AluOpType.not_equal,
+                fill=1.0,
+                base=-i * P // 2,
+                pattern=[[-1, P // 2]],
+                channel_multiplier=1,
+            )
+
         nc.gpsimd.memset(xs[:].bitcast(I32), 0)
-        nc.vector.memset(zeros[:, 0:P], 0.0)
-        nc.gpsimd.affine_select(
-            out=ident[:],
-            in_=zeros[:, 0:P],
-            compare_op=mybir.AluOpType.not_equal,
-            fill=1.0,
-            base=0,
-            pattern=[[-1, P]],
-            channel_multiplier=1,
-        )
-        for plane in (was[0], wbs[0], was[1], wbs[1]):
+        identity_half(0)
+        for plane in (was[0], wbs[0]):
             nc.vector.memset(plane[:].bitcast(I32), 0)
+        identity_half(1)
+        for plane in (was[1], wbs[1]):
+            nc.gpsimd.memset(plane[:].bitcast(I32), 0)
 
         nc.sync.dma_start(offsets[:], offs)
         load_words(nc.sync, wa[0], wa_words, WA_CUTS[0])
         load_plane(xs, x_scales[0])
         nc.sync.dma_start(out=xw[:], in_=x_words[0].rearrange("p t d -> p (t d)").bitcast(I32))
         load_planes([nc.sync] * 4, was[0], wa_scales, WA_SCALE_CUTS[0])
-        load_words(nc.gpsimd, wb[0], wb_words, WB_CUTS[0])
-        load_gates(nc.gpsimd, 0)
-        load_words(nc.gpsimd, wa[1], wa_words, WA_CUTS[1])
-        load_words(nc.gpsimd, wa[2], wa_words, WA_CUTS[2])
         load_planes([nc.sync] * 4, wbs[0], wb_scales, WB_CUTS[0])
+        load_words(nc.sync, wa[1], wa_words, WA_CUTS[1])
+        load_words(nc.sync, wb[0], wb_words, WB_CUTS[0])
+        load_gates(nc.sync, 0)
+        load_words(nc.sync, wa[2], wa_words, WA_CUTS[2])
         load_planes([nc.sync] * 4, was[1], wa_scales, WA_SCALE_CUTS[1])
         load_planes([nc.sync] * 4, wbs[1], wb_scales, WB_CUTS[1])
 

@@ -32,9 +32,10 @@ WA_CUTS = [(2 * g, 2 * g + 2) for g in range(PAIRS)]
 WA_SCALE_CUTS = [(0, 4), (4, E)]
 WB_CUTS = [(0, 4), (4, E)]
 GATE_CUTS = [(0, 2), (2, PAIRS)]
-WORD_CUTS = [(0, 1), (1, 2), (2, 8), (8, E)]
 FEWEST = T // 8
-BYTE_CUTS = [(0, 3), (3, PAIRS)]
+HELD = 7 * C
+WORD_CUTS = [(0, FEWEST), (FEWEST, 2 * FEWEST), (2 * FEWEST, HELD), (HELD, T)]
+BYTE_CUTS = [(0, 5), (5, E)]
 TOKEN_CHUNKS = [(0, BANK), (BANK, 2 * BANK), (2 * BANK, T)]
 FILLERS = 2
 WINDOW = 2048
@@ -50,7 +51,6 @@ def tile_moe_adp_gelu_kernel(
         keep = ctx.enter_context(tc.tile_pool(name="keep", bufs=1))
         shared = ctx.enter_context(tc.tile_pool(name="shared", bufs=1))
         soon = ctx.enter_context(tc.tile_pool(name="soon", bufs=1))
-        late = ctx.enter_context(tc.tile_pool(name="late", bufs=1))
         psum = ctx.enter_context(tc.psum_pool(name="psum", bufs=1))
 
         def own(name, shape, dtype):
@@ -59,8 +59,8 @@ def tile_moe_adp_gelu_kernel(
         def placed(pool, name, shape, dtype, at):
             return pool.tile(shape, dtype, name=name, align_bytes=64, offset=at)
 
-        def laid_out(pool, specs):
-            tiles, at = [], 0
+        def laid_out(pool, specs, at):
+            tiles = []
             for name, shape, dtype, size in specs:
                 tiles.append(placed(pool, name, shape, dtype, at))
                 at = at + size
@@ -81,7 +81,7 @@ def tile_moe_adp_gelu_kernel(
             ("xw", [P, T], I32, 4 * T),
             ("was0", [P, 4, H], U8, 4 * H),
             ("wbs0", [P, 4, N], U8, 4 * N),
-            ("xsg0", [P, 3, PS], U8, 3 * PS),
+            ("xsg0", [P, 5, C], U8, 5 * C),
         ]
         next_specs = [
             ("wa2", [P, 2, WA_BYTES], U8, 2 * WA_BYTES),
@@ -93,31 +93,33 @@ def tile_moe_adp_gelu_kernel(
         ]
         next_at = sum([s[3] for s in soon_specs])
         next_size = sum([s[3] for s in next_specs])
+        late_at = next_at + next_size
         zeros = [
-            placed(soon, "zeros0", [P, (next_at + next_size) // 4], F32, 0),
+            placed(soon, "zeros0", [P, (late_at + WA_BYTES) // 4], F32, 0),
             placed(soon, "zeros1", [P, next_size // 4], F32, next_at),
         ]
-        xw, was0, wbs0, xsg0, wa2, wa4, wb0, gates0, wbs4, was4 = laid_out(soon, soon_specs + next_specs)
+        xw, was0, wbs0, xsg0, wa2, wa4, wb0, gates0, wbs4, was4 = laid_out(soon, soon_specs + next_specs, 0)
         wbs = [wbs0, wbs4]
         was = [was0, was4]
 
         late_specs = [
-            ("xsg3", [P, 2, PS], U8, 2 * PS),
+            ("xsg3", [P, 5, C], U8, WA_BYTES),
             ("wb4", [P, 6, WB_BYTES], U8, 6 * WB_BYTES),
             ("gates2", [P, 3 * PS], F32, 4 * 3 * PS),
             ("ww", [P, WB_BYTES], U8, WB_BYTES),
-            ("ws", [P, N], U8, N),
+            ("ws", [P, N], U8, WB_BYTES),
             ("wa6", [P, 3, WA_BYTES], U8, 3 * WA_BYTES),
             ("h_rows2", [P, 2, H], BF16, REGION),
             ("wa8", [P, 3, WA_BYTES], U8, 3 * WA_BYTES),
         ]
-        rows3_at = sum([s[3] for s in late_specs])
+        late_size = sum([s[3] for s in late_specs])
+        rows3_at = late_at + late_size
         wa8_at = rows3_at - 3 * WA_BYTES
         rows2_at = wa8_at - REGION
         wa6_at = rows2_at - 3 * WA_BYTES
-        first_words = placed(late, "first_words", [P, rows3_at // 4], U32, 0)
-        xsg3, wb4, gates2, ww, ws, wa6, h_rows2, wa8 = laid_out(late, late_specs)
-        wa = [own("wa0", [P, 2, WA_BYTES], U8), wa2, wa4, wa6, wa8]
+        wa0 = placed(soon, "wa0", [P, late_size // WA_BYTES, WA_BYTES], U8, late_at)
+        xsg3, wb4, gates2, ww, ws, wa6, h_rows2, wa8 = laid_out(soon, late_specs, late_at)
+        wa = [wa0, wa2, wa4, wa6, wa8]
         wb = [wb0, wb4]
         gates = [gates0, gates2]
         xsg = [xsg0[:], xsg3[:]]
@@ -128,34 +130,29 @@ def tile_moe_adp_gelu_kernel(
             own("h_rows0", [P, 2, H], BF16),
             placed(shared, "h_rows1", [P, 2, H], BF16, 0),
             h_rows2,
-            placed(late, "h_rows3", [P, 2, H], BF16, rows3_at),
+            placed(soon, "h_rows3", [P, 2, H], BF16, rows3_at),
             placed(shared, "h_rows4", [P, 2, H], BF16, rows4_at),
         ]
         straddle = HALF_REGION // 2
         y_upper = [
             own("y_upper0", [P, PS], F32),
             own("y_upper1", [P, PS], F32),
-            placed(late, "y_upper2", [P, PS], F32, rows3_at - straddle),
+            placed(soon, "y_upper2", [P, PS], F32, rows3_at - straddle),
             placed(shared, "y_upper3", [P, PS], F32, rows4_at),
             own("y_upper4", [P, PS], F32),
         ]
         y_lower = [
             placed(shared, "y_lower0", [P, PS], F32, 0),
-            placed(late, "y_lower1", [P, PS], F32, rows2_at - straddle),
+            placed(soon, "y_lower1", [P, PS], F32, rows2_at - straddle),
         ]
         h_cols = [
             placed(shared, "h_cols0", [P, 4 * PS], BF16, cols0_at),
             own("h_cols1", [P, 4 * PS], BF16),
-            placed(late, "h_cols2", [P, 4 * PS], BF16, wa6_at),
-            placed(late, "h_cols3", [P, 4 * PS], BF16, wa8_at),
+            placed(soon, "h_cols2", [P, 4 * PS], BF16, wa6_at),
+            placed(soon, "h_cols3", [P, 4 * PS], BF16, wa8_at),
             own("h_cols4", [P, 4 * PS], BF16),
         ]
-        xwg = [
-            first_words[:, 0:FEWEST],
-            own("xwg1", [P, FEWEST], U32)[:],
-            own("xwg2", [P, 6 * C], U32)[:],
-            placed(shared, "xwg8", [P, 2 * C], U32, cols0_at)[:],
-        ]
+        xwg = [own("xwg0", [P, HELD], U32), placed(shared, "xwg7", [P, T - HELD], U32, cols0_at)]
         hcodes = [own("hcodes%d" % g, [P, PS], U32) for g in range(PAIRS)]
         side_first, side_end = TOKEN_CHUNKS[-1]
         base_side = own("base_side", [P, side_end - side_first], F32)
@@ -219,9 +216,9 @@ def tile_moe_adp_gelu_kernel(
             nc.gpsimd.memset(plane[:].bitcast(I32), 0)
 
         nc.sync.dma_start(offsets[:], offs)
-        load_words(nc.sync, wa[0], wa_words, WA_CUTS[0])
         load_plane(xs, x_scales[0])
         nc.sync.dma_start(out=xw[:], in_=x_words[0].rearrange("p t d -> p (t d)").bitcast(I32))
+        load_words(nc.sync, wa[0], wa_words, WA_CUTS[0])
         load_planes([nc.sync] * 4, was[0], wa_scales, WA_SCALE_CUTS[0])
         load_planes([nc.sync] * 4, wbs[0], wb_scales, WB_CUTS[0])
         load_words(nc.sync, wa[1], wa_words, WA_CUTS[1])
@@ -243,28 +240,24 @@ def tile_moe_adp_gelu_kernel(
         def entries(first_pair, end_pair):
             return offsets[:, first_pair * PS // PER_COLUMN : end_pair * PS // PER_COLUMN]
 
-        def gather_words(i):
-            first = WORD_CUTS[i][0] * C // PER_COLUMN
-            listed = offsets[:, first : first + xwg[i].shape[1] // PER_COLUMN]
-            nc.vector.tensor_copy(out=xwg[i], in_=xw[:].bitcast(U32).indirect(listed))
+        def slot_words(a, b):
+            return xwg[0][:, a:b] if a < HELD else xwg[1][:, a - HELD : b - HELD]
 
-        def slot_words(e):
-            i = [j for j, (a, b) in enumerate(WORD_CUTS) if a <= e < b][0]
-            at = (e - WORD_CUTS[i][0]) * C
-            return xwg[i][:, at : at + C]
+        def gather_words(i):
+            a, b = WORD_CUTS[i]
+            listed = offsets[:, a // PER_COLUMN : b // PER_COLUMN]
+            nc.vector.tensor_copy(out=slot_words(a, b), in_=xw[:].bitcast(U32).indirect(listed))
 
         def gather_bytes(i):
-            nc.vector.tensor_copy(
-                out=xsg[i].rearrange("p g j -> p (g j)"), in_=xs[:].indirect(entries(*BYTE_CUTS[i]))
-            )
+            a, b = BYTE_CUTS[i]
+            listed = offsets[:, a * C // PER_COLUMN : b * C // PER_COLUMN]
+            nc.vector.tensor_copy(out=xsg[i].rearrange("p e j -> p (e j)"), in_=xs[:].indirect(listed))
 
         def first_product(e):
-            g, x = divmod(e, 2)
-            slots = slice(x * C, (x + 1) * C)
             nc.tensor.matmul_mx(
                 out=first_acc[e][:],
-                lhsT=slot_words(e).bitcast(FP8X4),
-                lhsT_scale=pick(xsg, BYTE_CUTS, g)[:, slots],
+                lhsT=slot_words(e * C, (e + 1) * C).bitcast(FP8X4),
+                lhsT_scale=pick(xsg, BYTE_CUTS, e),
                 rhs=pick(wa, WA_CUTS, e).bitcast(FP4X4),
                 rhs_scale=pick(was, WA_SCALE_CUTS, e),
                 start=True,
@@ -293,8 +286,12 @@ def tile_moe_adp_gelu_kernel(
                 in_=turned.rearrange("p x u j -> p x j u"),
             )
 
-        def quantise(g):
-            nc.vector.quantize_mx(out=hcodes[g][:].bitcast(FP8X4), scales=hscales[g][:], in_=h_cols[g][:])
+        def quantise(e0, e1):
+            g, x0 = divmod(e0, 2)
+            a, b = x0 * C, (x0 + e1 - e0) * C
+            nc.vector.quantize_mx(
+                out=hcodes[g][:, a:b].bitcast(FP8X4), scales=hscales[g][:, a:b], in_=h_cols[g][:, 4 * a : 4 * b]
+            )
 
         def second_layer(half, g, acc):
             for x in range(2):
@@ -317,7 +314,7 @@ def tile_moe_adp_gelu_kernel(
 
         def to_codes(g):
             turn_h(2 * g, 2 * g + 2, turn[(g + 1) % 2])
-            quantise(g)
+            quantise(2 * g, 2 * g + 2)
 
         def second_layers(g):
             second_layer(UPPER, g, upper_acc[g])
@@ -374,8 +371,9 @@ def tile_moe_adp_gelu_kernel(
         gather_bytes(1)
         late_loads()
         turn_h(0, 1, turn_first[0])
+        quantise(0, 1)
         turn_h(1, 2, turn_first[1])
-        quantise(0)
+        quantise(1, 2)
         gather_words(3)
         second_layer(UPPER, 0, upper_acc[0])
         upper(0)

@@ -32,10 +32,10 @@ WA_CUTS = [(2 * g, 2 * g + 2) for g in range(PAIRS)]
 WA_SCALE_CUTS = [(0, 4), (4, E)]
 WB_CUTS = [(0, 4), (4, E)]
 GATE_CUTS = [(0, 2), (2, PAIRS)]
-FEWEST = T // 8
+SHORT = T // 8
 HELD = 7 * C
-WORD_CUTS = [(0, FEWEST), (FEWEST, 2 * FEWEST), (2 * FEWEST, HELD), (HELD, T)]
-BYTE_CUTS = [(0, 5), (5, E)]
+WORD_CUTS = [(0, SHORT), (SHORT, 2 * SHORT), (2 * SHORT, HELD), (HELD, T)]
+BYTE_CUTS = [(0, E // 2), (E // 2, E)]
 TOKEN_CHUNKS = [(0, BANK), (BANK, 2 * BANK), (2 * BANK, T)]
 FILLERS = 2
 WINDOW = 2048
@@ -50,7 +50,7 @@ def tile_moe_adp_gelu_kernel(
     with ExitStack() as ctx:
         keep = ctx.enter_context(tc.tile_pool(name="keep", bufs=1))
         shared = ctx.enter_context(tc.tile_pool(name="shared", bufs=1))
-        soon = ctx.enter_context(tc.tile_pool(name="soon", bufs=1))
+        staged = ctx.enter_context(tc.tile_pool(name="staged", bufs=1))
         psum = ctx.enter_context(tc.psum_pool(name="psum", bufs=1))
 
         def own(name, shape, dtype):
@@ -95,15 +95,15 @@ def tile_moe_adp_gelu_kernel(
         next_size = sum([s[3] for s in next_specs])
         late_at = next_at + next_size
         zeros = [
-            placed(soon, "zeros0", [P, (late_at + WA_BYTES) // 4], F32, 0),
-            placed(soon, "zeros1", [P, next_size // 4], F32, next_at),
+            placed(staged, "zeros0", [P, late_at // 4], F32, 0),
+            placed(staged, "zeros1", [P, next_size // 4], F32, next_at),
         ]
-        xw, was0, wbs0, xsg0, wa2, wa4, wb0, gates0, wbs4, was4 = laid_out(soon, soon_specs + next_specs, 0)
+        xw, was0, wbs0, xsg0, wa2, wa4, wb0, gates0, wbs4, was4 = laid_out(staged, soon_specs + next_specs, 0)
         wbs = [wbs0, wbs4]
         was = [was0, was4]
 
         late_specs = [
-            ("xsg3", [P, 5, C], U8, WA_BYTES),
+            ("xsg5", [P, 5, C], U8, WA_BYTES),
             ("wb4", [P, 6, WB_BYTES], U8, 6 * WB_BYTES),
             ("gates2", [P, 3 * PS], F32, 4 * 3 * PS),
             ("ww", [P, WB_BYTES], U8, WB_BYTES),
@@ -117,12 +117,12 @@ def tile_moe_adp_gelu_kernel(
         wa8_at = rows3_at - 3 * WA_BYTES
         rows2_at = wa8_at - REGION
         wa6_at = rows2_at - 3 * WA_BYTES
-        wa0 = placed(soon, "wa0", [P, late_size // WA_BYTES, WA_BYTES], U8, late_at)
-        xsg3, wb4, gates2, ww, ws, wa6, h_rows2, wa8 = laid_out(soon, late_specs, late_at)
+        wa0 = placed(staged, "wa0", [P, late_size // WA_BYTES, WA_BYTES], U8, late_at)
+        xsg5, wb4, gates2, ww, ws, wa6, h_rows2, wa8 = laid_out(staged, late_specs, late_at)
         wa = [wa0, wa2, wa4, wa6, wa8]
         wb = [wb0, wb4]
         gates = [gates0, gates2]
-        xsg = [xsg0[:], xsg3[:]]
+        xsg = [xsg0, xsg5]
 
         rows4_at = 3 * REGION
         cols0_at = rows4_at + REGION
@@ -130,26 +130,26 @@ def tile_moe_adp_gelu_kernel(
             own("h_rows0", [P, 2, H], BF16),
             placed(shared, "h_rows1", [P, 2, H], BF16, 0),
             h_rows2,
-            placed(soon, "h_rows3", [P, 2, H], BF16, rows3_at),
+            placed(staged, "h_rows3", [P, 2, H], BF16, rows3_at),
             placed(shared, "h_rows4", [P, 2, H], BF16, rows4_at),
         ]
         straddle = HALF_REGION // 2
         y_upper = [
             own("y_upper0", [P, PS], F32),
             own("y_upper1", [P, PS], F32),
-            placed(soon, "y_upper2", [P, PS], F32, rows3_at - straddle),
+            placed(staged, "y_upper2", [P, PS], F32, rows3_at - straddle),
             placed(shared, "y_upper3", [P, PS], F32, rows4_at),
             own("y_upper4", [P, PS], F32),
         ]
         y_lower = [
             placed(shared, "y_lower0", [P, PS], F32, 0),
-            placed(soon, "y_lower1", [P, PS], F32, rows2_at - straddle),
+            placed(staged, "y_lower1", [P, PS], F32, rows2_at - straddle),
         ]
         h_cols = [
             placed(shared, "h_cols0", [P, 4 * PS], BF16, cols0_at),
             own("h_cols1", [P, 4 * PS], BF16),
-            placed(soon, "h_cols2", [P, 4 * PS], BF16, wa6_at),
-            placed(soon, "h_cols3", [P, 4 * PS], BF16, wa8_at),
+            placed(staged, "h_cols2", [P, 4 * PS], BF16, wa6_at),
+            placed(staged, "h_cols3", [P, 4 * PS], BF16, wa8_at),
             own("h_cols4", [P, 4 * PS], BF16),
         ]
         xwg = [own("xwg0", [P, HELD], U32), placed(shared, "xwg7", [P, T - HELD], U32, cols0_at)]
@@ -180,20 +180,20 @@ def tile_moe_adp_gelu_kernel(
             for r in range(4):
                 nc.sync.dma_start(out=plane[r:P:32, :].bitcast(I32), in_=src[r])
 
-        def load_planes(queues, planes, rows, cut):
+        def load_planes(planes, rows, cut):
             src = rows.bitcast(I32)[cut[0] : cut[1], 0].rearrange("e (q r) n -> r q e n", r=4)
             for r in range(4):
-                queues[r].dma_start(out=planes[r:P:32, :, :].bitcast(I32), in_=src[r])
+                nc.sync.dma_start(out=planes[r:P:32, :, :].bitcast(I32), in_=src[r])
 
-        def load_words(queue, words, src, cut):
-            queue.dma_start(
+        def load_words(words, src, cut):
+            nc.sync.dma_start(
                 out=words[:, 0 : cut[1] - cut[0], :].bitcast(I32),
                 in_=src.bitcast(I32)[cut[0] : cut[1], 0].rearrange("e p n -> p e n"),
             )
 
-        def load_gates(queue, i):
+        def load_gates(i):
             a, b = GATE_CUTS[i]
-            queue.dma_start(out=gates[i][:], in_=gate[:, a * PS : b * PS])
+            nc.sync.dma_start(out=gates[i][:], in_=gate[:, a * PS : b * PS])
 
         def identity_half(i):
             nc.vector.memset(zeros[i][:, 0 : P // 2], 0.0)
@@ -216,23 +216,23 @@ def tile_moe_adp_gelu_kernel(
             nc.gpsimd.memset(plane[:].bitcast(I32), 0)
 
         nc.sync.dma_start(offsets[:], offs)
+        load_words(wa[0], wa_words, WA_CUTS[0])
         load_plane(xs, x_scales[0])
         nc.sync.dma_start(out=xw[:], in_=x_words[0].rearrange("p t d -> p (t d)").bitcast(I32))
-        load_words(nc.sync, wa[0], wa_words, WA_CUTS[0])
-        load_planes([nc.sync] * 4, was[0], wa_scales, WA_SCALE_CUTS[0])
-        load_planes([nc.sync] * 4, wbs[0], wb_scales, WB_CUTS[0])
-        load_words(nc.sync, wa[1], wa_words, WA_CUTS[1])
-        load_words(nc.sync, wb[0], wb_words, WB_CUTS[0])
-        load_gates(nc.sync, 0)
-        load_words(nc.sync, wa[2], wa_words, WA_CUTS[2])
-        load_planes([nc.sync] * 4, was[1], wa_scales, WA_SCALE_CUTS[1])
-        load_planes([nc.sync] * 4, wbs[1], wb_scales, WB_CUTS[1])
+        load_planes(was[0], wa_scales, WA_SCALE_CUTS[0])
+        load_planes(wbs[0], wb_scales, WB_CUTS[0])
+        load_words(wa[1], wa_words, WA_CUTS[1])
+        load_words(wb[0], wb_words, WB_CUTS[0])
+        load_gates(0)
+        load_words(wa[2], wa_words, WA_CUTS[2])
+        load_planes(was[1], wa_scales, WA_SCALE_CUTS[1])
+        load_planes(wbs[1], wb_scales, WB_CUTS[1])
 
         def late_loads():
-            load_words(nc.sync, wa[3], wa_words, WA_CUTS[3])
-            load_words(nc.sync, wb[1], wb_words, WB_CUTS[1])
-            load_words(nc.sync, wa[4], wa_words, WA_CUTS[4])
-            load_gates(nc.sync, 1)
+            load_words(wa[3], wa_words, WA_CUTS[3])
+            load_words(wb[1], wb_words, WB_CUTS[1])
+            load_words(wa[4], wa_words, WA_CUTS[4])
+            load_gates(1)
             nc.gpsimd.memset(ws[:].bitcast(I32), 0)
             load_plane(ws, w_scales[0])
             nc.sync.dma_start(out=ww[:].bitcast(I32), in_=w_words[0].bitcast(I32))
@@ -251,7 +251,7 @@ def tile_moe_adp_gelu_kernel(
         def gather_bytes(i):
             a, b = BYTE_CUTS[i]
             listed = offsets[:, a * C // PER_COLUMN : b * C // PER_COLUMN]
-            nc.vector.tensor_copy(out=xsg[i].rearrange("p e j -> p (e j)"), in_=xs[:].indirect(listed))
+            nc.vector.tensor_copy(out=xsg[i][:].rearrange("p e j -> p (e j)"), in_=xs[:].indirect(listed))
 
         def first_product(e):
             nc.tensor.matmul_mx(

@@ -156,11 +156,11 @@ def tile_moe_adp_gelu_kernel(
         hcodes = [own("hcodes%d" % g, [P, PS], U32) for g in range(PAIRS)]
         side_first, side_end = TOKEN_CHUNKS[-1]
         base_side = own("base_side", [P, side_end - side_first], F32)
-        result_side = own("result_side", [P, side_end - side_first], F32)
         y_rest = own("y_rest", [P, (PAIRS - FILLERS) * PS], F32)
         base_at = rows4_at + HALF_REGION
         base_upper = placed(shared, "base_upper", [P, T], F32, base_at)
         sum_turned = placed(shared, "sum_turned", [P, T], F32, base_at)
+        result_side = placed(shared, "result_side", [P, side_end - side_first], F32, base_at)
 
         bank = [psum.tile([P, BANK], F32, name="bank%d" % b) for b in range(8)]
         first_acc = [bank[0], bank[1]]
@@ -424,6 +424,7 @@ def tile_moe_adp_gelu_kernel(
         nc.gpsimd.tensor_tensor(
             out=result_side[:], in0=base_side[:], in1=window[LOWER][:, side_first:side_end], op=ADD
         )
+        nc.scalar.dma_start(out=out[P : 2 * P, side_first:side_end], in_=result_side[:])
         for a in range(0, side_first, PS):
             nc.vector.tensor_tensor(
                 out=result[LOWER][:, a : a + PS],
@@ -432,4 +433,3 @@ def tile_moe_adp_gelu_kernel(
                 op=ADD,
             )
             nc.sync.dma_start(out=out[P : 2 * P, a : a + PS], in_=result[LOWER][:, a : a + PS])
-        nc.sync.dma_start(out=out[P : 2 * P, side_first:side_end], in_=result_side[:])

@@ -81,9 +81,9 @@ def tile_moe_adp_gelu_kernel(
             ("xw", [P, T], I32, 4 * T),
             ("was0", [P, 4, H], U8, 4 * H),
             ("wbs0", [P, 4, N], U8, 4 * N),
-            ("xsg0", [P, 5, C], U8, 5 * C),
         ]
         next_specs = [
+            ("xsg0", [P, 5, C], U8, 5 * C),
             ("wa2", [P, 2, WA_BYTES], U8, 2 * WA_BYTES),
             ("wa4", [P, 2, WA_BYTES], U8, 2 * WA_BYTES),
             ("wb0", [P, 4, WB_BYTES], U8, 4 * WB_BYTES),
@@ -212,8 +212,8 @@ def tile_moe_adp_gelu_kernel(
         for plane in (was[0], wbs[0]):
             nc.vector.memset(plane[:].bitcast(I32), 0)
         identity_half(1)
-        for plane in (was[1], wbs[1]):
-            nc.gpsimd.memset(plane[:].bitcast(I32), 0)
+        nc.vector.memset(was[1][:].bitcast(I32), 0)
+        nc.gpsimd.memset(wbs[1][:].bitcast(I32), 0)
 
         nc.sync.dma_start(offsets[:], offs)
         load_words(wa[0], wa_words, WA_CUTS[0])

@@ -400,6 +400,9 @@ def tile_moe_adp_gelu_kernel(
         to_codes(4)
         second_layer(UPPER, 3, upper_acc[3])
         upper(3)
+        for i, (a, b) in enumerate(TOKEN_CHUNKS):
+            nc.scalar.copy(out=base_upper[:, a:b], in_=frozen(UPPER, i))
+            turn_into_sum(i, base_upper, True, False)
         second_layer(UPPER, 4, upper_acc[4])
         upper(4)
         second_layer(LOWER, 3, lower_acc[3])
@@ -408,9 +411,6 @@ def tile_moe_adp_gelu_kernel(
             nc.scalar.copy(out=y_rest[:, (g - FILLERS) * PS : (g - FILLERS + 1) * PS], in_=lower_acc[g])
         scatter(LOWER, FILLERS, PAIRS, y_rest[:])
 
-        for i, (a, b) in enumerate(TOKEN_CHUNKS):
-            nc.scalar.copy(out=base_upper[:, a:b], in_=frozen(UPPER, i))
-            turn_into_sum(i, base_upper, True, False)
         base_lower = [frozen(LOWER, i) for i in range(len(TOKEN_CHUNKS))]
         nc.scalar.copy(out=base_side[:], in_=base_lower[-1])
         for i, (a, b) in enumerate(TOKEN_CHUNKS):

@@ -14,6 +14,7 @@ U8 = mybir.dt.uint8
 FP8X4 = mybir.dt.float8_e4m3fn_x4
 FP4X4 = mybir.dt.float4_e2m1fn_x4
 GELU = mybir.ActivationFunctionType.Gelu_apprx_tanh
+COPY = mybir.ActivationFunctionType.Copy
 ADD = mybir.AluOpType.add
 MULT = mybir.AluOpType.mult
 
@@ -24,23 +25,20 @@ PS = 2 * C
 PER_COLUMN = 16
 UPPER, LOWER = 0, 1
 FP4_BYTES = 2
-
 WA_BYTES = FP4_BYTES * H
 WB_BYTES = FP4_BYTES * N
 
-WA_CUTS = [(2 * g, 2 * g + 2) for g in range(PAIRS)]
+WA_CUTS = [(0, 2), (2, 3), (3, 5), (5, 7), (7, E)]
 WA_SCALE_CUTS = [(0, 4), (4, E)]
-WB_CUTS = [(0, 4), (4, E)]
-GATE_CUTS = [(0, 2), (2, PAIRS)]
+WB_CUTS = [(0, 2), (2, 4), (4, E)]
+GATE_CUTS = [(0, 1), (1, 2), (2, PAIRS)]
 SHORT = T // 8
 HELD = 7 * C
-WORD_CUTS = [(0, SHORT), (SHORT, 2 * SHORT), (2 * SHORT, HELD), (HELD, T)]
+WORD_CUTS = [(0, SHORT), (SHORT, 3 * C), (3 * C, HELD), (HELD, T)]
 BYTE_CUTS = [(0, E // 2), (E // 2, E)]
+QUANT_CUTS = [(0, 1), (1, 2), (2, 3), (3, PAIRS)]
+LOWER_CUTS = [(0, PS), (PS, 2 * PS), (2 * PS, 7 * C), (7 * C, T)]
 TOKEN_CHUNKS = [(0, BANK), (BANK, 2 * BANK), (2 * BANK, T)]
-FILLERS = 2
-WINDOW = 2048
-REGION = 4 * H
-HALF_REGION = REGION // 2
 
 
 def tile_moe_adp_gelu_kernel(
@@ -49,131 +47,87 @@ def tile_moe_adp_gelu_kernel(
     nc = tc.nc
     with ExitStack() as ctx:
         keep = ctx.enter_context(tc.tile_pool(name="keep", bufs=1))
-        shared = ctx.enter_context(tc.tile_pool(name="shared", bufs=1))
         staged = ctx.enter_context(tc.tile_pool(name="staged", bufs=1))
         psum = ctx.enter_context(tc.psum_pool(name="psum", bufs=1))
 
         def own(name, shape, dtype):
             return keep.tile(shape, dtype, name=name, align_bytes=64)
 
-        def placed(pool, name, shape, dtype, at):
-            return pool.tile(shape, dtype, name=name, align_bytes=64, offset=at)
+        def placed(name, shape, dtype, at):
+            return staged.tile(shape, dtype, name=name, align_bytes=64, offset=at)
 
-        def laid_out(pool, specs, at):
+        def laid_out(specs, at):
             tiles = []
             for name, shape, dtype, size in specs:
-                tiles.append(placed(pool, name, shape, dtype, at))
+                tiles.append(placed(name, shape, dtype, at))
                 at = at + size
             return tiles
 
+        def cut_of(cuts, index):
+            return [j for j, (a, b) in enumerate(cuts) if a <= index < b][0]
+
         def pick(tiles, cuts, index):
-            i = [j for j, (a, b) in enumerate(cuts) if a <= index < b][0]
+            i = cut_of(cuts, index)
             return tiles[i][:, index - cuts[i][0], :]
 
         offsets = keep.tile([P, T // PER_COLUMN], U16, name="offsets")
         xs = own("xs", [P, T], U8)
         ident = own("ident", [P, P], F32)
-        hscales = [own("hscales%d" % g, [P, PS], U8) for g in range(PAIRS)]
-        window = [own("window%d" % half, [P, WINDOW], F32) for half in (UPPER, LOWER)]
         result = [own("result%d" % half, [P, T], F32) for half in (UPPER, LOWER)]
 
         soon_specs = [
             ("xw", [P, T], I32, 4 * T),
             ("was0", [P, 4, H], U8, 4 * H),
-            ("wbs0", [P, 4, N], U8, 4 * N),
         ]
         next_specs = [
             ("xsg0", [P, 5, C], U8, 5 * C),
-            ("wa2", [P, 2, WA_BYTES], U8, 2 * WA_BYTES),
-            ("wa4", [P, 2, WA_BYTES], U8, 2 * WA_BYTES),
-            ("wb0", [P, 4, WB_BYTES], U8, 4 * WB_BYTES),
-            ("gates0", [P, 2 * PS], F32, 4 * 2 * PS),
-            ("wbs4", [P, 6, N], U8, 6 * N),
+            ("wbs", [P, E, N], U8, E * N),
             ("was4", [P, 6, H], U8, 6 * H),
+            ("ww", [P, WB_BYTES], U8, WB_BYTES),
+            ("ws", [P, N], U8, N),
         ]
+        next_specs += [("wb%d" % a, [P, b - a, WB_BYTES], U8, (b - a) * WB_BYTES) for a, b in WB_CUTS]
+        next_specs += [("gates%d" % a, [P, (b - a) * PS], F32, 4 * (b - a) * PS) for a, b in GATE_CUTS]
+        next_specs += [("wa%d" % a, [P, b - a, WA_BYTES], U8, (b - a) * WA_BYTES) for a, b in WA_CUTS[1:]]
         next_at = sum([s[3] for s in soon_specs])
         next_size = sum([s[3] for s in next_specs])
         late_at = next_at + next_size
         zeros = [
-            placed(staged, "zeros0", [P, late_at // 4], F32, 0),
-            placed(staged, "zeros1", [P, next_size // 4], F32, next_at),
+            placed("zeros0", [P, late_at // 4], F32, 0),
+            placed("zeros1", [P, next_size // 4], F32, next_at),
         ]
-        xw, was0, wbs0, xsg0, wa2, wa4, wb0, gates0, wbs4, was4 = laid_out(staged, soon_specs + next_specs, 0)
-        wbs = [wbs0, wbs4]
+        tiles = laid_out(soon_specs + next_specs, 0)
+        xw, was0, xsg0, wbs, was4, ww, ws = tiles[0:7]
         was = [was0, was4]
-
-        late_specs = [
-            ("xsg5", [P, 5, C], U8, WA_BYTES),
-            ("wb4", [P, 6, WB_BYTES], U8, 6 * WB_BYTES),
-            ("gates2", [P, 3 * PS], F32, 4 * 3 * PS),
-            ("ww", [P, WB_BYTES], U8, WB_BYTES),
-            ("ws", [P, N], U8, WB_BYTES),
-            ("wa6", [P, 3, WA_BYTES], U8, 3 * WA_BYTES),
-            ("h_rows2", [P, 2, H], BF16, REGION),
-            ("wa8", [P, 3, WA_BYTES], U8, 3 * WA_BYTES),
-        ]
-        late_size = sum([s[3] for s in late_specs])
-        rows3_at = late_at + late_size
-        wa8_at = rows3_at - 3 * WA_BYTES
-        rows2_at = wa8_at - REGION
-        wa6_at = rows2_at - 3 * WA_BYTES
-        wa0 = placed(staged, "wa0", [P, late_size // WA_BYTES, WA_BYTES], U8, late_at)
-        xsg5, wb4, gates2, ww, ws, wa6, h_rows2, wa8 = laid_out(staged, late_specs, late_at)
-        wa = [wa0, wa2, wa4, wa6, wa8]
-        wb = [wb0, wb4]
-        gates = [gates0, gates2]
+        wa0 = placed("wa0", [P, 2, WA_BYTES], U8, late_at)
+        xsg5 = placed("xsg5", [P, 5, C], U8, late_at)
+        wb = tiles[7:10]
+        gates = tiles[10:13]
+        wa = [wa0] + tiles[13:]
         xsg = [xsg0, xsg5]
 
-        rows4_at = 3 * REGION
-        cols0_at = rows4_at + REGION
+        cols0_at = late_at + 2 * WA_BYTES
+        rows9_at = cols0_at + 8 * PS
+        rows_at = {a: late_at - (E - a) * WA_BYTES for a, b in WA_CUTS[2:]}
+        rows_at[E - 1] = rows9_at
         h_rows = [
-            own("h_rows0", [P, 2, H], BF16),
-            placed(shared, "h_rows1", [P, 2, H], BF16, 0),
-            h_rows2,
-            placed(staged, "h_rows3", [P, 2, H], BF16, rows3_at),
-            placed(shared, "h_rows4", [P, 2, H], BF16, rows4_at),
+            placed("h_rows%d" % e, [P, H], BF16, rows_at[e]) if e in rows_at else own("h_rows%d" % e, [P, H], BF16)
+            for e in range(E)
         ]
-        straddle = HALF_REGION // 2
-        y_upper = [
-            own("y_upper0", [P, PS], F32),
-            own("y_upper1", [P, PS], F32),
-            placed(staged, "y_upper2", [P, PS], F32, rows3_at - straddle),
-            placed(shared, "y_upper3", [P, PS], F32, rows4_at),
-            own("y_upper4", [P, PS], F32),
-        ]
-        y_lower = [
-            placed(shared, "y_lower0", [P, PS], F32, 0),
-            placed(staged, "y_lower1", [P, PS], F32, rows2_at - straddle),
-        ]
-        h_cols = [
-            placed(shared, "h_cols0", [P, 4 * PS], BF16, cols0_at),
-            own("h_cols1", [P, 4 * PS], BF16),
-            placed(staged, "h_cols2", [P, 4 * PS], BF16, wa6_at),
-            placed(staged, "h_cols3", [P, 4 * PS], BF16, wa8_at),
-            own("h_cols4", [P, 4 * PS], BF16),
-        ]
-        xwg = [own("xwg0", [P, HELD], U32), placed(shared, "xwg7", [P, T - HELD], U32, cols0_at)]
-        hcodes = [own("hcodes%d" % g, [P, PS], U32) for g in range(PAIRS)]
-        side_first, side_end = TOKEN_CHUNKS[-1]
-        base_side = own("base_side", [P, side_end - side_first], F32)
-        y_rest = own("y_rest", [P, (PAIRS - FILLERS) * PS], F32)
-        base_at = rows4_at + HALF_REGION
-        base_upper = placed(shared, "base_upper", [P, T], F32, base_at)
-        sum_turned = placed(shared, "sum_turned", [P, T], F32, base_at)
-        result_side = placed(shared, "result_side", [P, side_end - side_first], F32, base_at)
+        window = [own("window0", [P, T], F32), placed("window1", [P, T], F32, rows9_at)]
+        gated0 = own("gated0", [P, 2 * PS], F32)
+        gated_rest = own("gated_rest", [P, 2 * (T - PS)], F32)
+        h_cols = [placed("h_cols0", [P, 4 * PS], BF16, cols0_at)]
+        h_cols += [own("h_cols%d" % a, [P, 4 * PS * (b - a)], BF16) for a, b in QUANT_CUTS[1:]]
+        xwg = [own("xwg0", [P, HELD], U32), placed("xwg7", [P, T - HELD], U32, cols0_at)]
+        hcodes = [own("hcodes%d" % a, [P, PS * (b - a)], U32) for a, b in QUANT_CUTS]
+        hscales = [own("hscales%d" % a, [P, PS * (b - a)], U8) for a, b in QUANT_CUTS]
 
         bank = [psum.tile([P, BANK], F32, name="bank%d" % b) for b in range(8)]
-        first_acc = [bank[0], bank[1]]
-        for g in range(1, PAIRS):
-            first_acc += [bank[g % 2], [bank[5], bank[2]][g % 2]]
-        turn_first = [bank[2], bank[0]]
-        turn = bank[3:5]
-        second = [bank[6]] + [first_acc[2 * g + 3] for g in range(1, PAIRS - 1)]
-        second.append(turn[1])
-        upper_acc = [acc[:, 0:PS] for acc in second]
-        lower_acc = [acc[:, PS:] for acc in second]
-        frozen_acc = bank[0:3]
-        summing = [bank[6], bank[7], bank[3]]
+        first_acc = [bank[b] for b in (0, 1, 2, 1, 2, 1, 2, 1, 2, 0)]
+        turn_acc = [bank[b] for b in (3, 4, 3, 5, 6)]
+        second_acc = [bank[b] for b in (7, 3, 6, 5, 1)]
+        frozen_acc = [[bank[6][:], bank[5][:], bank[1][:, 0:PS]], [bank[4][:], bank[3][:], bank[1][:, PS:]]]
 
         def load_plane(plane, rows):
             src = rows.bitcast(I32).rearrange("(q r) n -> r q n", r=4)
@@ -187,7 +141,7 @@ def tile_moe_adp_gelu_kernel(
 
         def load_words(words, src, cut):
             nc.sync.dma_start(
-                out=words[:, 0 : cut[1] - cut[0], :].bitcast(I32),
+                out=words[:].bitcast(I32),
                 in_=src.bitcast(I32)[cut[0] : cut[1], 0].rearrange("e p n -> p e n"),
             )
 
@@ -209,51 +163,49 @@ def tile_moe_adp_gelu_kernel(
 
         nc.gpsimd.memset(xs[:].bitcast(I32), 0)
         identity_half(0)
-        for plane in (was[0], wbs[0]):
-            nc.vector.memset(plane[:].bitcast(I32), 0)
+        nc.vector.memset(was[0][:].bitcast(I32), 0)
         identity_half(1)
         nc.vector.memset(was[1][:].bitcast(I32), 0)
-        nc.gpsimd.memset(wbs[1][:].bitcast(I32), 0)
+        nc.gpsimd.memset(wbs[:].bitcast(I32), 0)
+        nc.gpsimd.memset(ws[:].bitcast(I32), 0)
 
         nc.sync.dma_start(offsets[:], offs)
         load_words(wa[0], wa_words, WA_CUTS[0])
         load_plane(xs, x_scales[0])
         nc.sync.dma_start(out=xw[:], in_=x_words[0].rearrange("p t d -> p (t d)").bitcast(I32))
         load_planes(was[0], wa_scales, WA_SCALE_CUTS[0])
-        load_planes(wbs[0], wb_scales, WB_CUTS[0])
         load_words(wa[1], wa_words, WA_CUTS[1])
-        load_words(wb[0], wb_words, WB_CUTS[0])
-        load_gates(0)
         load_words(wa[2], wa_words, WA_CUTS[2])
         load_planes(was[1], wa_scales, WA_SCALE_CUTS[1])
-        load_planes(wbs[1], wb_scales, WB_CUTS[1])
+        load_planes(wbs, wb_scales, (0, E))
+        load_words(wb[0], wb_words, WB_CUTS[0])
+        load_gates(0)
+        load_words(wa[3], wa_words, WA_CUTS[3])
+        load_words(wa[4], wa_words, WA_CUTS[4])
+        load_words(wb[1], wb_words, WB_CUTS[1])
+        load_gates(1)
+        load_words(wb[2], wb_words, WB_CUTS[2])
+        load_gates(2)
+        load_plane(ws, w_scales[0])
+        nc.sync.dma_start(out=ww[:].bitcast(I32), in_=w_words[0].bitcast(I32))
 
-        def late_loads():
-            load_words(wa[3], wa_words, WA_CUTS[3])
-            load_words(wb[1], wb_words, WB_CUTS[1])
-            load_words(wa[4], wa_words, WA_CUTS[4])
-            load_gates(1)
-            nc.gpsimd.memset(ws[:].bitcast(I32), 0)
-            load_plane(ws, w_scales[0])
-            nc.sync.dma_start(out=ww[:].bitcast(I32), in_=w_words[0].bitcast(I32))
-
-        def entries(first_pair, end_pair):
-            return offsets[:, first_pair * PS // PER_COLUMN : end_pair * PS // PER_COLUMN]
+        def entries(a, b):
+            return offsets[:, a // PER_COLUMN : b // PER_COLUMN]
 
         def slot_words(a, b):
             return xwg[0][:, a:b] if a < HELD else xwg[1][:, a - HELD : b - HELD]
 
         def gather_words(i):
             a, b = WORD_CUTS[i]
-            listed = offsets[:, a // PER_COLUMN : b // PER_COLUMN]
-            nc.vector.tensor_copy(out=slot_words(a, b), in_=xw[:].bitcast(U32).indirect(listed))
+            nc.vector.tensor_copy(out=slot_words(a, b), in_=xw[:].bitcast(U32).indirect(entries(a, b)))
 
         def gather_bytes(i):
             a, b = BYTE_CUTS[i]
-            listed = offsets[:, a * C // PER_COLUMN : b * C // PER_COLUMN]
-            nc.vector.tensor_copy(out=xsg[i][:].rearrange("p e j -> p (e j)"), in_=xs[:].indirect(listed))
+            nc.vector.tensor_copy(
+                out=xsg[i][:].rearrange("p e j -> p (e j)"), in_=xs[:].indirect(entries(a * C, b * C))
+            )
 
-        def first_product(e):
+        def first_layer(e):
             nc.tensor.matmul_mx(
                 out=first_acc[e][:],
                 lhsT=slot_words(e * C, (e + 1) * C).bitcast(FP8X4),
@@ -265,82 +217,87 @@ def tile_moe_adp_gelu_kernel(
             )
 
         def gelu(e):
-            g, x = divmod(e, 2)
             nc.scalar.activation(
-                out=h_rows[g][:, x, :].rearrange("j (u p d) -> j u p d", u=2, d=2),
+                out=h_rows[e][:].rearrange("j (u p d) -> j u p d", u=2, d=2),
                 in_=first_acc[e][:].rearrange("j (p u d) -> j u p d", u=2, d=2),
                 func=GELU,
             )
 
-        def turn_h(e0, e1, acc):
-            m = e1 - e0
-            g, x0 = divmod(e0, 2)
-            grouped = h_cols[g][:, x0 * 4 * C : (x0 + m) * 4 * C]
-            turned = acc[:, 0 : m * 2 * C].rearrange("p (x u j) -> p x u j", x=m, u=2)
-            for x in range(m):
-                words = h_rows[g][:, x0 + x, :].bitcast(F32)
+        def turn(g):
+            turned = turn_acc[g][:].rearrange("p (x u j) -> p x u j", x=2, u=2)
+            for x in range(2):
+                words = h_rows[2 * g + x][:].bitcast(F32)
                 for u in range(2):
                     nc.tensor.transpose(turned[:, x, u, :], words[:, u * P : (u + 1) * P], ident[:])
+
+        def weave(g):
+            i = cut_of(QUANT_CUTS, g)
+            at = (g - QUANT_CUTS[i][0]) * 4 * PS
             nc.scalar.copy(
-                out=grouped.bitcast(F32).rearrange("p (x j u) -> p x j u", x=m, u=2),
-                in_=turned.rearrange("p x u j -> p x j u"),
+                out=h_cols[i][:, at : at + 4 * PS].bitcast(F32).rearrange("p (x j u) -> p x j u", x=2, u=2),
+                in_=turn_acc[g][:].rearrange("p (x u j) -> p x j u", x=2, u=2),
             )
 
-        def quantise(e0, e1):
-            g, x0 = divmod(e0, 2)
-            a, b = x0 * C, (x0 + e1 - e0) * C
-            nc.vector.quantize_mx(
-                out=hcodes[g][:, a:b].bitcast(FP8X4), scales=hscales[g][:, a:b], in_=h_cols[g][:, 4 * a : 4 * b]
-            )
+        def quantise(i):
+            nc.vector.quantize_mx(out=hcodes[i][:].bitcast(FP8X4), scales=hscales[i][:], in_=h_cols[i][:])
 
-        def second_layer(half, g, acc):
-            for x in range(2):
-                e = 2 * g + x
-                slots = slice(x * C, (x + 1) * C)
-                nc.tensor.matmul_mx(
-                    out=acc[:, slots],
-                    lhsT=pick(wb, WB_CUTS, e)[:, half * FP4_BYTES * P : (half + 1) * FP4_BYTES * P].bitcast(FP4X4),
-                    lhsT_scale=pick(wbs, WB_CUTS, e)[:, half * P : (half + 1) * P],
-                    rhs=hcodes[g][:, slots].bitcast(FP8X4),
-                    rhs_scale=hscales[g][:, slots],
-                    start=True,
-                    stop=True,
-                )
+        def second_layer(g):
+            i = cut_of(QUANT_CUTS, g)
+            for half in (UPPER, LOWER):
+                for x in range(2):
+                    e = 2 * g + x
+                    at = (e - 2 * QUANT_CUTS[i][0]) * C
+                    nc.tensor.matmul_mx(
+                        out=second_acc[g][:, (1 - half) * PS + x * C : (1 - half) * PS + (x + 1) * C],
+                        lhsT=pick(wb, WB_CUTS, e)[:, half * FP4_BYTES * P : (half + 1) * FP4_BYTES * P].bitcast(FP4X4),
+                        lhsT_scale=wbs[:, e, half * P : (half + 1) * P],
+                        rhs=hcodes[i][:, at : at + C].bitcast(FP8X4),
+                        rhs_scale=hscales[i][:, at : at + C],
+                        start=True,
+                        stop=True,
+                    )
 
-        def open_pair(g):
-            first_product(2 * g)
-            first_product(2 * g + 1)
-            gelu(2 * g)
+        def pair_gates(g):
+            i = cut_of(GATE_CUTS, g)
+            at = (g - GATE_CUTS[i][0]) * PS
+            return gates[i][:, at : at + PS]
 
-        def to_codes(g):
-            turn_h(2 * g, 2 * g + 2, turn[(g + 1) % 2])
-            quantise(2 * g, 2 * g + 2)
+        def gated_slots(a, b):
+            if a < PS:
+                return gated0[:].rearrange("p (h t) -> p h t", h=2)[:, :, a:b]
+            return gated_rest[:].rearrange("p (h t) -> p h t", h=2)[:, :, a - PS : b - PS]
 
-        def second_layers(g):
-            second_layer(UPPER, g, upper_acc[g])
-            second_layer(LOWER, g, lower_acc[g])
+        def gated_half(half, a, b):
+            return gated_slots(a, b)[:, 1 - half, :]
 
-        def scatter(half, first_pair, end_pair, values):
-            i = [j for j, (a, b) in enumerate(GATE_CUTS) if a <= first_pair < b][0]
-            at = GATE_CUTS[i][0]
-            weights = gates[i][:, (first_pair - at) * PS : (end_pair - at) * PS]
+        def apply_gate(g):
             nc.vector.tensor_tensor(
-                out=window[half][:].indirect(entries(first_pair, end_pair)), in0=values, in1=weights, op=MULT
+                out=gated_slots(g * PS, (g + 1) * PS),
+                in0=second_acc[g][:].rearrange("p (h s) -> p h s", h=2),
+                in1=pair_gates(g).unsqueeze(1).to_broadcast([P, 2, PS]),
+                op=MULT,
             )
 
-        def upper(g):
-            nc.scalar.copy(out=y_upper[g][:], in_=upper_acc[g])
-            scatter(UPPER, g, g + 1, y_upper[g][:])
+        def apply_gate_half(g, half):
+            nc.vector.tensor_tensor(
+                out=gated_half(half, g * PS, (g + 1) * PS),
+                in0=second_acc[g][:, (1 - half) * PS : (2 - half) * PS],
+                in1=pair_gates(g),
+                op=MULT,
+            )
 
-        def lower(g):
-            nc.scalar.copy(out=y_lower[g][:], in_=lower_acc[g])
-            scatter(LOWER, g, g + 1, y_lower[g][:])
+        def scatter_upper(a, b):
+            nc.vector.tensor_copy(out=window[UPPER][:].indirect(entries(a, b)), in_=gated_half(UPPER, a, b))
+
+        def scatter_lower(a, b):
+            nc.scalar.activation(
+                out=window[LOWER][:].indirect(entries(a, b)), in_=gated_half(LOWER, a, b), func=COPY
+            )
 
         def frozen(half, i):
             a, b = TOKEN_CHUNKS[i]
-            acc = frozen_acc[i][:, 0 : b - a]
             nc.tensor.matmul_mx(
-                out=acc,
+                out=frozen_acc[half][i][:, 0 : b - a],
                 lhsT=ww[:, half * FP4_BYTES * P : (half + 1) * FP4_BYTES * P].bitcast(FP4X4),
                 lhsT_scale=ws[:, half * P : (half + 1) * P],
                 rhs=xw[:, a:b].bitcast(FP8X4),
@@ -348,88 +305,74 @@ def tile_moe_adp_gelu_kernel(
                 start=True,
                 stop=True,
             )
-            return acc
 
-        def turn_into_sum(i, src, opens, closes):
-            a, b = TOKEN_CHUNKS[i]
-            for c in range(a, b, P):
-                nc.tensor.matmul(
-                    summing[i][:, c - a : c - a + P],
-                    lhsT=src[:, c : c + P],
-                    rhs=ident[:],
-                    start=opens and c == a,
-                    stop=closes and c == b - P,
-                    is_transpose=True,
-                )
+        def add_and_store(half, a, b):
+            nc.vector.tensor_tensor(
+                out=result[half][:, a:b],
+                in0=frozen_acc[half][a // BANK][:, a % BANK : a % BANK + b - a],
+                in1=window[half][:, a:b],
+                op=ADD,
+            )
+            nc.sync.dma_start(out=out[half * P : (half + 1) * P, a:b], in_=result[half][:, a:b])
 
         gather_bytes(0)
         gather_words(0)
         gather_words(1)
         gather_words(2)
-        open_pair(0)
-        gelu(1)
+        for e in range(3):
+            first_layer(e)
+            gelu(e)
         gather_bytes(1)
-        late_loads()
-        turn_h(0, 1, turn_first[0])
-        quantise(0, 1)
-        turn_h(1, 2, turn_first[1])
-        quantise(1, 2)
+        turn(0)
+        weave(0)
+        quantise(0)
         gather_words(3)
-        second_layer(UPPER, 0, upper_acc[0])
-        upper(0)
-        open_pair(1)
+        first_layer(3)
+        first_layer(4)
         gelu(3)
-        second_layer(LOWER, 0, lower_acc[0])
-        to_codes(1)
-        lower(0)
-        open_pair(2)
+        gelu(4)
+        turn(1)
+        weave(1)
+        second_layer(0)
+        apply_gate(0)
+        quantise(1)
+        scatter_upper(0, PS)
+        first_layer(5)
+        first_layer(6)
         gelu(5)
-        second_layers(1)
-        upper(1)
-        open_pair(3)
-        to_codes(2)
-        lower(1)
-        gelu(7)
-        first_product(8)
-        gelu(8)
-        first_product(9)
-        to_codes(3)
-        second_layers(2)
-        upper(2)
-        gelu(9)
-        to_codes(4)
-        second_layer(UPPER, 3, upper_acc[3])
-        upper(3)
-        for i, (a, b) in enumerate(TOKEN_CHUNKS):
-            nc.scalar.copy(out=base_upper[:, a:b], in_=frozen(UPPER, i))
-            turn_into_sum(i, base_upper, True, False)
-        second_layer(UPPER, 4, upper_acc[4])
-        upper(4)
-        second_layer(LOWER, 3, lower_acc[3])
-        second_layer(LOWER, 4, lower_acc[4])
-        for g in range(FILLERS, PAIRS):
-            nc.scalar.copy(out=y_rest[:, (g - FILLERS) * PS : (g - FILLERS + 1) * PS], in_=lower_acc[g])
-        scatter(LOWER, FILLERS, PAIRS, y_rest[:])
+        gelu(6)
+        turn(2)
+        weave(2)
+        quantise(2)
+        for e in (7, 8, 9):
+            first_layer(e)
+        second_layer(1)
+        apply_gate_half(1, UPPER)
+        apply_gate_half(1, LOWER)
+        scatter_upper(PS, 2 * PS)
+        for e in (7, 8, 9):
+            gelu(e)
+        turn(3)
+        weave(3)
+        turn(4)
+        weave(4)
+        quantise(3)
+        second_layer(2)
+        apply_gate(2)
+        second_layer(3)
+        apply_gate(3)
+        second_layer(4)
+        apply_gate_half(4, UPPER)
+        apply_gate_half(4, LOWER)
+        scatter_upper(2 * PS, T)
+        for a, b in LOWER_CUTS:
+            scatter_lower(a, b)
 
-        base_lower = [frozen(LOWER, i) for i in range(len(TOKEN_CHUNKS))]
-        nc.scalar.copy(out=base_side[:], in_=base_lower[-1])
-        for i, (a, b) in enumerate(TOKEN_CHUNKS):
-            turn_into_sum(i, window[UPPER], False, True)
-            nc.scalar.copy(out=sum_turned[:, a:b], in_=summing[i][:, 0 : b - a])
-            for c in range(a, b, P):
-                nc.tensor.transpose(summing[i][:, c - a : c - a + P], sum_turned[:, c : c + P], ident[:])
-            nc.scalar.copy(out=result[UPPER][:, a:b], in_=summing[i][:, 0 : b - a])
-            nc.scalar.dma_start(out=out[0:P, a:b], in_=result[UPPER][:, a:b])
-
-        nc.gpsimd.tensor_tensor(
-            out=result_side[:], in0=base_side[:], in1=window[LOWER][:, side_first:side_end], op=ADD
-        )
-        nc.scalar.dma_start(out=out[P : 2 * P, side_first:side_end], in_=result_side[:])
-        for a in range(0, side_first, PS):
-            nc.vector.tensor_tensor(
-                out=result[LOWER][:, a : a + PS],
-                in0=base_lower[a // BANK][:, a % BANK : a % BANK + PS],
-                in1=window[LOWER][:, a : a + PS],
-                op=ADD,
-            )
-            nc.sync.dma_start(out=out[P : 2 * P, a : a + PS], in_=result[LOWER][:, a : a + PS])
+        for half in (UPPER, LOWER):
+            for i in range(len(TOKEN_CHUNKS)):
+                frozen(half, i)
+        for a, b in TOKEN_CHUNKS:
+            add_and_store(UPPER, a, b)
+        for a, b in TOKEN_CHUNKS:
+            for c in range(a, b, PS):
+                add_and_store(LOWER, c, c + PS)

@@ -28,16 +28,17 @@ FP4_BYTES = 2
 WA_BYTES = FP4_BYTES * H
 WB_BYTES = FP4_BYTES * N
 
-WA_CUTS = [(0, 2), (2, 3), (3, 5), (5, 7), (7, E)]
-WA_SCALE_CUTS = [(0, 4), (4, E)]
+WA_CUTS = [(2 * g, 2 * g + 2) for g in range(PAIRS)]
+WA_SCALE_CUTS = [(0, 6), (6, E)]
 WB_CUTS = [(0, 2), (2, 4), (4, E)]
-GATE_CUTS = [(0, 1), (1, 2), (2, PAIRS)]
+GATE_CUTS = [(0, 1), (1, 2), (2, 3), (3, PAIRS)]
 SHORT = T // 8
 HELD = 7 * C
 WORD_CUTS = [(0, SHORT), (SHORT, 3 * C), (3 * C, HELD), (HELD, T)]
 BYTE_CUTS = [(0, E // 2), (E // 2, E)]
-QUANT_CUTS = [(0, 1), (1, 2), (2, 3), (3, PAIRS)]
-LOWER_CUTS = [(0, PS), (PS, 2 * PS), (2 * PS, 7 * C), (7 * C, T)]
+QUANT_CUTS = [(g, g + 1) for g in range(PAIRS)]
+GATED_CUTS = [(g, g + 1) for g in range(PAIRS)]
+LOWER_CUTS = [(0, 3 * C), (3 * C, 6 * C), (6 * C, 8 * C), (8 * C, T)]
 TOKEN_CHUNKS = [(0, BANK), (BANK, 2 * BANK), (2 * BANK, T)]
 
 
@@ -77,13 +78,12 @@ def tile_moe_adp_gelu_kernel(
 
         soon_specs = [
             ("xw", [P, T], I32, 4 * T),
-            ("was0", [P, 4, H], U8, 4 * H),
+            ("was0", [P, 6, H], U8, 6 * H),
+            ("was4", [P, 4, H], U8, 4 * H),
+            ("wbs", [P, E, N], U8, E * N),
         ]
         next_specs = [
             ("xsg0", [P, 5, C], U8, 5 * C),
-            ("wbs", [P, E, N], U8, E * N),
-            ("was4", [P, 6, H], U8, 6 * H),
-            ("ww", [P, WB_BYTES], U8, WB_BYTES),
             ("ws", [P, N], U8, N),
         ]
         next_specs += [("wb%d" % a, [P, b - a, WB_BYTES], U8, (b - a) * WB_BYTES) for a, b in WB_CUTS]
@@ -97,37 +97,45 @@ def tile_moe_adp_gelu_kernel(
             placed("zeros1", [P, next_size // 4], F32, next_at),
         ]
         tiles = laid_out(soon_specs + next_specs, 0)
-        xw, was0, xsg0, wbs, was4, ww, ws = tiles[0:7]
+        xw, was0, was4, wbs, xsg0, ws = tiles[0:6]
         was = [was0, was4]
         wa0 = placed("wa0", [P, 2, WA_BYTES], U8, late_at)
         xsg5 = placed("xsg5", [P, 5, C], U8, late_at)
-        wb = tiles[7:10]
-        gates = tiles[10:13]
+        wb = tiles[6:9]
+        gates = tiles[9:13]
         wa = [wa0] + tiles[13:]
         xsg = [xsg0, xsg5]
 
         cols0_at = late_at + 2 * WA_BYTES
         rows9_at = cols0_at + 8 * PS
-        rows_at = {a: late_at - (E - a) * WA_BYTES for a, b in WA_CUTS[2:]}
-        rows_at[E - 1] = rows9_at
+        cols1_at = rows9_at + 4 * T
         h_rows = [
-            placed("h_rows%d" % e, [P, H], BF16, rows_at[e]) if e in rows_at else own("h_rows%d" % e, [P, H], BF16)
+            placed("h_rows8", [P, H], BF16, rows9_at) if e == 8 else own("h_rows%d" % e, [P, H], BF16)
             for e in range(E)
         ]
-        window = [own("window0", [P, T], F32), placed("window1", [P, T], F32, rows9_at)]
-        gated0 = own("gated0", [P, 2 * PS], F32)
-        gated_rest = own("gated_rest", [P, 2 * (T - PS)], F32)
         h_cols = [placed("h_cols0", [P, 4 * PS], BF16, cols0_at)]
         h_cols += [own("h_cols%d" % a, [P, 4 * PS * (b - a)], BF16) for a, b in QUANT_CUTS[1:]]
+        window = [own("window0", [P, T], F32), placed("window1", [P, T], F32, rows9_at)]
+        gated_upper = [own("gated_upper%d" % a, [P, (b - a) * PS], F32) for a, b in GATED_CUTS]
+        gated_lower = own("gated_lower", [P, T], F32)
         xwg = [own("xwg0", [P, HELD], U32), placed("xwg7", [P, T - HELD], U32, cols0_at)]
-        hcodes = [own("hcodes%d" % a, [P, PS * (b - a)], U32) for a, b in QUANT_CUTS]
+        gates_at = late_at - (E - 2) * WA_BYTES - 4 * T
+        hcodes = [
+            placed("hcodes0", [P, PS], U32, cols1_at),
+            placed("hcodes1", [P, PS], U32, cols1_at),
+            placed("hcodes2", [P, PS], U32, gates_at),
+            placed("hcodes3", [P, PS], U32, gates_at + 4 * PS),
+            placed("hcodes4", [P, PS], U32, gates_at + 8 * PS),
+        ]
+        ww = placed("ww", [P, WB_BYTES], U8, gates_at)
         hscales = [own("hscales%d" % a, [P, PS * (b - a)], U8) for a, b in QUANT_CUTS]
 
-        bank = [psum.tile([P, BANK], F32, name="bank%d" % b) for b in range(8)]
-        first_acc = [bank[b] for b in (0, 1, 2, 1, 2, 1, 2, 1, 2, 0)]
-        turn_acc = [bank[b] for b in (3, 4, 3, 5, 6)]
-        second_acc = [bank[b] for b in (7, 3, 6, 5, 1)]
-        frozen_acc = [[bank[6][:], bank[5][:], bank[1][:, 0:PS]], [bank[4][:], bank[3][:], bank[1][:, PS:]]]
+        bank = [psum.tile([P, BANK], F32, name="bank%d" % b) for b in range(7)]
+        first_acc = [bank[b] for b in (0, 1, 2, 3, 2, 3, 4, 3, 5, 6)]
+        turn_acc = [bank[b] for b in (4, 5, 4, 5, 1)]
+        second_acc = [[bank[0][:, 0:PS], bank[1][:, 0:PS]]]
+        second_acc += [[bank[b][:, 0:PS], bank[b][:, PS:]] for b in (4, 5, 1, 2)]
+        frozen_acc = [[bank[0][:], bank[6][:], bank[3][:, 0:PS]], [bank[4][:], bank[5][:], bank[3][:, PS:]]]
 
         def load_plane(plane, rows):
             src = rows.bitcast(I32).rearrange("(q r) n -> r q n", r=4)
@@ -164,9 +172,9 @@ def tile_moe_adp_gelu_kernel(
         nc.gpsimd.memset(xs[:].bitcast(I32), 0)
         identity_half(0)
         nc.vector.memset(was[0][:].bitcast(I32), 0)
+        nc.gpsimd.memset(wbs[:].bitcast(I32), 0)
         identity_half(1)
         nc.vector.memset(was[1][:].bitcast(I32), 0)
-        nc.gpsimd.memset(wbs[:].bitcast(I32), 0)
         nc.gpsimd.memset(ws[:].bitcast(I32), 0)
 
         nc.sync.dma_start(offsets[:], offs)
@@ -176,18 +184,18 @@ def tile_moe_adp_gelu_kernel(
         load_planes(was[0], wa_scales, WA_SCALE_CUTS[0])
         load_words(wa[1], wa_words, WA_CUTS[1])
         load_words(wa[2], wa_words, WA_CUTS[2])
-        load_planes(was[1], wa_scales, WA_SCALE_CUTS[1])
         load_planes(wbs, wb_scales, (0, E))
         load_words(wb[0], wb_words, WB_CUTS[0])
         load_gates(0)
+        load_planes(was[1], wa_scales, WA_SCALE_CUTS[1])
         load_words(wa[3], wa_words, WA_CUTS[3])
         load_words(wa[4], wa_words, WA_CUTS[4])
         load_words(wb[1], wb_words, WB_CUTS[1])
         load_gates(1)
         load_words(wb[2], wb_words, WB_CUTS[2])
         load_gates(2)
+        load_gates(3)
         load_plane(ws, w_scales[0])
-        nc.sync.dma_start(out=ww[:].bitcast(I32), in_=w_words[0].bitcast(I32))
 
         def entries(a, b):
             return offsets[:, a // PER_COLUMN : b // PER_COLUMN]
@@ -225,7 +233,7 @@ def tile_moe_adp_gelu_kernel(
 
         def turn(g):
             turned = turn_acc[g][:].rearrange("p (x u j) -> p x u j", x=2, u=2)
-            for x in range(2):
+            for x in (1, 0):
                 words = h_rows[2 * g + x][:].bitcast(F32)
                 for u in range(2):
                     nc.tensor.transpose(turned[:, x, u, :], words[:, u * P : (u + 1) * P], ident[:])
@@ -248,7 +256,7 @@ def tile_moe_adp_gelu_kernel(
                     e = 2 * g + x
                     at = (e - 2 * QUANT_CUTS[i][0]) * C
                     nc.tensor.matmul_mx(
-                        out=second_acc[g][:, (1 - half) * PS + x * C : (1 - half) * PS + (x + 1) * C],
+                        out=second_acc[g][half][:, x * C : (x + 1) * C],
                         lhsT=pick(wb, WB_CUTS, e)[:, half * FP4_BYTES * P : (half + 1) * FP4_BYTES * P].bitcast(FP4X4),
                         lhsT_scale=wbs[:, e, half * P : (half + 1) * P],
                         rhs=hcodes[i][:, at : at + C].bitcast(FP8X4),
@@ -262,26 +270,17 @@ def tile_moe_adp_gelu_kernel(
             at = (g - GATE_CUTS[i][0]) * PS
             return gates[i][:, at : at + PS]
 
-        def gated_slots(a, b):
-            if a < PS:
-                return gated0[:].rearrange("p (h t) -> p h t", h=2)[:, :, a:b]
-            return gated_rest[:].rearrange("p (h t) -> p h t", h=2)[:, :, a - PS : b - PS]
-
         def gated_half(half, a, b):
-            return gated_slots(a, b)[:, 1 - half, :]
+            if half == LOWER:
+                return gated_lower[:, a:b]
+            i = cut_of(GATED_CUTS, a // PS)
+            at = GATED_CUTS[i][0] * PS
+            return gated_upper[i][:, a - at : b - at]
 
-        def apply_gate(g):
-            nc.vector.tensor_tensor(
-                out=gated_slots(g * PS, (g + 1) * PS),
-                in0=second_acc[g][:].rearrange("p (h s) -> p h s", h=2),
-                in1=pair_gates(g).unsqueeze(1).to_broadcast([P, 2, PS]),
-                op=MULT,
-            )
-
-        def apply_gate_half(g, half):
+        def apply_gate(g, half):
             nc.vector.tensor_tensor(
                 out=gated_half(half, g * PS, (g + 1) * PS),
-                in0=second_acc[g][:, (1 - half) * PS : (2 - half) * PS],
+                in0=second_acc[g][half],
                 in1=pair_gates(g),
                 op=MULT,
             )
@@ -315,56 +314,50 @@ def tile_moe_adp_gelu_kernel(
             )
             nc.sync.dma_start(out=out[half * P : (half + 1) * P, a:b], in_=result[half][:, a:b])
 
+        def first_pair(g):
+            for e in (2 * g, 2 * g + 1):
+                first_layer(e)
+            for e in (2 * g, 2 * g + 1):
+                gelu(e)
+
         gather_bytes(0)
         gather_words(0)
         gather_words(1)
         gather_words(2)
-        for e in range(3):
-            first_layer(e)
-            gelu(e)
+        first_pair(0)
         gather_bytes(1)
+        first_pair(1)
         turn(0)
         weave(0)
         quantise(0)
         gather_words(3)
-        first_layer(3)
-        first_layer(4)
-        gelu(3)
-        gelu(4)
+        first_pair(2)
         turn(1)
         weave(1)
         second_layer(0)
-        apply_gate(0)
+        apply_gate(0, UPPER)
+        apply_gate(0, LOWER)
         quantise(1)
         scatter_upper(0, PS)
-        first_layer(5)
-        first_layer(6)
-        gelu(5)
-        gelu(6)
+        first_pair(3)
         turn(2)
         weave(2)
-        quantise(2)
-        for e in (7, 8, 9):
-            first_layer(e)
         second_layer(1)
-        apply_gate_half(1, UPPER)
-        apply_gate_half(1, LOWER)
-        scatter_upper(PS, 2 * PS)
-        for e in (7, 8, 9):
-            gelu(e)
+        quantise(2)
+        first_pair(4)
         turn(3)
         weave(3)
         turn(4)
         weave(4)
-        quantise(3)
-        second_layer(2)
-        apply_gate(2)
-        second_layer(3)
-        apply_gate(3)
-        second_layer(4)
-        apply_gate_half(4, UPPER)
-        apply_gate_half(4, LOWER)
-        scatter_upper(2 * PS, T)
+        for g in range(1, PAIRS):
+            apply_gate(g, UPPER)
+            apply_gate(g, LOWER)
+            scatter_upper(g * PS, (g + 1) * PS)
+            if g + 1 < PAIRS:
+                second_layer(g + 1)
+            if g + 2 < PAIRS:
+                quantise(g + 2)
+        nc.sync.dma_start(out=ww[:].bitcast(I32), in_=w_words[0].bitcast(I32))
         for a, b in LOWER_CUTS:
             scatter_lower(a, b)
 

@@ -130,11 +130,12 @@ def tile_moe_adp_gelu_kernel(
         ww = placed("ww", [P, WB_BYTES], U8, gates_at)
         hscales = [own("hscales%d" % a, [P, PS * (b - a)], U8) for a, b in QUANT_CUTS]
 
-        bank = [psum.tile([P, BANK], F32, name="bank%d" % b) for b in range(7)]
+        bank = [psum.tile([P, BANK], F32, name="bank%d" % b) for b in range(8)]
         first_acc = [bank[b] for b in (0, 1, 2, 3, 2, 3, 4, 3, 5, 6)]
         turn_acc = [bank[b] for b in (4, 5, 4, 5, 1)]
         second_acc = [[bank[0][:, 0:PS], bank[1][:, 0:PS]]]
-        second_acc += [[bank[b][:, 0:PS], bank[b][:, PS:]] for b in (4, 5, 1, 2)]
+        second_acc += [[bank[b][:, 0:PS], bank[b][:, PS:]] for b in (4, 5, 1)]
+        second_acc.append([bank[2][:, 0:PS], bank[7][:, 0:PS]])
         frozen_acc = [[bank[0][:], bank[6][:], bank[3][:, 0:PS]], [bank[4][:], bank[5][:], bank[3][:, PS:]]]
 
         def load_plane(plane, rows):
@@ -347,24 +348,34 @@ def tile_moe_adp_gelu_kernel(
         first_pair(4)
         turn(3)
         weave(3)
-        turn(4)
-        weave(4)
-        for g in range(1, PAIRS):
+        last = PAIRS - 1
+        turn(last)
+        weave(last)
+        for g in range(1, last):
             apply_gate(g, UPPER)
             apply_gate(g, LOWER)
             scatter_upper(g * PS, (g + 1) * PS)
-            if g + 1 < PAIRS:
-                second_layer(g + 1)
+            second_layer(g + 1)
             if g + 2 < PAIRS:
                 quantise(g + 2)
         nc.sync.dma_start(out=ww[:].bitcast(I32), in_=w_words[0].bitcast(I32))
-        for a, b in LOWER_CUTS:
+        for a, b in LOWER_CUTS[:2]:
+            scatter_lower(a, b)
+        nc.scalar.copy(out=gated_half(UPPER, last * PS, T), in_=second_acc[last][UPPER])
+        apply_gate(last, LOWER)
+        nc.vector.tensor_tensor(
+            out=window[UPPER][:].indirect(entries(last * PS, T)),
+            in0=gated_half(UPPER, last * PS, T),
+            in1=pair_gates(last),
+            op=MULT,
+        )
+        for a, b in LOWER_CUTS[2:]:
             scatter_lower(a, b)
 
         for half in (UPPER, LOWER):
             for i in range(len(TOKEN_CHUNKS)):
                 frozen(half, i)
-        for a, b in TOKEN_CHUNKS:
+        for a, b in [(0, C), (C, BANK)] + TOKEN_CHUNKS[1:]:
             add_and_store(UPPER, a, b)
         for a, b in TOKEN_CHUNKS:
             for c in range(a, b, PS):

@@ -29,12 +29,11 @@ WA_BYTES = FP4_BYTES * H
 WB_BYTES = FP4_BYTES * N
 
 WA_CUTS = [(2 * g, 2 * g + 2) for g in range(PAIRS)]
-WA_SCALE_CUTS = [(0, 6), (6, E)]
+WA_SCALE_CUTS = [(0, 3), (3, 6), (6, E)]
 WB_CUTS = [(0, 2), (2, 4), (4, E)]
 GATE_CUTS = [(0, 1), (1, 2), (2, 3), (3, PAIRS)]
-SHORT = T // 8
 HELD = 7 * C
-WORD_CUTS = [(0, SHORT), (SHORT, 3 * C), (3 * C, HELD), (HELD, T)]
+WORD_CUTS = [(0, C), (C, 2 * C), (2 * C, 4 * C), (4 * C, HELD), (HELD, T)]
 BYTE_CUTS = [(0, E // 2), (E // 2, E)]
 QUANT_CUTS = [(g, g + 1) for g in range(PAIRS)]
 GATED_CUTS = [(g, g + 1) for g in range(PAIRS)]
@@ -78,10 +77,9 @@ def tile_moe_adp_gelu_kernel(
 
         soon_specs = [
             ("xw", [P, T], I32, 4 * T),
-            ("was0", [P, 6, H], U8, 6 * H),
-            ("was4", [P, 4, H], U8, 4 * H),
             ("wbs", [P, E, N], U8, E * N),
         ]
+        soon_specs += [("was%d" % a, [P, b - a, H], U8, (b - a) * H) for a, b in WA_SCALE_CUTS]
         next_specs = [
             ("xsg0", [P, 5, C], U8, 5 * C),
             ("ws", [P, N], U8, N),
@@ -97,24 +95,26 @@ def tile_moe_adp_gelu_kernel(
             placed("zeros1", [P, next_size // 4], F32, next_at),
         ]
         tiles = laid_out(soon_specs + next_specs, 0)
-        xw, was0, was4, wbs, xsg0, ws = tiles[0:6]
-        was = [was0, was4]
+        xw, wbs = tiles[0:2]
+        was = tiles[2:5]
+        xsg0, ws = tiles[5:7]
         wa0 = placed("wa0", [P, 2, WA_BYTES], U8, late_at)
         xsg5 = placed("xsg5", [P, 5, C], U8, late_at)
-        wb = tiles[6:9]
-        gates = tiles[9:13]
-        wa = [wa0] + tiles[13:]
+        wb = tiles[7:10]
+        gates = tiles[10:14]
+        wa = [wa0] + tiles[14:]
         xsg = [xsg0, xsg5]
 
         cols0_at = late_at + 2 * WA_BYTES
         rows9_at = cols0_at + 8 * PS
         cols1_at = rows9_at + 4 * T
         h_rows = [
-            placed("h_rows8", [P, H], BF16, rows9_at) if e == 8 else own("h_rows%d" % e, [P, H], BF16)
+            placed("h_rows%d" % e, [P, H], BF16, {3: cols0_at, 8: rows9_at}[e])
+            if e in (3, 8)
+            else own("h_rows%d" % e, [P, H], BF16)
             for e in range(E)
         ]
-        h_cols = [placed("h_cols0", [P, 4 * PS], BF16, cols0_at)]
-        h_cols += [own("h_cols%d" % a, [P, 4 * PS * (b - a)], BF16) for a, b in QUANT_CUTS[1:]]
+        h_cols = [own("h_cols%d" % a, [P, 4 * PS * (b - a)], BF16) for a, b in QUANT_CUTS]
         window = [own("window0", [P, T], F32), placed("window1", [P, T], F32, rows9_at)]
         gated_upper = [own("gated_upper%d" % a, [P, (b - a) * PS], F32) for a, b in GATED_CUTS]
         gated_lower = own("gated_lower", [P, T], F32)
@@ -134,7 +134,7 @@ def tile_moe_adp_gelu_kernel(
         first_acc = [bank[b] for b in (0, 1, 2, 3, 2, 3, 4, 3, 5, 6)]
         turn_acc = [bank[b] for b in (4, 5, 4, 5, 1)]
         second_acc = [[bank[0][:, 0:PS], bank[1][:, 0:PS]]]
-        second_acc += [[bank[b][:, 0:PS], bank[b][:, PS:]] for b in (4, 5, 1)]
+        second_acc += [[bank[b][:, 0:PS], bank[b][:, PS:]] for b in (3, 5, 1)]
         second_acc.append([bank[2][:, 0:PS], bank[7][:, 0:PS]])
         frozen_acc = [[bank[0][:], bank[6][:], bank[3][:, 0:PS]], [bank[4][:], bank[5][:], bank[3][:, PS:]]]
 
@@ -176,6 +176,7 @@ def tile_moe_adp_gelu_kernel(
         nc.gpsimd.memset(wbs[:].bitcast(I32), 0)
         identity_half(1)
         nc.vector.memset(was[1][:].bitcast(I32), 0)
+        nc.vector.memset(was[2][:].bitcast(I32), 0)
         nc.gpsimd.memset(ws[:].bitcast(I32), 0)
 
         nc.sync.dma_start(offsets[:], offs)
@@ -184,11 +185,12 @@ def tile_moe_adp_gelu_kernel(
         nc.sync.dma_start(out=xw[:], in_=x_words[0].rearrange("p t d -> p (t d)").bitcast(I32))
         load_planes(was[0], wa_scales, WA_SCALE_CUTS[0])
         load_words(wa[1], wa_words, WA_CUTS[1])
+        load_planes(was[1], wa_scales, WA_SCALE_CUTS[1])
         load_words(wa[2], wa_words, WA_CUTS[2])
         load_planes(wbs, wb_scales, (0, E))
         load_words(wb[0], wb_words, WB_CUTS[0])
         load_gates(0)
-        load_planes(was[1], wa_scales, WA_SCALE_CUTS[1])
+        load_planes(was[2], wa_scales, WA_SCALE_CUTS[2])
         load_words(wa[3], wa_words, WA_CUTS[3])
         load_words(wa[4], wa_words, WA_CUTS[4])
         load_words(wb[1], wb_words, WB_CUTS[1])
@@ -325,15 +327,33 @@ def tile_moe_adp_gelu_kernel(
         gather_words(0)
         gather_words(1)
         gather_words(2)
-        first_pair(0)
+        gather_words(3)
+        for part, acc in enumerate((bank[7], bank[0])):
+            nc.tensor.matmul_mx(
+                out=acc[:, 0:PS],
+                lhsT=slot_words(0, C).bitcast(FP8X4),
+                lhsT_scale=pick(xsg, BYTE_CUTS, 0),
+                rhs=wa[0][:, 0, part * FP4_BYTES * PS : (part + 1) * FP4_BYTES * PS].bitcast(FP4X4),
+                rhs_scale=was[0][:, 0, part * PS : (part + 1) * PS],
+                start=True,
+                stop=True,
+            )
+        first_layer(1)
+        for part, acc in enumerate((bank[7], bank[0])):
+            nc.scalar.activation(
+                out=h_rows[0][:].rearrange("j (u p d) -> j u p d", u=2, d=2)[:, :, part * P // 2 : (part + 1) * P // 2, :],
+                in_=acc[:, 0:PS].rearrange("j (p u d) -> j u p d", u=2, d=2),
+                func=GELU,
+            )
+        gelu(1)
         gather_bytes(1)
         first_pair(1)
         turn(0)
         weave(0)
         quantise(0)
-        gather_words(3)
         first_pair(2)
         turn(1)
+        gather_words(4)
         weave(1)
         second_layer(0)
         apply_gate(0, UPPER)
@@ -377,6 +397,5 @@ def tile_moe_adp_gelu_kernel(
                 frozen(half, i)
         for a, b in [(0, C), (C, BANK)] + TOKEN_CHUNKS[1:]:
             add_and_store(UPPER, a, b)
-        for a, b in TOKEN_CHUNKS:
-            for c in range(a, b, PS):
-                add_and_store(LOWER, c, c + PS)
+        for a, b in [(0, C), (C, BANK)] + [(c, c + PS) for c in range(BANK, T, PS)]:
+            add_and_store(LOWER, a, b)

from contextlib import ExitStack

import concourse.mybir as mybir

K, T, E, C, H, N = 512, 1280, 10, 128, 512, 256
FLOPS = 2 * K * N * T + 2 * K * H * E * C + 2 * H * N * E * C

F32 = mybir.dt.float32
BF16 = mybir.dt.bfloat16
I32 = mybir.dt.int32
U32 = mybir.dt.uint32
U16 = mybir.dt.uint16
U8 = mybir.dt.uint8
FP8X4 = mybir.dt.float8_e4m3fn_x4
FP4X4 = mybir.dt.float4_e2m1fn_x4
GELU = mybir.ActivationFunctionType.Gelu_apprx_tanh
COPY = mybir.ActivationFunctionType.Copy
ADD = mybir.AluOpType.add
MULT = mybir.AluOpType.mult

P = 128
BANK = 512
PAIRS = E // 2
PS = 2 * C
PER_COLUMN = 16
UPPER, LOWER = 0, 1
FP4_BYTES = 2
WA_BYTES = FP4_BYTES * H
WB_BYTES = FP4_BYTES * N

WA_CUTS = [(2 * g, 2 * g + 2) for g in range(PAIRS)]
WA_SCALE_CUTS = [(0, 3), (3, 6), (6, E)]
WB_CUTS = [(0, 2), (2, 4), (4, E)]
GATE_CUTS = [(0, 1), (1, 2), (2, 3), (3, PAIRS)]
HELD = 7 * C
WORD_CUTS = [(0, C), (C, 2 * C), (2 * C, 4 * C), (4 * C, HELD), (HELD, T)]
BYTE_CUTS = [(0, E // 2), (E // 2, E)]
QUANT_CUTS = [(g, g + 1) for g in range(PAIRS)]
GATED_CUTS = [(g, g + 1) for g in range(PAIRS)]
LOWER_CUTS = [(0, 3 * C), (3 * C, 6 * C), (6 * C, 8 * C), (8 * C, T)]
TOKEN_CHUNKS = [(0, BANK), (BANK, 2 * BANK), (2 * BANK, T)]


def tile_moe_adp_gelu_kernel(
    tc, x_words, x_scales, w_words, w_scales, wa_words, wa_scales, wb_words, wb_scales, gate, offs, out
):
    nc = tc.nc
    with ExitStack() as ctx:
        keep = ctx.enter_context(tc.tile_pool(name="keep", bufs=1))
        staged = ctx.enter_context(tc.tile_pool(name="staged", bufs=1))
        psum = ctx.enter_context(tc.psum_pool(name="psum", bufs=1))

        def own(name, shape, dtype):
            return keep.tile(shape, dtype, name=name, align_bytes=64)

        def placed(name, shape, dtype, at):
            return staged.tile(shape, dtype, name=name, align_bytes=64, offset=at)

        def laid_out(specs, at):
            tiles = []
            for name, shape, dtype, size in specs:
                tiles.append(placed(name, shape, dtype, at))
                at = at + size
            return tiles

        def cut_of(cuts, index):
            return [j for j, (a, b) in enumerate(cuts) if a <= index < b][0]

        def pick(tiles, cuts, index):
            i = cut_of(cuts, index)
            return tiles[i][:, index - cuts[i][0], :]

        offsets = keep.tile([P, T // PER_COLUMN], U16, name="offsets")
        xs = own("xs", [P, T], U8)
        ident = own("ident", [P, P], F32)
        result = [own("result%d" % half, [P, T], F32) for half in (UPPER, LOWER)]

        soon_specs = [
            ("xw", [P, T], I32, 4 * T),
            ("wbs", [P, E, N], U8, E * N),
        ]
        soon_specs += [("was%d" % a, [P, b - a, H], U8, (b - a) * H) for a, b in WA_SCALE_CUTS]
        next_specs = [
            ("xsg0", [P, 5, C], U8, 5 * C),
            ("ws", [P, N], U8, N),
        ]
        next_specs += [("wb%d" % a, [P, b - a, WB_BYTES], U8, (b - a) * WB_BYTES) for a, b in WB_CUTS]
        next_specs += [("gates%d" % a, [P, (b - a) * PS], F32, 4 * (b - a) * PS) for a, b in GATE_CUTS]
        next_specs += [("wa%d" % a, [P, b - a, WA_BYTES], U8, (b - a) * WA_BYTES) for a, b in WA_CUTS[1:]]
        next_at = sum([s[3] for s in soon_specs])
        next_size = sum([s[3] for s in next_specs])
        late_at = next_at + next_size
        zeros = [
            placed("zeros0", [P, late_at // 4], F32, 0),
            placed("zeros1", [P, next_size // 4], F32, next_at),
        ]
        tiles = laid_out(soon_specs + next_specs, 0)
        xw, wbs = tiles[0:2]
        was = tiles[2:5]
        xsg0, ws = tiles[5:7]
        wa0 = placed("wa0", [P, 2, WA_BYTES], U8, late_at)
        xsg5 = placed("xsg5", [P, 5, C], U8, late_at)
        wb = tiles[7:10]
        gates = tiles[10:14]
        wa = [wa0] + tiles[14:]
        xsg = [xsg0, xsg5]

        cols0_at = late_at + 2 * WA_BYTES
        rows9_at = cols0_at + 8 * PS
        cols1_at = rows9_at + 4 * T
        h_rows = [
            placed("h_rows%d" % e, [P, H], BF16, {3: cols0_at, 8: rows9_at}[e])
            if e in (3, 8)
            else own("h_rows%d" % e, [P, H], BF16)
            for e in range(E)
        ]
        h_cols = [own("h_cols%d" % a, [P, 4 * PS * (b - a)], BF16) for a, b in QUANT_CUTS]
        window = [own("window0", [P, T], F32), placed("window1", [P, T], F32, rows9_at)]
        gated_upper = [own("gated_upper%d" % a, [P, (b - a) * PS], F32) for a, b in GATED_CUTS]
        gated_lower = own("gated_lower", [P, T], F32)
        xwg = [own("xwg0", [P, HELD], U32), placed("xwg7", [P, T - HELD], U32, cols0_at)]
        gates_at = late_at - (E - 2) * WA_BYTES - 4 * T
        hcodes = [
            placed("hcodes0", [P, PS], U32, cols1_at),
            placed("hcodes1", [P, PS], U32, cols1_at),
            placed("hcodes2", [P, PS], U32, gates_at),
            placed("hcodes3", [P, PS], U32, gates_at + 4 * PS),
            placed("hcodes4", [P, PS], U32, gates_at + 8 * PS),
        ]
        ww = placed("ww", [P, WB_BYTES], U8, gates_at)
        hscales = [own("hscales%d" % a, [P, PS * (b - a)], U8) for a, b in QUANT_CUTS]

        bank = [psum.tile([P, BANK], F32, name="bank%d" % b) for b in range(8)]
        first_acc = [bank[b] for b in (0, 1, 2, 3, 2, 3, 4, 3, 5, 6)]
        turn_acc = [bank[b] for b in (4, 5, 4, 5, 1)]
        second_acc = [[bank[0][:, 0:PS], bank[1][:, 0:PS]]]
        second_acc += [[bank[b][:, 0:PS], bank[b][:, PS:]] for b in (3, 5, 1)]
        second_acc.append([bank[2][:, 0:PS], bank[7][:, 0:PS]])
        frozen_acc = [[bank[0][:], bank[6][:], bank[3][:, 0:PS]], [bank[4][:], bank[5][:], bank[3][:, PS:]]]

        def load_plane(plane, rows):
            src = rows.bitcast(I32).rearrange("(q r) n -> r q n", r=4)
            for r in range(4):
                nc.sync.dma_start(out=plane[r:P:32, :].bitcast(I32), in_=src[r])

        def load_planes(planes, rows, cut):
            src = rows.bitcast(I32)[cut[0] : cut[1], 0].rearrange("e (q r) n -> r q e n", r=4)
            for r in range(4):
                nc.sync.dma_start(out=planes[r:P:32, :, :].bitcast(I32), in_=src[r])

        def load_words(words, src, cut):
            nc.sync.dma_start(
                out=words[:].bitcast(I32),
                in_=src.bitcast(I32)[cut[0] : cut[1], 0].rearrange("e p n -> p e n"),
            )

        def load_gates(i):
            a, b = GATE_CUTS[i]
            nc.sync.dma_start(out=gates[i][:], in_=gate[:, a * PS : b * PS])

        def identity_half(i):
            nc.vector.memset(zeros[i][:, 0 : P // 2], 0.0)
            nc.gpsimd.affine_select(
                out=ident[:, i * P // 2 : (i + 1) * P // 2],
                in_=zeros[i][:, 0 : P // 2],
                compare_op=mybir.AluOpType.not_equal,
                fill=1.0,
                base=-i * P // 2,
                pattern=[[-1, P // 2]],
                channel_multiplier=1,
            )

        nc.gpsimd.memset(xs[:].bitcast(I32), 0)
        identity_half(0)
        nc.vector.memset(was[0][:].bitcast(I32), 0)
        nc.gpsimd.memset(wbs[:].bitcast(I32), 0)
        identity_half(1)
        nc.vector.memset(was[1][:].bitcast(I32), 0)
        nc.vector.memset(was[2][:].bitcast(I32), 0)
        nc.gpsimd.memset(ws[:].bitcast(I32), 0)

        nc.sync.dma_start(offsets[:], offs)
        load_words(wa[0], wa_words, WA_CUTS[0])
        load_plane(xs, x_scales[0])
        nc.sync.dma_start(out=xw[:], in_=x_words[0].rearrange("p t d -> p (t d)").bitcast(I32))
        load_planes(was[0], wa_scales, WA_SCALE_CUTS[0])
        load_words(wa[1], wa_words, WA_CUTS[1])
        load_planes(was[1], wa_scales, WA_SCALE_CUTS[1])
        load_words(wa[2], wa_words, WA_CUTS[2])
        load_planes(wbs, wb_scales, (0, E))
        load_words(wb[0], wb_words, WB_CUTS[0])
        load_gates(0)
        load_planes(was[2], wa_scales, WA_SCALE_CUTS[2])
        load_words(wa[3], wa_words, WA_CUTS[3])
        load_words(wa[4], wa_words, WA_CUTS[4])
        load_words(wb[1], wb_words, WB_CUTS[1])
        load_gates(1)
        load_words(wb[2], wb_words, WB_CUTS[2])
        load_gates(2)
        load_gates(3)
        load_plane(ws, w_scales[0])

        def entries(a, b):
            return offsets[:, a // PER_COLUMN : b // PER_COLUMN]

        def slot_words(a, b):
            return xwg[0][:, a:b] if a < HELD else xwg[1][:, a - HELD : b - HELD]

        def gather_words(i):
            a, b = WORD_CUTS[i]
            nc.vector.tensor_copy(out=slot_words(a, b), in_=xw[:].bitcast(U32).indirect(entries(a, b)))

        def gather_bytes(i):
            a, b = BYTE_CUTS[i]
            nc.vector.tensor_copy(
                out=xsg[i][:].rearrange("p e j -> p (e j)"), in_=xs[:].indirect(entries(a * C, b * C))
            )

        def first_layer(e):
            nc.tensor.matmul_mx(
                out=first_acc[e][:],
                lhsT=slot_words(e * C, (e + 1) * C).bitcast(FP8X4),
                lhsT_scale=pick(xsg, BYTE_CUTS, e),
                rhs=pick(wa, WA_CUTS, e).bitcast(FP4X4),
                rhs_scale=pick(was, WA_SCALE_CUTS, e),
                start=True,
                stop=True,
            )

        def gelu(e):
            nc.scalar.activation(
                out=h_rows[e][:].rearrange("j (u p d) -> j u p d", u=2, d=2),
                in_=first_acc[e][:].rearrange("j (p u d) -> j u p d", u=2, d=2),
                func=GELU,
            )

        def turn(g):
            turned = turn_acc[g][:].rearrange("p (x u j) -> p x u j", x=2, u=2)
            for x in (1, 0):
                words = h_rows[2 * g + x][:].bitcast(F32)
                for u in range(2):
                    nc.tensor.transpose(turned[:, x, u, :], words[:, u * P : (u + 1) * P], ident[:])

        def weave(g):
            i = cut_of(QUANT_CUTS, g)
            at = (g - QUANT_CUTS[i][0]) * 4 * PS
            nc.scalar.copy(
                out=h_cols[i][:, at : at + 4 * PS].bitcast(F32).rearrange("p (x j u) -> p x j u", x=2, u=2),
                in_=turn_acc[g][:].rearrange("p (x u j) -> p x j u", x=2, u=2),
            )

        def quantise(i):
            nc.vector.quantize_mx(out=hcodes[i][:].bitcast(FP8X4), scales=hscales[i][:], in_=h_cols[i][:])

        def second_layer(g):
            i = cut_of(QUANT_CUTS, g)
            for half in (UPPER, LOWER):
                for x in range(2):
                    e = 2 * g + x
                    at = (e - 2 * QUANT_CUTS[i][0]) * C
                    nc.tensor.matmul_mx(
                        out=second_acc[g][half][:, x * C : (x + 1) * C],
                        lhsT=pick(wb, WB_CUTS, e)[:, half * FP4_BYTES * P : (half + 1) * FP4_BYTES * P].bitcast(FP4X4),
                        lhsT_scale=wbs[:, e, half * P : (half + 1) * P],
                        rhs=hcodes[i][:, at : at + C].bitcast(FP8X4),
                        rhs_scale=hscales[i][:, at : at + C],
                        start=True,
                        stop=True,
                    )

        def pair_gates(g):
            i = cut_of(GATE_CUTS, g)
            at = (g - GATE_CUTS[i][0]) * PS
            return gates[i][:, at : at + PS]

        def gated_half(half, a, b):
            if half == LOWER:
                return gated_lower[:, a:b]
            i = cut_of(GATED_CUTS, a // PS)
            at = GATED_CUTS[i][0] * PS
            return gated_upper[i][:, a - at : b - at]

        def apply_gate(g, half):
            nc.vector.tensor_tensor(
                out=gated_half(half, g * PS, (g + 1) * PS),
                in0=second_acc[g][half],
                in1=pair_gates(g),
                op=MULT,
            )

        def scatter_upper(a, b):
            nc.vector.tensor_copy(out=window[UPPER][:].indirect(entries(a, b)), in_=gated_half(UPPER, a, b))

        def scatter_lower(a, b):
            nc.scalar.activation(
                out=window[LOWER][:].indirect(entries(a, b)), in_=gated_half(LOWER, a, b), func=COPY
            )

        def frozen(half, i):
            a, b = TOKEN_CHUNKS[i]
            nc.tensor.matmul_mx(
                out=frozen_acc[half][i][:, 0 : b - a],
                lhsT=ww[:, half * FP4_BYTES * P : (half + 1) * FP4_BYTES * P].bitcast(FP4X4),
                lhsT_scale=ws[:, half * P : (half + 1) * P],
                rhs=xw[:, a:b].bitcast(FP8X4),
                rhs_scale=xs[:, a:b],
                start=True,
                stop=True,
            )

        def add_and_store(half, a, b):
            nc.vector.tensor_tensor(
                out=result[half][:, a:b],
                in0=frozen_acc[half][a // BANK][:, a % BANK : a % BANK + b - a],
                in1=window[half][:, a:b],
                op=ADD,
            )
            nc.sync.dma_start(out=out[half * P : (half + 1) * P, a:b], in_=result[half][:, a:b])

        def first_pair(g):
            for e in (2 * g, 2 * g + 1):
                first_layer(e)
            for e in (2 * g, 2 * g + 1):
                gelu(e)

        gather_bytes(0)
        gather_words(0)
        gather_words(1)
        gather_words(2)
        gather_words(3)
        for part, acc in enumerate((bank[7], bank[0])):
            nc.tensor.matmul_mx(
                out=acc[:, 0:PS],
                lhsT=slot_words(0, C).bitcast(FP8X4),
                lhsT_scale=pick(xsg, BYTE_CUTS, 0),
                rhs=wa[0][:, 0, part * FP4_BYTES * PS : (part + 1) * FP4_BYTES * PS].bitcast(FP4X4),
                rhs_scale=was[0][:, 0, part * PS : (part + 1) * PS],
                start=True,
                stop=True,
            )
        first_layer(1)
        for part, acc in enumerate((bank[7], bank[0])):
            nc.scalar.activation(
                out=h_rows[0][:].rearrange("j (u p d) -> j u p d", u=2, d=2)[:, :, part * P // 2 : (part + 1) * P // 2, :],
                in_=acc[:, 0:PS].rearrange("j (p u d) -> j u p d", u=2, d=2),
                func=GELU,
            )
        gelu(1)
        gather_bytes(1)
        first_pair(1)
        turn(0)
        weave(0)
        quantise(0)
        first_pair(2)
        turn(1)
        gather_words(4)
        weave(1)
        second_layer(0)
        apply_gate(0, UPPER)
        apply_gate(0, LOWER)
        quantise(1)
        scatter_upper(0, PS)
        first_pair(3)
        turn(2)
        weave(2)
        second_layer(1)
        quantise(2)
        first_pair(4)
        turn(3)
        weave(3)
        last = PAIRS - 1
        turn(last)
        weave(last)
        for g in range(1, last):
            apply_gate(g, UPPER)
            apply_gate(g, LOWER)
            scatter_upper(g * PS, (g + 1) * PS)
            second_layer(g + 1)
            if g + 2 < PAIRS:
                quantise(g + 2)
        nc.sync.dma_start(out=ww[:].bitcast(I32), in_=w_words[0].bitcast(I32))
        for a, b in LOWER_CUTS[:2]:
            scatter_lower(a, b)
        nc.scalar.copy(out=gated_half(UPPER, last * PS, T), in_=second_acc[last][UPPER])
        apply_gate(last, LOWER)
        nc.vector.tensor_tensor(
            out=window[UPPER][:].indirect(entries(last * PS, T)),
            in0=gated_half(UPPER, last * PS, T),
            in1=pair_gates(last),
            op=MULT,
        )
        for a, b in LOWER_CUTS[2:]:
            scatter_lower(a, b)

        for half in (UPPER, LOWER):
            for i in range(len(TOKEN_CHUNKS)):
                frozen(half, i)
        for a, b in [(0, C), (C, BANK)] + TOKEN_CHUNKS[1:]:
            add_and_store(UPPER, a, b)
        for a, b in [(0, C), (C, BANK)] + [(c, c + PS) for c in range(BANK, T, PS)]:
            add_and_store(LOWER, a, b)
